import numpy as np, ml_dtypes
CORES = [5,29,101,125,133,157,229,253]
N = 8
BF = ml_dtypes.bfloat16
def gentries(a):
    return np.ascontiguousarray(a.reshape(8, 16, -1).transpose(0, 2, 1)).reshape(8, -1)
def gtable(e):
    e = np.asarray(e); return np.ascontiguousarray(e.reshape(8, -1, 16).transpose(0, 2, 1)).reshape(128, -1).astype(np.int32)
L, T, K, R = 128, 16, 16, 3
W = L * T
def mix(rng, a):
    return np.take_along_axis(a, np.argsort(rng.random(a.shape), axis=2), 2)
def spots(rng, q, m, n):
    a = np.add.accumulate(rng.integers(1, n // m + 1, (q, 8, m, L)), axis=2)
    return mix(rng, (a + rng.integers(0, n, (q, 8, 1, L))) % n)
def reals(rng, n):
    v = 2 * rng.random((N, 8, 16, n)) - 1
    return np.where(v < 0, -1.0, 1.0) * (0.25 + 0.75 * np.abs(v)) * rng.choice(np.array([0.5, 0.75, 1.0]), (N, 8, 1, n))
def parts(rng):
    pa = rng.integers(-128, 128, (N, 8, 16, W)); fc = rng.integers(-128, 128, (N, 8, 16, R * L))
    return pa, reals(rng, W), spots(rng, N, K, W), fc, reals(rng, R * L), np.exp2(-5 + 3 * rng.random((N, 8, 16, 1)))
def flat(a):
    return np.asarray(a, np.float32).reshape(N, 128, -1).astype(BF)
def pack(pa, ea, nd, fc, er, dl):
    return {"pa": flat(pa), "ea": flat(ea), "nd": np.stack([gtable(a.reshape(8, K * L)) for a in nd]), "fc": flat(fc), "er": flat(er),
            "dl": np.clip(np.asarray(dl, np.float32), np.float32(0.03125), np.float32(0.25)).reshape(N, 128, 1)}
def setup_inputs(rng):
    return pack(*parts(rng))
def setup_inputs_spread(rng):
    pa, ea, nd, fc, er, dl = parts(rng)
    pa = np.floor((2 * rng.random(pa.shape) - 1) * np.exp2(rng.integers(3, 8, (N, 8, 1, W))))
    fc = np.floor((2 * rng.random(fc.shape) - 1) * np.exp2(rng.integers(3, 8, (N, 8, 1, R * L))))
    ea = ea * np.exp2(-rng.integers(0, 2, (N, 8, 1, W)))
    er = er * np.exp2(-rng.integers(0, 2, (N, 8, 1, R * L)))
    return pack(pa, ea, nd, fc, er, dl)
def setup_inputs_ends(rng):
    pa, ea, nd, fc, er, dl = parts(rng)
    def ends(n):
        whole = rng.random((N, 8, 1, n)) < 0.5
        return np.where(whole, rng.random((N, 8, 1, n)) < 0.5, rng.random((N, 8, 16, n)) < 0.5)
    pa = np.where(ends(W), 127, -128); fc = np.where(ends(R * L), 127, -128)
    pa[..., [1, W - 2, W - 1]] = 127; pa[..., [2, W - 3]] = -128
    for t in range(R): fc[..., t * L + L - 1] = 127 if t % 2 else -128
    ea = np.where(ends(W), 1.0, -1.0); er = np.where(ends(R * L), 1.0, -1.0); dl = np.where(rng.random(dl.shape) < 0.5, 0.25, 0.03125)
    ea[:, :, 0] = 1.0; er[:, :, 0] = -1.0; ea[:, :, 15] = -1.0; er[:, :, 15] = 1.0
    dl[:, :, 0] = 0.25; dl[:, :, 15] = 0.25; dl[:, :, 1] = 0.03125
    a = rng.integers(1, K, (N, 8, 1, L)); a[N - 1, :, 0, L - 1] = K // 2; j = np.arange(K)[:, None]
    far = np.where(j < a, j, W - K + j)
    near = T * (1 + spots(rng, N, K, L - 2)) + rng.choice(np.array([0, T - 2, T - 1]), (N, 8, K, L)); near[:, :, 0] = 0; near[:, :, 1] = W - 1
    nd = np.where((np.arange(8) % 2 == 1)[None, :, None, None], far, near)
    return pack(pa, ea, mix(rng, nd), fc, er, dl)
def setup_inputs_corners(rng):
    pa, ea, nd, fc, er, dl = parts(rng); one = spots(rng, 1, N * K, W)[0]; s = spots(rng, N, K, L); j = np.arange(K)[:, None]; i = np.arange(L)
    for q in range(N):
        nd[q, 0] = one[0, :K]
        nd[q, 1] = np.concatenate([one[1, :K - 1], one[1, K - 1 + q:K + q]])
        nd[q, 2] = one[2, q * K:(q + 1) * K]
        nd[q, 6] = np.where(j < (i % (K + 1))[None, :], one[6, :K], one[6, q * K:(q + 1) * K])
    nd[:, 3] = s[:, 3] * T + T - 1
    nd[:, 4] = (T * rng.integers(0, L, (N, 1, L)) + j) % W
    nd[:, 5] = ((s[:, 5] - s[:, 5, :1] + i) % L) * T + rng.choice(np.array([0, T - 2, T - 1]), (N, K, L))
    pa[::2, 7] = -128; pa[1::2, 7] = np.where(rng.random((N // 2, 1, W)) < 0.5, 127, -128)
    dl[:, ::2, ::2] = 0.03125; dl[:, 1::2, ::4] = 0.25
    return pack(pa, ea, mix(rng, nd), fc, er, dl)
def setup_inputs_crowd(rng):
    pa, ea, nd, fc, er, dl = parts(rng)
    pa[:, ::2] = rng.integers(-1, 2, (N, 4, 1, W)); fc[:, ::2] = rng.integers(-1, 2, (N, 4, 1, R * L))
    s = spots(rng, N, K, L)[..., :1]; day = np.where(np.arange(K)[:, None] % 2 == 0, T - 2, rng.integers(0, T, (N, 8, K, 1)))
    c = s * T + day; c[:, 0] = c[:1, 0]
    same = np.zeros((N, 8, K, L), np.int64) + c
    same[:, 4:, :, L - 1] = nd[:, 4:, :, L - 1]
    nd = mix(rng, same); nd[:, 1] = same[:, 1]
    return pack(pa, ea, nd, fc, er, dl)
def setup_inputs_late(rng):
    pa, ea, nd, fc, er, dl = parts(rng); c = spots(rng, N, K, L); i = np.arange(L)
    def off(n, few):
        if few: return (np.arange(16)[:, None] == rng.integers(0, 32, (N, 1, n))).astype(np.int64)
        return rng.integers(0, 8, (N, 16, n))
    for g, few in ((1, False), (3, True), (4, False), (7, True)):
        a = off(W, few); w = off(R * L, few); low = (np.arange(R * L) // L + g) % 2 == 1
        pa[:, g] = 127 - a if g % 2 else a - 128
        fc[:, g] = np.where(low, w - 128, 127 - w)
    s = spots(rng, N, K, L // 2)[:, 6]
    c[:, 6] = 2 * s + (i + (np.arange(K)[:, None] == K - 1)) % 2
    x = rng.choice(np.array([-1.0, 1.0]), (N, 16, 1)) * np.where((np.arange(R)[:, None] + i) % 2 == 0, 1.0, -1.0).reshape(-1)
    er[:, 6] = x; ea[:, 6, :, T - 1::T] = -x[:, :, :L]; dl[:, 6] = 0.25
    return pack(pa, ea, mix(rng, c * T + T - 2), fc, er, dl)
def check_ranges(d):
    bad = []
    for k, lo, hi in (("pa", -128, 127), ("fc", -128, 127), ("ea", -1, 1), ("er", -1, 1), ("dl", 0.03125, 0.25), ("nd", 0, W - 1)):
        v = np.asarray(d[k]).astype(np.float64)
        if not (np.min(v) >= lo and np.max(v) <= hi): bad.append("range of " + k)
        elif k in ("pa", "fc") and np.any(v != np.floor(v)): bad.append(k + " holds a number that isn't whole")
        elif k in ("ea", "er") and np.any(np.abs(v) < 0.0625): bad.append("sizes of " + k)
    s = np.sort(np.stack([gentries(a) for a in d["nd"]]).reshape(N, 8, K, L), axis=2)
    if np.any(s[:, :, 1:] == s[:, :, :-1]): bad.append("nd names a place twice in one lane")
    return bad
def reference(pa, ea, nd, fc, er, dl):
    P = pa.astype(np.int32).reshape(N, 8, 16, W); E = ea.astype(np.float64).reshape(N, 8, 16, W)
    f = fc.astype(np.int32).reshape(N, 8, 16, R, L); z = er.astype(np.float64).reshape(N, 8, 16, R, L); lim = dl.astype(np.float64).reshape(N, 8, 16, 1)
    A = np.stack([gentries(a) for a in nd]).astype(np.int64).reshape(N, 8, K, L)
    yb, ys = [], []
    for t in range(R):
        own = A - A % T + (A + 1) % T
        come = np.roll(own, 1, axis=0)
        void = np.any(come[:, :, :, None, :] == own[:, :, None, :, :], axis=3)
        c = np.concatenate([own, come], axis=2)
        g = np.take_along_axis(P, c.reshape(N, 8, 1, 2 * K * L), 3).reshape(N, 8, 16, 2 * K, L)
        d = np.add.reduce(np.abs(g - f[:, :, :, t][:, :, :, None, :]), axis=2)
        d[:, :, K:] = np.where(void, 2 ** 20, d[:, :, K:])
        o = np.argsort(d, axis=2, kind="stable")[:, :, :K][:, :, ::-1]
        A = np.take_along_axis(c, o, 2)
        e = np.take_along_axis(E, A.reshape(N, 8, 1, K * L), 3).reshape(N, 8, 16, K, L)
        b = np.zeros((N, 8, 16, L))
        for k in range(K): b = b + np.minimum(np.maximum(0.5 * (e[:, :, :, k] - b), -lim), lim)
        yb.append(b); ys.append(np.add.reduce(np.exp(-np.abs(e - b[:, :, :, None, :])), axis=3))
        if t < R - 1:
            P[..., t::T] = f[:, :, :, t]; E[..., t::T] = z[:, :, :, t] - b
    return {"yb": np.concatenate(yb, axis=3).reshape(N, 128, R * L).astype(np.float32), "ys": np.concatenate(ys, axis=3).reshape(N, 128, R * L).astype(np.float32)}

def check_inputs(d):
    bad = list(check_ranges(d))
    if not bad:
        for name, y in reference(**d).items():
            for q in range(N):
                v = np.abs(np.asarray(y[q], np.float64)); s = np.sqrt(np.mean(v * v))
                if v.max() > 9 * s or s < 2.0 ** -4: bad.append('%s of rank %d is uneven or too small' % (name, q))
    return bad

@@ -1,0 +1,710 @@
+import numpy as np
+from concourse.bass import DstId, RemoteDMATransfer
+from concourse.mybir import AluOpType as ALU, ActivationFunctionType as AF
+
+DAYS = 3
+NCH = 2
+BIAS = (("whole", "whole"), ("whole", "whole"), ("dve3", "dve3"))
+ACTG = ((4, 6), (0, 4, 6), (0, 1, 2, 4, 6))
+LOOK = (((8, "act"), (8, "dve")), ((8, "act"), (8, "act")), ((2, "act"), (4, "act"), (4, "act"), (6, "act")))
+FOLD = (False, False, False)
+SUBPE = (0, 0, 0)
+VOIDW = True
+TAILQ = (4, 4, 4, 2, 2)
+ECH = ((4, 4, 4, 4), (4, 4, 4, 4), (2, 4, 4, 6))
+COST = dict(CY=0.00083 * 1.25, GA=1.56, PCY=0.00042 * 1.25, WS=0.06, WX=0.10, HOP=5.0, FIX=0.02)
+VARY = ((2, {}), (0.5, dict(PCY=0.00105)), (1, dict(WS=0.15, WX=0.2)), (1, dict(GA=1.04, HOP=3.5)), (1, dict(GA=2.08, HOP=6.5)),
+        (1, dict(CY=0.00083, HOP=6.0)), (1, dict(FIX=0.05)), (1, dict(FIX=0.0)))
+TRIES, SEED = 1000, 0
+
+B5 = [128, 2, 2, 2, 2, 8]
+SCRATCH = {
+    "KO": ("psum", [128, 512], "float32"), "KA": ("psum", [128, 512], "float32"), "LK": ("psum", [128, 512], "float32"),
+    "SM": ("psum", [128, 512], "float32"), "BA": ("psum", [128, 512], "float32"), "BB": ("psum", [128, 512], "float32"),
+    "SB": ("psum", [128, 512], "float32"), "DV": ("psum", [128, 4, 2, 2, 2, 2, 8], "float32"),
+    "ND": ("sbuf", [128, 128], "int32"), "Pb": ("sbuf", [128, 2064], "bfloat16"), "Ew": ("sbuf", [128, 2048], "float32"),
+    "FR": ("sbuf", [128, 3, 512], "bfloat16"), "ER": ("sbuf", [128, 384], "bfloat16"), "DL": ("sbuf", [128, 4], "float32"),
+    "BT": ("sbuf", [128, 20], "float32"), "MM": ("sbuf", [128, 4], "float32"), "IO": ("sbuf", [128, 256], "int32"), "TI": ("sbuf", [128, 16], "int32"),
+    "TF": ("sbuf", [128, 32], "float32"), "Ib": ("sbuf", [128, 128], "bfloat16"), "nIb": ("sbuf", [128, 128], "bfloat16"),
+    "Ibig": ("sbuf", [128, 128], "bfloat16"), "Ih": ("sbuf", [128, 128], "float32"), "Z": ("sbuf", [128, 144], "bfloat16"),
+    "If": ("sbuf", [128, 128], "float32"), "nIf": ("sbuf", [128, 128], "float32"),
+    "Dm": ("sbuf", [128, 2048], "bfloat16"), "CR": ("sbuf", [128, 768], "bfloat16"), "SC": ("sbuf", [128, 256], "float32"),
+    "PT": ("sbuf", [128, 128], "bfloat16"), "AB": ("sbuf", [128, 4096], "bfloat16"), "PG": ("sbuf", [128, 1024], "bfloat16"),
+    "EQ": ("sbuf", [128, 2048], "bfloat16"), "JG": ("sbuf", [128, 2048], "bfloat16"), "JW": ("sbuf", [128, 3, 256], "bfloat16"),
+    "RR": ("sbuf", [128, 4, 256], "bfloat16"), "LF": ("sbuf", [128, 256], "float32"),
+    "LO": ("sbuf", [128, 512], "uint16"), "LA": ("sbuf", [128, 384], "uint16"),
+    "KS": ("sbuf", B5, "float32"), "S0": ("sbuf", B5, "float32"), "S1": ("sbuf", B5, "float32"), "ZZ": ("sbuf", B5, "float32"),
+    "KI": ("sbuf", B5, "int32"), "O32": ("sbuf", [128, 128], "int32"), "D32": ("sbuf", [128, 128], "int32"),
+    "O16": ("sbuf", [128, 128], "uint16"), "E0": ("sbuf", [128, 2048], "float32"), "E1": ("sbuf", [128, 2048], "float32"),
+    "E2": ("sbuf", [128, 2048], "float32"), "U": ("sbuf", [128, 128], "float32"), "X": ("sbuf", [128, 128], "float32"),
+    "YB": ("sbuf", [128, 384], "float32"), "YS": ("sbuf", [128, 384], "float32"),
+}
+DMA_SEMS = ["d%d" % i for i in range(20)]
+SEMAPHORES = (["pe", "dve", "act", "pool", "sent", "cast"] + DMA_SEMS + ["ar%d%d" % (t, c) for t in range(DAYS) for c in range(NCH)]
+              + ["fo%d" % t for t in range(DAYS)])
+EXT = {"pa": [128, 2048], "ea": [128, 2048], "nd": [128, 128], "fc": [128, 384], "er": [128, 384], "dl": [128, 1],
+       "yb": [128, 384], "ys": [128, 384]}
+S_ = slice(None)
+R_ = slice(None, None, -1)
+MAGIC = float(3 * 2 ** 26)
+
+
+def A(name, *key):
+    return (name, (S_,) + tuple(key))
+
+
+def C(name, a, b, step=None):
+    return A(name, slice(a, b, step))
+
+
+def IND(win, off):
+    return ("*", win, off)
+
+
+def shape_of(n):
+    return EXT[n] if n in EXT else SCRATCH[n][1]
+
+
+def elems(ap):
+    sh = shape_of(ap[0])[1:]
+    return np.arange(int(np.prod(sh))).reshape(sh)[ap[1][1:]].ravel()
+
+
+def where(ap):
+    return "dram" if ap[0] in EXT else SCRATCH[ap[0]][0]
+
+
+def width(ap):
+    return 2 if SCRATCH[ap[0]][2] in ("bfloat16", "uint16") else 4
+
+
+def isap(x):
+    return isinstance(x, tuple)
+
+
+def build(cost):
+    CY, GA, PCY, HOP, FIX = cost["CY"], cost["GA"], cost["PCY"], cost["HOP"], cost["FIX"]
+    ops, hist, bank, ndma, part = [], {}, {}, [0], [0]
+
+    def add(eng, call, args, outs, ins, busy, lat=None, sem=None, after=(), grp=None):
+        i = len(ops)
+        deps = dict((d, True) for d in after)
+        flat = []
+        for x in ins:
+            flat += [x[1], x[2]] if x[0] == "*" else [x]
+        for aps, wr in ((flat, False), (outs, True)):
+            for ap in aps:
+                m = np.zeros(int(np.prod(shape_of(ap[0])[1:])), bool)
+                m[elems(ap)] = True
+                h = hist.setdefault(ap[0], [])
+                for (j, jw, jm) in h:
+                    if j != i and (wr or jw) and (m & jm).any():
+                        deps[j] = True
+                if wr:
+                    h[:] = [e for e in h if (e[2] & ~m).any()]
+                h.append((i, wr, m))
+        for n in set(ap[0] for ap in flat + list(outs) if where(ap) == "psum"):
+            b = bank.setdefault(n, [None, [], []])
+            if b[0] != eng:
+                b[0], b[2], b[1] = eng, b[1], []
+            for j in b[2]:
+                deps[j] = True
+            if eng == "pe":
+                for j in b[1]:
+                    deps[j] = True
+            b[1].append(i)
+        if grp is not None:
+            deps = dict((d, True) for d in deps if ops[d]["grp"] != grp or d in after)
+        ops.append(dict(grp=grp, part=part[0], eng=eng, call=call, args=args, deps=sorted(deps), busy=busy, lat=busy if lat is None else lat, sem=sem))
+        return i
+
+    def n_of(ap):
+        return 16 * len(elems(ap[2])) if ap[0] == "*" else len(elems(ap))
+
+    def vcost(n, c):
+        return FIX + max(64, n * c) * CY
+
+    def one(out, x):
+        if x[0] == "*":
+            return 0.05 + n_of(x) * GA * CY
+        return vcost(n_of(x), 0.5 if width(out) == 2 and width(x) == 2 else 1)
+
+    def cp(out, x):
+        return add("dve", "tensor_copy", (out, x), [out], [x], one(out, x))
+
+    def ts(out, x, s1, o0, s2=None, o1=None):
+        a = (out, x, s1, s2, o0) + (() if o1 is None else (o1,))
+        return add("dve", "tensor_scalar", a, [out], [x] + [s for s in (s1, s2) if isap(s)], one(out, x))
+
+    def tt(out, x, y, op):
+        c = one(out, x) if x[0] == "*" else vcost(n_of(x), 2 if where(x) == where(y) == "sbuf" else 1)
+        return add("dve", "tensor_tensor", (out, x, y, op), [out], [x, y], c)
+
+    def ms(out, v):
+        return add("dve", "memset", (out, v), [out], [], vcost(n_of(out), width(out) / 4))
+
+    def act(out, x, f, scale=1.0, bias=0.0):
+        c = 0.065 + n_of(x) * GA * CY if x[0] == "*" else vcost(n_of(x), 1)
+        return add("act", "activation", (out, x, f, scale, bias), [out], [x] + [s for s in (bias,) if isap(s)], c)
+
+    def mm(out, l, r, start, stop, grp=None, after=()):
+        c = max(64, n_of(r)) * PCY * (4 if width(r) == 4 else 1)
+        return add("pe", "matmul", (out, l, r, start, stop), [out], [l, r], c, grp=grp, after=after)
+
+    def dma(q, out, x, lat):
+        if q == "pool":
+            return add(q, "dma_start", (out, x), [out], [x], 1.0, lat, "cast")
+        ndma[0] += 1
+        return add(q, "dma_start", (out, x), [out], [x], 0.1, lat, DMA_SEMS[ndma[0] - 1])
+
+    def row(a, b):
+        return ("CR", (slice(0, 1), slice(a, b)))
+
+    def send(t, cs):
+        src = [C("LO", t * 128 + c * 64, t * 128 + c * 64 + 64) for c in cs]
+        s = add("pool", "send", (t, cs), [], src, 1.0, 1.0, "sent")
+        for c in cs:
+            add("rx", "rx", (), [C("LA", t * 128 + c * 64, t * 128 + c * 64 + 64)], [], 0.0, HOP + (2.0 if t == 0 else 0.0),
+                "ar%d%d" % (t, c), after=[s])
+
+    dma("sp", C("ND", 0, 128), C("nd", 0, 128), 2.2)
+    dma("act", C("Pb", 15, 2063), C("pa", 0, 2048), 3.0)
+    for r in range(4):
+        dma("sp", A("FR", S_, slice(r * 128, r * 128 + 128)), C("fc", 0, 384), 2.5)
+    dma("sp", C("DL", 0, 1), A("dl", S_), 2.5)
+    dma("sp", C("ER", 0, 384), C("er", 0, 384), 2.5)
+    add("pool", "iota", (), [C("IO", 0, 256)], [], 0.6)
+    io = C("IO", 0, 128)
+    ts(C("Ib", 0, 128), io, 0.0, ALU.is_equal)
+    ts(C("nIb", 0, 128), io, 0.0, ALU.is_equal, -1.0, ALU.mult)
+    ts(C("Ibig", 0, 128), io, 0.0, ALU.is_equal, float(2 ** 26), ALU.mult)
+    ts(C("Ih", 0, 128), io, 0.0, ALU.is_equal, 0.5, ALU.mult)
+    if any("pe" in m for m in BIAS) or any(SUBPE):
+        ts(C("If", 0, 128), io, 0.0, ALU.is_equal)
+        ts(C("nIf", 0, 128), io, 0.0, ALU.is_equal, -1.0, ALU.mult)
+    ms(C("Z", 0, 144), 0.0)
+    ts(C("TF", 16, 24), C("IO", 0, 128, 16), 0.0, ALU.is_le, 8192.0, ALU.mult)
+    ts(C("TF", 24, 32), C("IO", 0, 128, 16), -15.0, ALU.is_ge)
+    tt(C("Z", 16, 144, 16), C("TF", 16, 24), C("TF", 24, 32), ALU.mult)
+    ts(C("TI", 0, 16), C("IO", 0, 16), 15, ALU.bitwise_and)
+    ts(C("TF", 0, 16), C("TI", 0, 16), 0.0, ALU.is_equal)
+    for il in range(16):
+        ts(C("Dm", il * 128, il * 128 + 128), C("Ib", 0, 128), C("TF", il, il + 1), ALU.mult)
+    cp(row(0, 256), ("IO", (slice(0, 1), slice(0, 256))))
+    for k, v in enumerate((1.0, 32.0, 8.5, -float(2 ** 24))):
+        ms(row(256 + 128 * k, 384 + 128 * k), v)
+    ms(C("SC", 0, 256, 2), 0.0)
+    ms(C("SC", 1, 256, 2), 0.5)
+    cp(C("LO", 0, 128), C("ND", 0, 128))
+    send(0, list(range(NCH)))
+    dma("pool", C("Ew", 0, 2048), C("ea", 0, 2048), 5.0)
+    cp(C("PT", 0, 128), C("Pb", 15, 2063, 16))
+    cp(C("Pb", 31, 2064, 16), C("PT", 0, 128))
+    for k, v in enumerate((1.0, -1.0, 2.0, -2.0)):
+        ts(C("MM", k, k + 1), C("DL", 0, 1), v, ALU.mult)
+    m1, mn1, m2, mn2 = [C("MM", k, k + 1) for k in range(4)]
+    if any("act" in m for m in BIAS):
+        cp(C("BT", 17, 18), C("IO", 0, 1))
+        ts(C("BT", 0, 16), C("IO", 0, 16), C("BT", 17, 18), ALU.subtract, -0.5, ALU.mult)
+        ts(C("BT", 0, 16), C("BT", 0, 16), 1.0, ALU.add, m1, ALU.mult)
+        ts(C("BT", 16, 17), C("DL", 0, 1), 16.0, ALU.mult)
+    ts(C("LF", 0, 128), C("ND", 0, 128), -7.5, ALU.add)
+    ts(C("LF", 128, 256), C("ND", 0, 128), -7.5, ALU.add)
+    ts(A("JW", 0, slice(0, 128)), C("LF", 0, 128), MAGIC, ALU.add, -MAGIC, ALU.add)
+    tt(A("RR", 0, slice(0, 128)), C("LF", 0, 128), A("JW", 0, slice(0, 128)), ALU.subtract)
+    Pw, Ew = C("Pb", 16, 2064), C("Ew", 0, 2048)
+    npg = [0]
+
+    def distances(t, half):
+        kb, lst = ("KO", "LO") if half == 0 else ("KA", "LA")
+        key = C(kb, 0, 128)
+        mm(key, row(512, 640), row(256, 384), True, False)
+        mm(key, row(384, 512), row(half * 128, half * 128 + 128), False, False)
+        low = []
+        for c in range(2):
+            kc, lo = C(kb, c * 64, c * 64 + 64), half * 128 + c * 64
+            i = mm(kc, C("Ib", 0, 128), A("RR", t, slice(lo, lo + 64)), False, False, (t, half))
+            low.append(mm(kc, row(640, 768), row(256, 320), False, False, (t, half), [i]))
+        if half == 1:
+            for r in range(16):
+                if VOIDW:
+                    tt(C("EQ", r * 128, r * 128 + 128), A("DV", 2), C("LF", r * 8, r * 8 + 128), ALU.is_equal)
+                    mm(key, C("Ibig", 0, 128), C("EQ", r * 128, r * 128 + 128), False, False, (t, half))
+                for c in range(0 if VOIDW else 2):
+                    tt(C("EQ", r * 128 + c * 64, r * 128 + c * 64 + 64), A("DV", 2, c), C("LF", r * 8 + c * 64, r * 8 + c * 64 + 64),
+                       ALU.is_equal)
+                    mm(C(kb, c * 64, c * 64 + 64), C("Ibig", 0, 128), C("EQ", r * 128 + c * 64, r * 128 + c * 64 + 64), False, False,
+                       (t, half))
+        for q in range(4):
+            off = C(lst, t * 128 + q * 32, t * 128 + q * 32 + 32)
+            base = half * 2048 + q * 512
+            ab = C("AB", base, base + 512)
+            if half * 4 + q in ACTG[t]:
+                pg = C("PG", (npg[0] % 2) * 512, (npg[0] % 2) * 512 + 512)
+                npg[0] += 1
+                act(pg, IND(Pw, off), AF.Identity)
+                mm(C("SB", 0, 512), C("Ib", 0, 128), pg, True, False)
+                mm(C("SB", 0, 512), C("nIb", 0, 128), A("FR", t, S_), False, True)
+                act(ab, C("SB", 0, 512), AF.Abs)
+            else:
+                tt(ab, IND(Pw, off), A("FR", t, S_), ALU.subtract)
+                act(ab, ab, AF.Abs)
+            if q % 2 == 1:
+                b0 = base - 512
+                for il in range(16):
+                    mm(C(kb, (q - 1) * 32, (q + 1) * 32), C("Z", 16 - il, 144 - il), C("AB", b0 + il, b0 + 1024, 16), False, False,
+                       (t, half), [low[q // 2]])
+
+    def sel(buf, dims, fix, rev=()):
+        name, pre = buf
+        return A(name, *(pre + tuple(fix[b] if b in fix else (R_ if b in rev else S_) for b in dims) + (S_,)))
+
+    def sort():
+        sb, ps = [("S0", ()), ("S1", ())], [("DV", (0,)), ("DV", (1,))]
+        seq = [(c, c == lv - 1) for lv in range(1, 5) for c in range(lv - 1, -1, -1)] + [(4, True)]
+        x0, x1, dims = ("KS", ()), None, [1, 4, 3, 2]
+        for s, (c, first) in enumerate(seq):
+            last = c == 4
+            c2 = 3 if last else seq[s + 1][0]
+            rev = [b for b in range(c)] if first else []
+            yd = [2, 1, 0] if last else sorted([b for b in dims if b != c2] + [c], reverse=True)
+            ys = [sb[s % 2], ps[s % 2]]
+            if last:
+                ys = [(y[0], y[1] + (0,)) for y in ys]
+            for side, op in ((0, ALU.min), (1, ALU.max))[:1 if last else 2]:
+                for v in (0, 1):
+                    a = sel(x0, dims, {c2: 1 - v if c2 in rev else v}, rev)
+                    b = C("KA", v * 64, v * 64 + 64) if s == 0 else sel(x1, dims, {c2: v})
+                    tt(sel(ys[v], yd, {c: side}), a, b, op)
+            x0, x1, dims = ys[0], ys[1], yd
+        full, zz = [3, 2, 1, 0], ("ZZ", ())
+        for side, op in ((0, ALU.max), (1, ALU.min)):
+            tt(sel(zz, full, {3: side}), sel(x0, dims, {}), sel(x1, dims, {}), op)
+        ys = [("S1", (0,)), ("DV", (1, 0))]
+        for side, op in ((0, ALU.max), (1, ALU.min)):
+            for v in (0, 1):
+                tt(sel(ys[v], [3, 2, 0], {2: side}), sel(zz, full, {2: 0, 1: v}), sel(zz, full, {2: 1, 1: v}), op)
+        for side, op in ((0, ALU.max), (1, ALU.min)):
+            tt(sel(zz, full, {1: side}), sel(ys[0], [3, 2, 0], {}), sel(ys[1], [3, 2, 0], {}), op)
+        for side, op in ((0, ALU.max), (1, ALU.min)):
+            tt(sel(("KI", ()), full, {0: side}), sel(zz, full, {0: 0}), sel(zz, full, {0: 1}), op)
+
+    def choose(t):
+        part[0] += 1
+        for c in range(NCH):
+            la = C("LA", t * 128 + c * 64, t * 128 + c * 64 + 64)
+            jw = A("JW", t, slice(128 + c * 64, 192 + c * 64))
+            ts(A("DV", 2, c), la, -7.5, ALU.add)
+            ts(jw, A("DV", 2, c), MAGIC, ALU.add, -MAGIC, ALU.add)
+            tt(A("RR", t, slice(128 + c * 64, 192 + c * 64)), A("DV", 2, c), jw, ALU.subtract)
+        distances(t, 0)
+        act(A("KS"), C("KO", 0, 128), AF.Identity)
+        distances(t, 1)
+        if t < DAYS - 1:
+            cp(C("Pb", 31 if t == 0 else 15 + t, 2064, 16), A("FR", t, slice(0, 128)))
+        sort()
+        ts(C("O32", 0, 128), A("KI"), 5, ALU.arith_shift_right, 255, ALU.bitwise_and)
+        cp(C("O16", 0, 128), C("O32", 0, 128))
+        ts(C("D32", 0, 128), A("KI"), 15, ALU.bitwise_and)
+        ts(A("RR", t + 1, slice(0, 128)), C("D32", 0, 128), -7.5, ALU.add)
+        c0 = 0
+        for n, who in LOOK[t]:
+            c1 = c0 + 8 * n
+            jg, src = C("JG", c0 * 16, c1 * 16), IND(A("JW", t, S_), C("O16", c0, c1))
+            if who == "act":
+                act(jg, src, AF.Identity)
+            else:
+                cp(jg, src)
+            lk = C("LK", c0, c1)
+            mm(lk, C("Ib", 0, 128), A("RR", t + 1, slice(c0, c1)), True, False)
+            for il in range(16):
+                mm(lk, C("Dm", il * 128, il * 128 + 128), C("JG", c0 * 16 + il, c1 * 16, 16), False, il == 15)
+            ts(C("LO", (t + 1) * 128 + c0, (t + 1) * 128 + c1), lk, 7.5, ALU.add)
+            if t < DAYS - 1 and c1 % 64 == 0:
+                send(t + 1, [c1 // 64 - 1])
+            c0 = c1
+        if t < DAYS - 1:
+            act(C("LF", 0, 128), C("LK", 0, 128), AF.Identity)
+            act(C("LF", 128, 256), C("LK", 0, 128), AF.Identity)
+            ts(A("JW", t + 1, slice(0, 128)), C("LF", 0, 128), MAGIC, ALU.add, -MAGIC, ALU.add)
+
+    def bias(t):
+        part[0] += 1
+        e, k0, p0 = "E%d" % t, 0, part[0]
+        for n in ECH[t]:
+            act(C(e, k0 * 128, (k0 + n) * 128), IND(Ew, C("LO", (t + 1) * 128 + k0 * 8, (t + 1) * 128 + (k0 + n) * 8)), AF.Identity)
+            k0 += n
+        for k in range(16 if BIAS[t][0] == "whole" else 0):
+            ek, u, x, w0, w1 = C(e, k * 128, k * 128 + 128), C("U", 0, 128), C("X", 0, 128), (k % 2) * 256, (1 - k % 2) * 256
+            if k == 0:
+                ts(x, ek, 0.5, ALU.mult, m1, ALU.min)
+                ts(C("BA", w1 + 1, w1 + 256, 2), x, mn1, ALU.max)
+                continue
+            tt(u, ek, C("BA", w0 + 1, w0 + 256, 2), ALU.subtract)
+            ts(C("BA", w0, w0 + 256, 2), u, m2, ALU.min, mn2, ALU.max)
+            o, d1 = C("BA", w1, w1 + 256), C("BA", w0, w0 + 256)
+            add("dve", "tensor_tensor_scan", (o, C("SC", 0, 256), d1, 0.0, ALU.mult, ALU.add), [o], [C("SC", 0, 256), d1], vcost(256, 1))
+            if k == 15 and t < DAYS - 1:
+                cp(A("DV", 3), C("BA", w1 + 1, w1 + 256, 2))
+        for k in range(0 if BIAS[t][0] == "whole" else 16):
+            for h in range(2):
+                ek, u, x = C(e, k * 128 + h * 64, k * 128 + h * 64 + 64), C("U", h * 64, h * 64 + 64), C("X", h * 64, h * 64 + 64)
+                part[0] = p0 + h
+                mode = BIAS[t][h]
+                if mode == "act":
+                    b = C("BA", h * 128, h * 128 + 64)
+                    if k > 0:
+                        tt(u, ek, b, ALU.add)
+                    act(x, u if k > 0 else ek, AF.Relu, 0.5, C("BT", k, k + 1))
+                    act(x, x, AF.Relu, -1.0, m2)
+                    if k > 0:
+                        tt(b, x, b, ALU.add)
+                    else:
+                        cp(b, x)
+                    if k == 15:
+                        ts(A("DV", 3, h), b, -1.0, ALU.mult, C("BT", 16, 17), ALU.add)
+                elif mode == "pe":
+                    b = C("BA" if h == 0 else "BB", 0, 64)
+                    if k > 0:
+                        tt(u, ek, b, ALU.subtract)
+                        mm(b, C("If", 0, 128), ek, True, False)
+                        mm(b, C("nIf", 0, 128), u, False, False)
+                    ts(x, u if k > 0 else ek, m2, ALU.min, mn2, ALU.max)
+                    mm(b, C("Ih", 0, 128), x, k == 0, True)
+                    if k == 15:
+                        cp(A("DV", 3, h), b)
+                elif mode == "dve4" or k == 0:
+                    b = A("DV", 3, h) if mode == "dve4" else C("BA", 256 + h * 128 + 1, 256 + h * 128 + 128, 2)
+                    if k > 0:
+                        tt(u, ek, b, ALU.subtract)
+                    ts(x, u if k > 0 else ek, 0.5, ALU.mult, m1, ALU.min)
+                    if k > 0:
+                        ts(x, x, mn1, ALU.max)
+                        tt(b, x, b, ALU.add)
+                    else:
+                        ts(b, x, mn1, ALU.max)
+                else:
+                    w0, w1 = (k % 2) * 256 + h * 128, (1 - k % 2) * 256 + h * 128
+                    tt(u, ek, C("BA", w0 + 1, w0 + 128, 2), ALU.subtract)
+                    ts(C("BA", w0, w0 + 128, 2), u, m2, ALU.min, mn2, ALU.max)
+                    o, d1 = C("BA", w1, w1 + 128), C("BA", w0, w0 + 128)
+                    add("dve", "tensor_tensor_scan", (o, C("SC", 0, 128), d1, 0.0, ALU.mult, ALU.add), [o], [C("SC", 0, 128), d1],
+                        vcost(128, 1))
+                    if k == 15 and t < DAYS - 1:
+                        cp(A("DV", 3, h), C("BA", w1 + 1, w1 + 128, 2))
+        if t == DAYS - 1:
+            for h in range(2):
+                b, lo, sm = C("BA", h * 128 + 1, h * 128 + 128, 2), t * 128 + h * 64, C("SM" if h == 0 else "BB", 0, 64)
+                cp(C("YB", lo, lo + 64), b)
+                dma("act", C("yb", lo, lo + 64), C("YB", lo, lo + 64), 2.0)
+                k0 = 0
+                for n in TAILQ:
+                    for k in range(k0, k0 + n):
+                        tt(C("E0", h * 1024 + k * 64, h * 1024 + k * 64 + 64), C(e, k * 128 + h * 64, k * 128 + h * 64 + 64), b, ALU.subtract)
+                    eq = C("E0", h * 1024 + k0 * 64, h * 1024 + (k0 + n) * 64)
+                    act(eq, eq, AF.Abs)
+                    act(eq, eq, AF.Exp, -1.0)
+                    for k in range(k0, k0 + n):
+                        mm(sm, C("Ih", 0, 128), C("E0", h * 1024 + k * 64, h * 1024 + k * 64 + 64), k == 0, k == 15)
+                    k0 += n
+                ts(C("YS", lo, lo + 64), sm, 2.0, ALU.mult)
+                dma("sp", C("ys", lo, lo + 64), C("YS", lo, lo + 64), 2.0)
+            return
+        b = A("DV", 3)
+        if t < DAYS - 1:
+            tt(C("Ew", t, 2048, 16), C("ER", t * 128, t * 128 + 128), b, ALU.subtract)
+        yb, ys = C("YB", t * 128, t * 128 + 128), C("YS", t * 128, t * 128 + 128)
+        cp(yb, b)
+        dma("sp", C("yb", t * 128, t * 128 + 128), yb, 2.0)
+        for q in range(4):
+            eq = C(e, q * 512, q * 512 + 512)
+            if q < SUBPE[t]:
+                mm(C("BB", 0, 512), C("If", 0, 128), eq, True, False)
+                for k in range(4):
+                    mm(C("BB", k * 128, k * 128 + 128), C("nIf", 0, 128), yb, False, k == 3)
+                act(eq, C("BB", 0, 512), AF.Abs)
+            else:
+                for k in range(4 * q, 4 * q + 4):
+                    ek = C(e, k * 128, k * 128 + 128)
+                    tt(ek, ek, b, ALU.subtract)
+                act(eq, eq, AF.Abs)
+            act(eq, eq, AF.Exp, -1.0)
+            if not FOLD[t]:
+                for k in range(4 * q, 4 * q + 4):
+                    mm(C("SM", 0, 128), C("Ih", 0, 128), C(e, k * 128, k * 128 + 128), k == 0, k == 15)
+        if FOLD[t]:
+            s = add("pool", "fold", (t,), [], [C(e, 0, 2048)], 1.0, 1.0, "sent")
+            add("rx", "rx", (), [ys], [], 0.0, 9.0, "fo%d" % t, after=[s])
+        else:
+            act(ys, C("SM", 0, 128), AF.Identity, 2.0)
+        dma("sp", C("ys", t * 128, t * 128 + 128), ys, 2.0)
+
+    choose(0)
+    for t in range(DAYS):
+        if t + 1 < DAYS:
+            choose(t + 1)
+        bias(t)
+    return ops
+
+
+def kind(o):
+    a = o["args"]
+    return "%d%s%s" % (o["part"], o["eng"], a[0][0] if a and isap(a[0]) else o["call"])
+
+
+def replay(ops, seq, cost):
+    free, fin, ws, wx = {}, [0.0] * len(ops), cost["WS"], cost["WX"]
+    for i in seq:
+        o = ops[i]
+        e = o["eng"]
+        t = free.get(e, 0.0) if e != "rx" else 0.0
+        for d in o["deps"]:
+            a = ops[d]["eng"]
+            t = max(t, fin[d] + (0.0 if (a == e == "pe" or e == "rx") else (ws if a == e else wx)))
+        free[e] = t + o["busy"]
+        fin[i] = t + o["lat"]
+    return max(fin)
+
+
+def search(ops, tries):
+    sets = [(w, build(dict(COST, **v)), dict(COST, **v)) for w, v in VARY]
+    kinds = sorted(set(kind(o) for o in ops if o["eng"] != "rx"))
+    rs = np.random.RandomState(SEED)
+
+    def length(sh):
+        schedule(ops, sh)
+        seq = sorted(range(len(ops)), key=lambda j: (ops[j]["t"], j))
+        r = [replay(o, seq, c) for _, o, c in sets]
+        return sum(x * s[0] for x, s in zip(r, sets)) / sum(s[0] for s in sets), r
+    cur = {}
+    best = length(cur)
+    for _ in range(tries):
+        sh = dict(cur)
+        for _ in range(int(rs.randint(1, 4))):
+            k = kinds[int(rs.randint(len(kinds)))]
+            sh[k] = sh.get(k, 0.0) + float(rs.randn()) * (0.5, 3.0, 10.0)[int(rs.randint(3))]
+        new = length(sh)
+        if new[0] <= best[0]:
+            cur, best = sh, new
+    return cur, best
+
+
+def schedule(ops, shift):
+    n, WS, WX = len(ops), COST["WS"], COST["WX"]
+    succ = [[] for _ in range(n)]
+    for i, o in enumerate(ops):
+        for d in o["deps"]:
+            succ[d].append(i)
+
+    def gap(d, i):
+        a, b = ops[d]["eng"], ops[i]["eng"]
+        return 0.0 if (a == b == "pe" or b == "rx") else (WS if a == b else WX)
+    pr = [0.0] * n
+    for i in range(n - 1, -1, -1):
+        pr[i] = ops[i]["lat"] + max([gap(i, s) + pr[s] for s in succ[i]] + [0.0])
+    for i in range(n):
+        pr[i] += shift.get(kind(ops[i]), 0.0)
+    left = [len(o["deps"]) for o in ops]
+    rdy = [0.0] * n
+    ready = dict((e, []) for e in ("pe", "dve", "act", "pool", "sp", "rx"))
+    free = dict((e, 0.0) for e in ready)
+    order = dict((e, []) for e in ready)
+    for i in range(n):
+        if left[i] == 0:
+            ready[ops[i]["eng"]].append(i)
+    end = 0.0
+    for _ in range(n):
+        best = None
+        for e, r in ready.items():
+            if r:
+                t0 = max(free[e], min(rdy[i] for i in r))
+                if best is None or t0 < best[0]:
+                    best = (t0, e)
+        t0, e = best
+        i = max((j for j in ready[e] if rdy[j] <= t0 + 0.03), key=lambda j: pr[j])
+        ready[e].remove(i)
+        st = max(t0, rdy[i])
+        free[e] = st + ops[i]["busy"]
+        ops[i]["t"] = st
+        order[e].append(i)
+        end = max(end, st + ops[i]["lat"])
+        for s in succ[i]:
+            rdy[s] = max(rdy[s], st + ops[i]["lat"] + gap(i, s))
+            left[s] -= 1
+            if left[s] == 0:
+                ready[ops[s]["eng"]].append(s)
+    return order, end
+
+
+def waits(ops, order):
+    inc = set()
+    for i, o in enumerate(ops):
+        if o["eng"] != "rx":
+            inc.update(d for d in o["deps"] if not (o["eng"] == "pe" == ops[d]["eng"]))
+    tick, total = {}, {}
+    for e in order:
+        for i in order[e]:
+            if ops[i]["sem"] is None and i in inc:
+                total[e] = total.get(e, 0) + 1
+                tick[i] = (e, total[e])
+            elif ops[i]["sem"] is not None:
+                tick[i] = (ops[i]["sem"], 1)
+    know = dict((e, {}) for e in order)
+    after = {}
+    for i in sorted(range(len(ops)), key=lambda j: (ops[j]["t"], j)):
+        o = ops[i]
+        k = know[o["eng"]]
+        need = {}
+        if o["eng"] != "rx":
+            for d in sorted(o["deps"], key=lambda j: -ops[j]["t"]):
+                if o["eng"] == "pe" == ops[d]["eng"]:
+                    continue
+                s, v = tick[d]
+                if k.get(s, 0) < v:
+                    need[s] = max(need.get(s, 0), v)
+                    for s2, v2 in after[d].items():
+                        k[s2] = max(k.get(s2, 0), v2)
+        o["wait"] = need
+        o["tick"] = tick.get(i)
+        a = {} if o["eng"] == "rx" else dict(k)
+        if i in tick:
+            a[tick[i][0]] = max(a.get(tick[i][0], 0), tick[i][1])
+        after[i] = a
+    return total
+
+
+PLAN = {}
+
+
+def plan():
+    if not PLAN:
+        ops = build(COST)
+        shift, best = search(ops, TRIES)
+        order, end = schedule(ops, shift)
+        PLAN.update(best=best)
+        last = dict((ops[i]["grp"], i) for i in order["pe"] if ops[i]["grp"] is not None)
+        for i in last.values():
+            ops[i]["args"] = ops[i]["args"][:4] + (True,)
+        PLAN.update(ops=ops, order=order, end=end, total=waits(ops, order))
+    return PLAN
+
+
+def bits(engs):
+    return sum(1 << e for e in engs)
+
+
+def helpers(T, topo, r):
+    src, dst = T.cores[r], T.cores[(r + 1) % len(T.cores)]
+    free = sorted((c for c in topo.cores_of(src) if T.rank_of(c) is None), key=lambda c: (topo.die(c) != topo.die(src), c))
+    relays = [c for c in free if topo.may_write(c, dst)][:NCH]
+    return relays, [c for c in free if c not in relays][0]
+
+
+def helper_program(g, core, T, topo):
+    for r, src in enumerate(T.cores):
+        if core not in topo.cores_of(src):
+            continue
+        relays, fold = helpers(T, topo, r)
+        if core in relays:
+            c, dst = relays.index(core), T.cores[(r + 1) % len(T.cores)]
+            n_in = len(topo.engines(src, core)) // 2
+            out = topo.engines(core, dst)
+            rid, pid = topo.addr(dst, core)
+            for t in range(DAYS):
+                ap, sem = T.LA[:, t * 128 + c * 64:t * 128 + c * 64 + 64], T.sem["ar%d%d" % (t, c)]
+                g.wait_ge(sem, n_in)
+                g.remote_dma(ap, ap, sem, T.sem.sent, pid, rid, bits(out))
+            g.wait_ge(T.sem.sent, DAYS * len(out))
+        elif core == fold and any(FOLD):
+            n_in = len(topo.engines(src, core)) // 2
+            out = topo.engines(core, src)
+            rid, pid = topo.addr(src, core)
+            for t in range(DAYS):
+                if FOLD[t]:
+                    ap, sem = T.YS[:, t * 128:t * 128 + 128], T.sem["fo%d" % t]
+                    g.wait_ge(sem, n_in)
+                    g.remote_dma(ap, ap, sem, T.sem.sent, pid, rid, bits(out))
+            g.wait_ge(T.sem.sent, sum(FOLD) * len(out))
+
+
+def rank_program(g, core, T, topo):
+    r = T.rank_of(core)
+    if r is None:
+        return helper_program(g, core, T, topo)
+    p = plan()
+    ops = p["ops"]
+    relays, fold = helpers(T, topo, r)
+    before = helpers(T, topo, (r - 1) % len(T.cores))[0]
+    unit = dict((s, 16) for s in DMA_SEMS + ["cast"])
+    for t in range(DAYS):
+        unit["fo%d" % t] = len(topo.engines(fold, core))
+        for c in range(NCH):
+            unit["ar%d%d" % (t, c)] = len(topo.engines(before[c], core))
+    queue = {"pe": g.tensor, "dve": g.vector, "act": g.scalar, "pool": g, "sp": g.sync}
+    sent, used = [0], []
+
+    def ap(x):
+        if not isap(x):
+            return x
+        if x[0] == "*":
+            return ap(x[1]).indirect(ap(x[2]))
+        return T[x[0]][x[1]]
+
+    def dst_of(c):
+        rid, pid = topo.addr(c, core)
+        return DstId(rid=rid, pnc=pid)
+
+    for i in sorted(range(len(ops)), key=lambda j: (ops[j]["t"], j)):
+        o = ops[i]
+        if o["sem"] not in (None, "sent"):
+            used.append(o["sem"])
+        if o["eng"] == "rx":
+            continue
+        q, a, call = queue[o["eng"]], [ap(x) for x in o["args"]], o["call"]
+        for s, v in o["wait"].items():
+            q.wait_ge(T.sem[s], v * unit.get(s, 1))
+        if call == "send":
+            t, tr = a[0], []
+            for j, c in enumerate(a[1]):
+                en = topo.engines(core, relays[c])
+                en = en[j * len(en) // 2:(j + 1) * len(en) // 2]
+                lo = t * 128 + c * 64
+                tr.append(RemoteDMATransfer(dst_ids=[dst_of(relays[c])], dma_engine_mask=bits(en), remote_sem=T.sem["ar%d%d" % (t, c)],
+                                            src=T.LO[:, lo:lo + 64], dst=T.LA[:, lo:lo + 64]))
+                sent[0] += len(en)
+            g.remote_dma_fused(tr, local_sem=T.sem.sent)
+            continue
+        if call == "fold":
+            t = a[0]
+            en = topo.engines(core, fold)
+            en = en[len(en) // 2:]
+            g.remote_dma_fused([RemoteDMATransfer(dst_ids=[dst_of(fold)], dma_engine_mask=bits(en), remote_sem=T.sem["fo%d" % t],
+                                                  srcs=[T["E%d" % t][:, k * 128:k * 128 + 128] for k in range(16)],
+                                                  dsts=[T.YS[:, t * 128:t * 128 + 128]], alu_op=1)], local_sem=T.sem.sent)
+            sent[0] += len(en)
+            continue
+        if call == "iota":
+            ins = g.iota(T.IO[:], [[1, 256]], 0, -1)
+        elif call == "dma_start":
+            ins = q.dma_start(a[0], a[1])
+        elif call == "activation":
+            ins = q.activation(a[0], a[1], a[2], bias=a[4], scale=a[3])
+        elif call == "matmul":
+            ins = q.matmul(*a)
+        elif call == "tensor_copy":
+            ins = q.tensor_copy(*a)
+        elif call == "tensor_scalar":
+            ins = q.tensor_scalar(*a)
+        elif call == "tensor_tensor":
+            ins = q.tensor_tensor(*a)
+        elif call == "tensor_tensor_scan":
+            ins = q.tensor_tensor_scan(*a)
+        else:
+            ins = q.memset(*a)
+        if o["tick"]:
+            ins.then_inc(T.sem[o["tick"][0]], unit.get(o["tick"][0], 1))
+    g.wait_ge(T.sem.sent, sent[0])
+    for s, v in p["total"].items():
+        g.wait_ge(T.sem[s], v)
+    for s in used:
+        g.wait_ge(T.sem[s], unit[s])

@@ -4,18 +4,21 @@ from concourse.mybir import AluOpType as ALU, ActivationFunctionType as AF
 
 DAYS = 3
 NCH = 2
-BIAS = (("whole", "whole"), ("whole", "whole"), ("dve3", "dve3"))
+BIAS = (("dve3", "dve3"), ("dve3", "dve3"), ("dve3", "dve3"))
 ACTG = ((4, 6), (0, 4, 6), (0, 1, 2, 4, 6))
-LOOK = (((8, "act"), (8, "dve")), ((8, "act"), (8, "act")), ((2, "act"), (4, "act"), (4, "act"), (6, "act")))
+LOOK = (((8, "act"), (8, "dve")), ((8, "act"), (8, "act")), ((4, "act"), (4, "dve"), (8, "act")))
 FOLD = (False, False, False)
 SUBPE = (0, 0, 0)
 VOIDW = True
+FUSE = (True, False, False)
+SUBDMA = (4, 4, 0)
 TAILQ = (4, 4, 4, 2, 2)
-ECH = ((4, 4, 4, 4), (4, 4, 4, 4), (2, 4, 4, 6))
-COST = dict(CY=0.00083 * 1.25, GA=1.56, PCY=0.00042 * 1.25, WS=0.06, WX=0.10, HOP=5.0, FIX=0.02)
-VARY = ((2, {}), (0.5, dict(PCY=0.00105)), (1, dict(WS=0.15, WX=0.2)), (1, dict(GA=1.04, HOP=3.5)), (1, dict(GA=2.08, HOP=6.5)),
-        (1, dict(CY=0.00083, HOP=6.0)), (1, dict(FIX=0.05)), (1, dict(FIX=0.0)))
-TRIES, SEED = 1000, 0
+ECH = ((4, 4, 4, 4), (4, 4, 4, 4), (2, 2, 4, 4, 4))
+COST = dict(CY=0.0012, GA=1.7, PCY=0.0006, WS=0.17, WX=0.18, HOP=6.5, FIX=0.01)
+VARY = ((1, dict(CY=0.00087, PCY=0.00045, WS=0.2, WX=0.2)), (3, dict(CY=0.00125, GA=2.0, PCY=0.00063, FIX=0.015, WS=0.2, WX=0.2)),
+        (2, dict(CY=0.00125, GA=1.3, PCY=0.00063, FIX=0.015, WS=0.12, WX=0.15)),
+        (0.5, dict(CY=0.0011, PCY=0.0007, FIX=0.015, WS=0.25, WX=0.25, HOP=8.0)))
+TRIES, SEED = 1500, 3
 
 B5 = [128, 2, 2, 2, 2, 8]
 SCRATCH = {
@@ -37,10 +40,13 @@ SCRATCH = {
     "KI": ("sbuf", B5, "int32"), "O32": ("sbuf", [128, 128], "int32"), "D32": ("sbuf", [128, 128], "int32"),
     "O16": ("sbuf", [128, 128], "uint16"), "E0": ("sbuf", [128, 2048], "float32"), "E1": ("sbuf", [128, 2048], "float32"),
     "E2": ("sbuf", [128, 2048], "float32"), "U": ("sbuf", [128, 128], "float32"), "X": ("sbuf", [128, 128], "float32"),
+    "V": ("sbuf", [128, 800], "float32"), "S3": ("sbuf", [128, 192], "float32"),
+    "NB": ("sbuf", [128, 1024], "float32"),
     "YB": ("sbuf", [128, 384], "float32"), "YS": ("sbuf", [128, 384], "float32"),
 }
 DMA_SEMS = ["d%d" % i for i in range(20)]
-SEMAPHORES = (["pe", "dve", "act", "pool", "sent", "cast"] + DMA_SEMS + ["ar%d%d" % (t, c) for t in range(DAYS) for c in range(NCH)]
+ADD_SEMS = ["ad%d%d" % (t, q) for t in range(DAYS - 1) for q in range(4)]
+SEMAPHORES = (["pe", "dve", "act", "pool", "sent", "cast"] + DMA_SEMS + ADD_SEMS + ["ar%d%d" % (t, c) for t in range(DAYS) for c in range(NCH)]
               + ["fo%d" % t for t in range(DAYS)])
 EXT = {"pa": [128, 2048], "ea": [128, 2048], "nd": [128, 128], "fc": [128, 384], "er": [128, 384], "dl": [128, 1],
        "yb": [128, 384], "ys": [128, 384]}
@@ -195,9 +201,9 @@ def build(cost):
         ms(row(256 + 128 * k, 384 + 128 * k), v)
     ms(C("SC", 0, 256, 2), 0.0)
     ms(C("SC", 1, 256, 2), 0.5)
-    cp(C("LO", 0, 128), C("ND", 0, 128))
+    first = cp(C("LO", 0, 128), C("ND", 0, 128))
     send(0, list(range(NCH)))
-    dma("pool", C("Ew", 0, 2048), C("ea", 0, 2048), 5.0)
+    add("pool", "dma_start", (C("Ew", 0, 2048), C("ea", 0, 2048)), [C("Ew", 0, 2048)], [], 2.0, 6.0, "cast", after=[first])
     cp(C("PT", 0, 128), C("Pb", 15, 2063, 16))
     cp(C("Pb", 31, 2064, 16), C("PT", 0, 128))
     for k, v in enumerate((1.0, -1.0, 2.0, -2.0)):
@@ -301,7 +307,7 @@ def build(cost):
         act(A("KS"), C("KO", 0, 128), AF.Identity)
         distances(t, 1)
         if t < DAYS - 1:
-            cp(C("Pb", 31 if t == 0 else 15 + t, 2064, 16), A("FR", t, slice(0, 128)))
+            act(C("Pb", 31 if t == 0 else 15 + t, 2064, 16), A("FR", t, slice(0, 128)), AF.Identity)
         sort()
         ts(C("O32", 0, 128), A("KI"), 5, ALU.arith_shift_right, 255, ALU.bitwise_and)
         cp(C("O16", 0, 128), C("O32", 0, 128))
@@ -320,8 +326,8 @@ def build(cost):
             for il in range(16):
                 mm(lk, C("Dm", il * 128, il * 128 + 128), C("JG", c0 * 16 + il, c1 * 16, 16), False, il == 15)
             ts(C("LO", (t + 1) * 128 + c0, (t + 1) * 128 + c1), lk, 7.5, ALU.add)
-            if t < DAYS - 1 and c1 % 64 == 0:
-                send(t + 1, [c1 // 64 - 1])
+            if t < DAYS - 1 and c1 % 64 == 0 and (c1 == 128 or not FUSE[t + 1]):
+                send(t + 1, [0, 1] if FUSE[t + 1] else [c1 // 64 - 1])
             c0 = c1
         if t < DAYS - 1:
             act(C("LF", 0, 128), C("LK", 0, 128), AF.Identity)
@@ -331,6 +337,10 @@ def build(cost):
     def bias(t):
         part[0] += 1
         e, k0, p0 = "E%d" % t, 0, part[0]
+        tri, direct = BIAS[t][0] == "tri", SUBDMA[t] == 4 and BIAS[t] == ("dve3", "dve3")
+        if tri:
+            for j, v in enumerate((0.0, 1.0, -0.5)):
+                ms(C("S3", j, 192, 3), v)
         for n in ECH[t]:
             act(C(e, k0 * 128, (k0 + n) * 128), IND(Ew, C("LO", (t + 1) * 128 + k0 * 8, (t + 1) * 128 + (k0 + n) * 8)), AF.Identity)
             k0 += n
@@ -351,7 +361,21 @@ def build(cost):
                 ek, u, x = C(e, k * 128 + h * 64, k * 128 + h * 64 + 64), C("U", h * 64, h * 64 + 64), C("X", h * 64, h * 64 + 64)
                 part[0] = p0 + h
                 mode = BIAS[t][h]
-                if mode == "act":
+                if mode == "tri":
+                    w0, w1 = (2 * h + k % 2) * 200, (2 * h + 1 - k % 2) * 200
+                    x = C("V", w0 + 2, w0 + 193, 3)
+                    if k == 0:
+                        ms(C("V", w0 + 1, w0 + 193, 3), 0.0)
+                    if k < 15:
+                        cp(C("V", w0 + 3, w0 + 194, 3), C(e, (k + 1) * 128 + h * 64, (k + 1) * 128 + h * 64 + 64))
+                    else:
+                        ms(C("V", w0 + 3, w0 + 194, 3), 0.0)
+                    ts(x, x if k > 0 else ek, m2, ALU.min, mn2, ALU.max)
+                    d1 = C("V", w0 + 1, w0 + 193)
+                    o = C("V", w1, w1 + 192) if k < 15 else C("BA", h * 192, h * 192 + 192)
+                    add("dve", "tensor_tensor_scan", (o, C("S3", 0, 192), d1, 0.0, ALU.mult, ALU.add), [o], [C("S3", 0, 192), d1],
+                        vcost(192, 1))
+                elif mode == "act":
                     b = C("BA", h * 128, h * 128 + 64)
                     if k > 0:
                         tt(u, ek, b, ALU.add)
@@ -390,17 +414,27 @@ def build(cost):
                     o, d1 = C("BA", w1, w1 + 128), C("BA", w0, w0 + 128)
                     add("dve", "tensor_tensor_scan", (o, C("SC", 0, 128), d1, 0.0, ALU.mult, ALU.add), [o], [C("SC", 0, 128), d1],
                         vcost(128, 1))
-                    if k == 15 and t < DAYS - 1:
+                    if k == 15 and direct:
+                        lo, bh = t * 128 + h * 64, C("BA", w1 + 1, w1 + 128, 2)
+                        tt(C("Ew", t + h * 1024, (h + 1) * 1024, 16), C("ER", lo, lo + 64), bh, ALU.subtract)
+                        cp(C("YB", lo, lo + 64), bh)
+                    elif k == 15 and t < DAYS - 1:
                         cp(A("DV", 3, h), C("BA", w1 + 1, w1 + 128, 2))
         if t == DAYS - 1:
             for h in range(2):
                 b, lo, sm = C("BA", h * 128 + 1, h * 128 + 128, 2), t * 128 + h * 64, C("SM" if h == 0 else "BB", 0, 64)
-                cp(C("YB", lo, lo + 64), b)
+                if tri:
+                    b = C("BA", h * 192 + 2, h * 192 + 192, 3)
+                    ts(C("YB", lo, lo + 64), b, -1.0, ALU.mult)
+                else:
+                    cp(C("YB", lo, lo + 64), b)
                 dma("act", C("yb", lo, lo + 64), C("YB", lo, lo + 64), 2.0)
                 k0 = 0
                 for n in TAILQ:
                     for k in range(k0, k0 + n):
-                        tt(C("E0", h * 1024 + k * 64, h * 1024 + k * 64 + 64), C(e, k * 128 + h * 64, k * 128 + h * 64 + 64), b, ALU.subtract)
+                        r0 = k * 128 + h * 64
+                        tt(C("E0", h * 1024 + k * 64, h * 1024 + k * 64 + 64), C(e, r0, r0 + 64),
+                           b, ALU.add if tri else ALU.subtract)
                     eq = C("E0", h * 1024 + k0 * 64, h * 1024 + (k0 + n) * 64)
                     act(eq, eq, AF.Abs)
                     act(eq, eq, AF.Exp, -1.0)
@@ -411,14 +445,20 @@ def build(cost):
                 dma("sp", C("ys", lo, lo + 64), C("YS", lo, lo + 64), 2.0)
             return
         b = A("DV", 3)
-        if t < DAYS - 1:
-            tt(C("Ew", t, 2048, 16), C("ER", t * 128, t * 128 + 128), b, ALU.subtract)
         yb, ys = C("YB", t * 128, t * 128 + 128), C("YS", t * 128, t * 128 + 128)
-        cp(yb, b)
+        if not direct:
+            tt(C("Ew", t, 2048, 16), C("ER", t * 128, t * 128 + 128), b, ALU.subtract)
+            cp(yb, b)
         dma("sp", C("yb", t * 128, t * 128 + 128), yb, 2.0)
         for q in range(4):
             eq = C(e, q * 512, q * 512 + 512)
-            if q < SUBPE[t]:
+            if q < SUBDMA[t]:
+                nb = C("NB", t * 512, t * 512 + 512)
+                for k in range(4 if q == 0 else 0):
+                    act(C("NB", t * 512 + k * 128, t * 512 + k * 128 + 128), yb, AF.Identity, -1.0)
+                add("pool", "dma_add", (eq, nb), [eq], [nb], 1.2, 4.5, "ad%d%d" % (t, q))
+                act(eq, eq, AF.Abs)
+            elif q < SUBPE[t]:
                 mm(C("BB", 0, 512), C("If", 0, 128), eq, True, False)
                 for k in range(4):
                     mm(C("BB", k * 128, k * 128 + 128), C("nIf", 0, 128), yb, False, k == 3)
@@ -607,12 +647,12 @@ def helper_program(g, core, T, topo):
         relays, fold = helpers(T, topo, r)
         if core in relays:
             c, dst = relays.index(core), T.cores[(r + 1) % len(T.cores)]
-            n_in = len(topo.engines(src, core)) // 2
+            n_in = len(topo.engines(src, core))
             out = topo.engines(core, dst)
             rid, pid = topo.addr(dst, core)
             for t in range(DAYS):
                 ap, sem = T.LA[:, t * 128 + c * 64:t * 128 + c * 64 + 64], T.sem["ar%d%d" % (t, c)]
-                g.wait_ge(sem, n_in)
+                g.wait_ge(sem, n_in // NCH if FUSE[t] else n_in)
                 g.remote_dma(ap, ap, sem, T.sem.sent, pid, rid, bits(out))
             g.wait_ge(T.sem.sent, DAYS * len(out))
         elif core == fold and any(FOLD):
@@ -635,7 +675,7 @@ def rank_program(g, core, T, topo):
     ops = p["ops"]
     relays, fold = helpers(T, topo, r)
     before = helpers(T, topo, (r - 1) % len(T.cores))[0]
-    unit = dict((s, 16) for s in DMA_SEMS + ["cast"])
+    unit = dict((s, 16) for s in DMA_SEMS + ADD_SEMS + ["cast"])
     for t in range(DAYS):
         unit["fo%d" % t] = len(topo.engines(fold, core))
         for c in range(NCH):
@@ -667,7 +707,7 @@ def rank_program(g, core, T, topo):
             t, tr = a[0], []
             for j, c in enumerate(a[1]):
                 en = topo.engines(core, relays[c])
-                en = en[j * len(en) // 2:(j + 1) * len(en) // 2]
+                en = en[j * len(en) // len(a[1]):(j + 1) * len(en) // len(a[1])]
                 lo = t * 128 + c * 64
                 tr.append(RemoteDMATransfer(dst_ids=[dst_of(relays[c])], dma_engine_mask=bits(en), remote_sem=T.sem["ar%d%d" % (t, c)],
                                             src=T.LO[:, lo:lo + 64], dst=T.LA[:, lo:lo + 64]))
@@ -687,6 +727,8 @@ def rank_program(g, core, T, topo):
             ins = g.iota(T.IO[:], [[1, 256]], 0, -1)
         elif call == "dma_start":
             ins = q.dma_start(a[0], a[1])
+        elif call == "dma_add":
+            ins = q.dma_start(a[0], a[1], accum_op=ALU.add)
         elif call == "activation":
             ins = q.activation(a[0], a[1], a[2], bias=a[4], scale=a[3])
         elif call == "matmul":

@@ -3,51 +3,46 @@ from concourse.bass import DstId, RemoteDMATransfer
 from concourse.mybir import AluOpType as ALU, ActivationFunctionType as AF
 
 DAYS = 3
-NCH = 2
-BIAS = (("dve3", "dve3"), ("dve3", "dve3"), ("dve3", "dve3"))
-ACTG = ((4, 6), (0, 4, 6), (0, 1, 2, 4, 6))
-LOOK = (((8, "act"), (8, "dve")), ((8, "act"), (8, "act")), ((4, "act"), (4, "dve"), (8, "act")))
-FOLD = (False, False, False)
-SUBPE = (0, 0, 0)
-VOIDW = True
-FUSE = (True, False, False)
-SUBDMA = (4, 4, 0)
-TAILQ = (4, 4, 4, 2, 2)
-ECH = ((4, 4, 4, 4), (4, 4, 4, 4), (2, 2, 4, 4, 4))
-COST = dict(CY=0.0012, GA=1.7, PCY=0.0006, WS=0.17, WX=0.18, HOP=6.5, FIX=0.01)
-VARY = ((1, dict(CY=0.00087, PCY=0.00045, WS=0.2, WX=0.2)), (3, dict(CY=0.00125, GA=2.0, PCY=0.00063, FIX=0.015, WS=0.2, WX=0.2)),
-        (2, dict(CY=0.00125, GA=1.3, PCY=0.00063, FIX=0.015, WS=0.12, WX=0.15)),
-        (0.5, dict(CY=0.0011, PCY=0.0007, FIX=0.015, WS=0.25, WX=0.25, HOP=8.0)))
-TRIES, SEED = 1500, 3
+PAR = dict(
+    OWN=(("mm", "mm"), ("mm", "mm"), ("mm", "mm")),
+    ARR=(("ma", "ma"), ("aa", "aa"), ("aa", "aa")),
+    LOOK=(("8a8v", "8a8a"), ("8a8a", "8a8a"), ("8a8a", "8a8v")),
+    BIAS=(("pz", "pz"), ("dve3", "dve3"), ("tri", "tri")),
+    TRICP="dve", SUBS=(1, 1),
+    ECH=(("8a8a", "8a8a"), ("4a4a8a", "4a4a8a"), ("4a4a8a", "4a4a8a")),
+    BACK=5, SHIFT={}, SUBPE=(0, 0), PAIR=True, DADD=(0, 0), EARLY=0.5, NG=2, PUPD="a", NACT=8, EC=False, NREP=8, TAILQ=(4, 4, 4, 2, 2), FUSE0=True,
+)
+COST = dict(CY=0.001044, GA=1.55, PCY=0.000684, WS=0.21, WX=0.21, HOP=6.2, FIX=0.012)
+VARY = ((1, {}),)
+TRIES, SEED = 4000, 6
 
-B5 = [128, 2, 2, 2, 2, 8]
+F32, BF = "float32", "bfloat16"
 SCRATCH = {
-    "KO": ("psum", [128, 512], "float32"), "KA": ("psum", [128, 512], "float32"), "LK": ("psum", [128, 512], "float32"),
-    "SM": ("psum", [128, 512], "float32"), "BA": ("psum", [128, 512], "float32"), "BB": ("psum", [128, 512], "float32"),
-    "SB": ("psum", [128, 512], "float32"), "DV": ("psum", [128, 4, 2, 2, 2, 2, 8], "float32"),
-    "ND": ("sbuf", [128, 128], "int32"), "Pb": ("sbuf", [128, 2064], "bfloat16"), "Ew": ("sbuf", [128, 2048], "float32"),
-    "FR": ("sbuf", [128, 3, 512], "bfloat16"), "ER": ("sbuf", [128, 384], "bfloat16"), "DL": ("sbuf", [128, 4], "float32"),
-    "BT": ("sbuf", [128, 20], "float32"), "MM": ("sbuf", [128, 4], "float32"), "IO": ("sbuf", [128, 256], "int32"), "TI": ("sbuf", [128, 16], "int32"),
-    "TF": ("sbuf", [128, 32], "float32"), "Ib": ("sbuf", [128, 128], "bfloat16"), "nIb": ("sbuf", [128, 128], "bfloat16"),
-    "Ibig": ("sbuf", [128, 128], "bfloat16"), "Ih": ("sbuf", [128, 128], "float32"), "Z": ("sbuf", [128, 144], "bfloat16"),
-    "If": ("sbuf", [128, 128], "float32"), "nIf": ("sbuf", [128, 128], "float32"),
-    "Dm": ("sbuf", [128, 2048], "bfloat16"), "CR": ("sbuf", [128, 768], "bfloat16"), "SC": ("sbuf", [128, 256], "float32"),
-    "PT": ("sbuf", [128, 128], "bfloat16"), "AB": ("sbuf", [128, 4096], "bfloat16"), "PG": ("sbuf", [128, 1024], "bfloat16"),
-    "EQ": ("sbuf", [128, 2048], "bfloat16"), "JG": ("sbuf", [128, 2048], "bfloat16"), "JW": ("sbuf", [128, 3, 256], "bfloat16"),
-    "RR": ("sbuf", [128, 4, 256], "bfloat16"), "LF": ("sbuf", [128, 256], "float32"),
-    "LO": ("sbuf", [128, 512], "uint16"), "LA": ("sbuf", [128, 384], "uint16"),
-    "KS": ("sbuf", B5, "float32"), "S0": ("sbuf", B5, "float32"), "S1": ("sbuf", B5, "float32"), "ZZ": ("sbuf", B5, "float32"),
-    "KI": ("sbuf", B5, "int32"), "O32": ("sbuf", [128, 128], "int32"), "D32": ("sbuf", [128, 128], "int32"),
-    "O16": ("sbuf", [128, 128], "uint16"), "E0": ("sbuf", [128, 2048], "float32"), "E1": ("sbuf", [128, 2048], "float32"),
-    "E2": ("sbuf", [128, 2048], "float32"), "U": ("sbuf", [128, 128], "float32"), "X": ("sbuf", [128, 128], "float32"),
-    "V": ("sbuf", [128, 800], "float32"), "S3": ("sbuf", [128, 192], "float32"),
-    "NB": ("sbuf", [128, 1024], "float32"),
-    "YB": ("sbuf", [128, 384], "float32"), "YS": ("sbuf", [128, 384], "float32"),
+    "K0": ("psum", [128, 512], F32), "K1": ("psum", [128, 512], F32), "B0": ("psum", [128, 512], F32), "B1": ("psum", [128, 512], F32),
+    "D0": ("psum", [128, 8, 2, 2, 2, 2, 4], F32), "D1": ("psum", [128, 8, 2, 2, 2, 2, 4], F32),
+    "SB": ("psum", [128, 512], F32), "SM": ("psum", [128, 512], F32),
+    "ND": ("sbuf", [128, 16, 2, 4], "int32"), "P0": ("sbuf", [128, 2064], BF), "P1": ("sbuf", [128, 2064], BF),
+    "P2": ("sbuf", [128, 2064], BF), "PT": ("sbuf", [128, 128], BF), "Ew": ("sbuf", [128, 2048], F32), "Es": ("sbuf", [128, 2064], F32),
+    "FC": ("sbuf", [128, 384], BF), "FR": ("sbuf", [128, 3072], BF), "ER": ("sbuf", [128, 384], BF), "DL": ("sbuf", [128, 4], F32),
+    "MM": ("sbuf", [128, 4], F32), "IO": ("sbuf", [128, 256], "int32"), "TI": ("sbuf", [128, 24], "int32"), "TF": ("sbuf", [128, 40], F32),
+    "Ib": ("sbuf", [128, 128], BF), "nIb": ("sbuf", [128, 128], BF), "Ibig": ("sbuf", [128, 128], BF), "Ih": ("sbuf", [128, 128], F32),
+    "If": ("sbuf", [128, 128], F32), "nIf": ("sbuf", [128, 128], F32), "Zp": ("sbuf", [128, 144], BF), "Zn": ("sbuf", [128, 144], BF),
+    "Dm": ("sbuf", [128, 2048], BF), "CR": ("sbuf", [128, 640], BF), "WR": ("sbuf", [128, 768], BF), "SC": ("sbuf", [128, 128], F32), "S3": ("sbuf", [128, 192], F32),
+    "AX": ("sbuf", [128, 4096], BF), "AB": ("sbuf", [128, 4096], BF), "PG": ("sbuf", [128, 1024], BF), "EQ": ("sbuf", [128, 2048], BF),
+    "JG": ("sbuf", [128, 2048], BF), "JW": ("sbuf", [128, 768], BF), "RR": ("sbuf", [128, 1024], BF), "LF": ("sbuf", [128, 256], F32),
+    "LL": ("sbuf", [128, 1024], "uint16"),
+    "H": ("sbuf", [128, 4, 2, 2, 2, 2, 4], F32), "Y0": ("sbuf", [128, 2, 2, 2, 2, 2, 4], F32),
+    "Y1": ("sbuf", [128, 2, 2, 2, 2, 2, 4], F32), "Y2": ("sbuf", [128, 2, 2, 2, 2, 2, 4], F32), "Y3": ("sbuf", [128, 2, 2, 2, 2, 2, 4], F32), "KI": ("sbuf", [128, 2, 2, 2, 2, 2, 4], "int32"),
+    "O32": ("sbuf", [128, 128], "int32"), "D32": ("sbuf", [128, 128], "int32"), "O16": ("sbuf", [128, 128], "uint16"),
+    "E": ("sbuf", [128, 6144], F32), "EC": ("sbuf", [128, 4096], F32), "X2": ("sbuf", [128, 2048], F32),
+    "U": ("sbuf", [128, 128], F32), "X": ("sbuf", [128, 128], F32), "V": ("sbuf", [128, 1600], F32), "NB": ("sbuf", [128, 4096], F32),
+    "EB": ("sbuf", [128, 2048], BF), "WB": ("sbuf", [128, 4096], BF), "WF": ("sbuf", [128, 4096], F32), "I2": ("sbuf", [128, 128], F32),
+    "MK": ("sbuf", [128, 32], F32), "BT": ("sbuf", [128, 20], F32), "SN": ("sbuf", [128, 128], F32),
+    "YB": ("sbuf", [128, 384], F32), "YS": ("sbuf", [128, 384], F32),
 }
-DMA_SEMS = ["d%d" % i for i in range(20)]
-ADD_SEMS = ["ad%d%d" % (t, q) for t in range(DAYS - 1) for q in range(4)]
-SEMAPHORES = (["pe", "dve", "act", "pool", "sent", "cast"] + DMA_SEMS + ADD_SEMS + ["ar%d%d" % (t, c) for t in range(DAYS) for c in range(NCH)]
-              + ["fo%d" % t for t in range(DAYS)])
+DMA_SEMS = ["d%d" % i for i in range(40)]
+POOL_SEMS = ["p%d" % i for i in range(30)]
+SEMAPHORES = ["pe", "dve", "act", "pool", "sent"] + DMA_SEMS + POOL_SEMS + ["ar%d%d" % (t, h) for t in range(DAYS) for h in range(2)]
 EXT = {"pa": [128, 2048], "ea": [128, 2048], "nd": [128, 128], "fc": [128, 384], "er": [128, 384], "dl": [128, 1],
        "yb": [128, 384], "ys": [128, 384]}
 S_ = slice(None)
@@ -59,8 +54,8 @@ def A(name, *key):
     return (name, (S_,) + tuple(key))
 
 
-def C(name, a, b, step=None):
-    return A(name, slice(a, b, step))
+def C(name, a, n, step=1):
+    return A(name, slice(a, a + (n - 1) * step + 1, step if step > 1 else None))
 
 
 def IND(win, off):
@@ -81,18 +76,45 @@ def where(ap):
 
 
 def width(ap):
-    return 2 if SCRATCH[ap[0]][2] in ("bfloat16", "uint16") else 4
+    return 2 if SCRATCH[ap[0]][2] in (BF, "uint16") else 4
 
 
 def isap(x):
     return isinstance(x, tuple)
 
 
-def build(cost):
-    CY, GA, PCY, HOP, FIX = cost["CY"], cost["GA"], cost["PCY"], cost["HOP"], cost["FIX"]
-    ops, hist, bank, ndma, part = [], {}, {}, [0], [0]
+def shapes():
+    ng = PAR["NG"]
+    nb = 8 // ng
+    SCRATCH.update({"ND": ("sbuf", [128, 16, ng, nb], "int32"), "H": ("sbuf", [128, 4, 2, 2, 2, 2, nb], F32),
+                    "KI": ("sbuf", [128, ng, 2, 2, 2, 2, nb], "int32")})
+    for j in range(4):
+        SCRATCH["Y%d" % j] = ("sbuf", [128, 2, 2, 2, 2, 2, nb], F32)
+    for j in range(2):
+        SCRATCH["D%d" % j] = ("psum", [128, 32 // nb, 2, 2, 2, 2, nb], F32)
 
-    def add(eng, call, args, outs, ins, busy, lat=None, sem=None, after=(), grp=None):
+
+shapes()
+
+
+def unit(u):
+    return (u, 0) if PAR["NG"] == 2 else (0, 64 * u)
+
+
+def own_list(t, h, a=0, n=64):
+    return C("LL", t * 256 + h * 128 + a, n)
+
+
+def arr_list(t, h, a=0, n=64):
+    return C("LL", t * 256 + h * 128 + 128 // PAR["NG"] + a, n)
+
+
+def build():
+    ops, hist, bank, nsem, part, npg = [], {}, {}, {"hw": 0, "pool": 0}, [""], [0]
+    NG = PAR["NG"]
+    W, NB = 128 // NG, 8 // NG
+
+    def add(eng, call, args, outs, ins, busy, lat=0.0, sem=None, after=(), grp=None):
         i = len(ops)
         deps = dict((d, True) for d in after)
         flat = []
@@ -121,19 +143,19 @@ def build(cost):
             b[1].append(i)
         if grp is not None:
             deps = dict((d, True) for d in deps if ops[d]["grp"] != grp or d in after)
-        ops.append(dict(grp=grp, part=part[0], eng=eng, call=call, args=args, deps=sorted(deps), busy=busy, lat=busy if lat is None else lat, sem=sem))
+        ops.append(dict(grp=grp, part=part[0], eng=eng, call=call, args=args, deps=sorted(deps), busy=busy, lat=lat, sem=sem))
         return i
 
     def n_of(ap):
         return 16 * len(elems(ap[2])) if ap[0] == "*" else len(elems(ap))
 
-    def vcost(n, c):
-        return FIX + max(64, n * c) * CY
+    def cyc(n):
+        return (0.0, max(64, n), 0, 0)
 
     def one(out, x):
         if x[0] == "*":
-            return 0.05 + n_of(x) * GA * CY
-        return vcost(n_of(x), 0.5 if width(out) == 2 and width(x) == 2 else 1)
+            return (0.05, 0, n_of(x), 0)
+        return cyc(n_of(x) * (0.5 if width(out) == 2 and width(x) == 2 else 1))
 
     def cp(out, x):
         return add("dve", "tensor_copy", (out, x), [out], [x], one(out, x))
@@ -143,132 +165,252 @@ def build(cost):
         return add("dve", "tensor_scalar", a, [out], [x] + [s for s in (s1, s2) if isap(s)], one(out, x))
 
     def tt(out, x, y, op):
-        c = one(out, x) if x[0] == "*" else vcost(n_of(x), 2 if where(x) == where(y) == "sbuf" else 1)
+        c = one(out, x) if x[0] == "*" else cyc(n_of(x) * (2 if where(x) == where(y) == "sbuf" else 1))
         return add("dve", "tensor_tensor", (out, x, y, op), [out], [x, y], c)
 
-    def ms(out, v):
-        return add("dve", "memset", (out, v), [out], [], vcost(n_of(out), width(out) / 4))
+    def scan(out, d0, d1):
+        return add("dve", "tensor_tensor_scan", (out, d0, d1, 0.0, ALU.mult, ALU.add), [out], [d0, d1], cyc(n_of(d1)))
 
-    def act(out, x, f, scale=1.0, bias=0.0):
-        c = 0.065 + n_of(x) * GA * CY if x[0] == "*" else vcost(n_of(x), 1)
+    def ms(out, v):
+        return add("dve", "memset", (out, v), [out], [], cyc(n_of(out) * width(out) / 4))
+
+    def act(out, x, f=AF.Identity, scale=1.0, bias=0.0):
+        c = (0.065, 0, n_of(x), 0) if x[0] == "*" else cyc(n_of(x))
         return add("act", "activation", (out, x, f, scale, bias), [out], [x] + [s for s in (bias,) if isap(s)], c)
 
+    def move(who, out, x):
+        return act(out, x) if who in ("a", "act") else cp(out, x)
+
     def mm(out, l, r, start, stop, grp=None, after=()):
-        c = max(64, n_of(r)) * PCY * (4 if width(r) == 4 else 1)
+        c = (0.0, 0, 0, max(64, n_of(r)) * (4 if width(r) == 4 else 1))
         return add("pe", "matmul", (out, l, r, start, stop), [out], [l, r], c, grp=grp, after=after)
 
-    def dma(q, out, x, lat):
-        if q == "pool":
-            return add(q, "dma_start", (out, x), [out], [x], 1.0, lat, "cast")
-        ndma[0] += 1
-        return add(q, "dma_start", (out, x), [out], [x], 0.1, lat, DMA_SEMS[ndma[0] - 1])
+    def dma(q, out, x, lat, call="dma_start", after=()):
+        k = "pool" if q == "pool" else "hw"
+        nsem[k] += 1
+        sem = (POOL_SEMS if q == "pool" else DMA_SEMS)[nsem[k] - 1]
+        return add(q, call, (out, x), [out], [x], (2.0 if q == "pool" else 0.1, 0, 0, 0), lat + (0.2 if q == "pool" else 0.3), sem, after)
 
-    def row(a, b):
-        return ("CR", (slice(0, 1), slice(a, b)))
+    def row(a, n):
+        return ("CR", (slice(0, 1), slice(a, a + n)))
 
-    def send(t, cs):
-        src = [C("LO", t * 128 + c * 64, t * 128 + c * 64 + 64) for c in cs]
-        s = add("pool", "send", (t, cs), [], src, 1.0, 1.0, "sent")
-        for c in cs:
-            add("rx", "rx", (), [C("LA", t * 128 + c * 64, t * 128 + c * 64 + 64)], [], 0.0, HOP + (2.0 if t == 0 else 0.0),
-                "ar%d%d" % (t, c), after=[s])
+    def send(t, hs):
+        s = add("pool", "send", (t, hs), [], [own_list(t, *unit(c)) for c in hs], (1.0, 0, 0, 0), 0.0, "sent")
+        return [add("rx", "rx", (arr_list(t, *unit(c)), own_list(t, *unit(c))), [arr_list(t, *unit(c))], [], (0.0, 0, 0, 0),
+                    ("hop", 2.0 if t == 0 else 0.0), "ar%d%d" % (t, c), after=[s]) for c in hs]
 
-    dma("sp", C("ND", 0, 128), C("nd", 0, 128), 2.2)
-    dma("act", C("Pb", 15, 2063), C("pa", 0, 2048), 3.0)
-    for r in range(4):
-        dma("sp", A("FR", S_, slice(r * 128, r * 128 + 128)), C("fc", 0, 384), 2.5)
-    dma("sp", C("DL", 0, 1), A("dl", S_), 2.5)
-    dma("sp", C("ER", 0, 384), C("er", 0, 384), 2.5)
-    add("pool", "iota", (), [C("IO", 0, 256)], [], 0.6)
+    def fr(t, h, a, n):
+        return C("FR", (t * 2 + h) * 512 + a, n)
+
+    def rr(t, h, a, n):
+        return C("RR", t * 256 + h * 128 + a, n)
+
+    def wr(t, h, a, n):
+        return C("WR", t * 256 + h * 128 + a, n)
+
+    def jw(t, h, a, n):
+        return C("JW", t * 256 + h * 128 + a, n)
+
+    part[0] = "0"
+    dma("sp", A("ND"), C("nd", 0, 128), 2.1)
+    dma("act", C("P0", 15, 2048), C("pa", 0, 2048), 2.9)
+    dma("sp", C("FC", 0, 384), C("fc", 0, 384), 2.2)
+    dma("sp", C("DL", 0, 1), A("dl", S_), 2.2)
+    dma("sp", C("ER", 0, 384), C("er", 0, 384), 2.2)
+    add("pool", "iota", (C("IO", 0, 2 * W), [[1, 2 * W]], 0, -1), [C("IO", 0, 2 * W)], [], (0.6, 0, 0, 0))
     io = C("IO", 0, 128)
+    for h in range(NG):
+        first = cp(own_list(0, h, 0, W), A("ND", S_, h))
+    rx0 = send(0, [0, 1]) if PAR["FUSE0"] else send(0, [0]) + send(0, [1])
+    dma("pool", C("Ew", 0, 2048), C("ea", 0, 2048), 5.0, after=rx0)
+    if PAR["EC"]:
+        dma("sp", C("Es", 15, 2048), C("Ew", 0, 2048), 3.5, after=rx0)
+    for p in ("P1", "P2"):
+        dma("sp", C(p, 15, 2048), C("pa", 0, 2048), 3.0, after=rx0)
     ts(C("Ib", 0, 128), io, 0.0, ALU.is_equal)
     ts(C("nIb", 0, 128), io, 0.0, ALU.is_equal, -1.0, ALU.mult)
     ts(C("Ibig", 0, 128), io, 0.0, ALU.is_equal, float(2 ** 26), ALU.mult)
-    ts(C("Ih", 0, 128), io, 0.0, ALU.is_equal, 0.5, ALU.mult)
-    if any("pe" in m for m in BIAS) or any(SUBPE):
-        ts(C("If", 0, 128), io, 0.0, ALU.is_equal)
+    ts(C("If", 0, 128), io, 0.0, ALU.is_equal)
+    if any("pe" in m or "pd" in m for m in PAR["BIAS"]) or any(PAR["SUBPE"]):
+        ts(C("Ih", 0, 128), io, 0.0, ALU.is_equal, 0.5, ALU.mult)
         ts(C("nIf", 0, 128), io, 0.0, ALU.is_equal, -1.0, ALU.mult)
-    ms(C("Z", 0, 144), 0.0)
-    ts(C("TF", 16, 24), C("IO", 0, 128, 16), 0.0, ALU.is_le, 8192.0, ALU.mult)
-    ts(C("TF", 24, 32), C("IO", 0, 128, 16), -15.0, ALU.is_ge)
-    tt(C("Z", 16, 144, 16), C("TF", 16, 24), C("TF", 24, 32), ALU.mult)
+    ts(C("TF", 16, 8), C("IO", 0, 8, 16), 0.0, ALU.is_le)
+    ts(C("TF", 24, 8), C("IO", 0, 8, 16), -15.0, ALU.is_ge)
+    tt(C("TF", 32, 8), C("TF", 16, 8), C("TF", 24, 8), ALU.mult)
+    for z, v in (("Zp", 8192.0), ("Zn", -4096.0)):
+        ms(C(z, 0, 144), 0.0)
+        ts(C(z, 16, 8, 16), C("TF", 32, 8), v, ALU.mult)
     ts(C("TI", 0, 16), C("IO", 0, 16), 15, ALU.bitwise_and)
     ts(C("TF", 0, 16), C("TI", 0, 16), 0.0, ALU.is_equal)
     for il in range(16):
-        ts(C("Dm", il * 128, il * 128 + 128), C("Ib", 0, 128), C("TF", il, il + 1), ALU.mult)
-    cp(row(0, 256), ("IO", (slice(0, 1), slice(0, 256))))
-    for k, v in enumerate((1.0, 32.0, 8.5, -float(2 ** 24))):
-        ms(row(256 + 128 * k, 384 + 128 * k), v)
-    ms(C("SC", 0, 256, 2), 0.0)
-    ms(C("SC", 1, 256, 2), 0.5)
-    first = cp(C("LO", 0, 128), C("ND", 0, 128))
-    send(0, list(range(NCH)))
-    add("pool", "dma_start", (C("Ew", 0, 2048), C("ea", 0, 2048)), [C("Ew", 0, 2048)], [], 2.0, 6.0, "cast", after=[first])
-    cp(C("PT", 0, 128), C("Pb", 15, 2063, 16))
-    cp(C("Pb", 31, 2064, 16), C("PT", 0, 128))
+        ts(C("Dm", il * 128, 128), C("Ib", 0, 128), C("TF", il, 1), ALU.mult)
+    cp(row(0, 2 * W), ("IO", (slice(0, 1), slice(0, 2 * W))))
+    for k, v in enumerate((1.0, 16.0 * NG, 8.5)):
+        ms(row(256 + 128 * k, 128), v)
+    ms(C("SC", 0, 64, 2), 0.0)
+    ms(C("SC", 1, 64, 2), 0.5)
+    for j, v in enumerate((0.0, 1.0, -0.5)):
+        ms(C("S3", j, 64, 3), v)
     for k, v in enumerate((1.0, -1.0, 2.0, -2.0)):
-        ts(C("MM", k, k + 1), C("DL", 0, 1), v, ALU.mult)
-    m1, mn1, m2, mn2 = [C("MM", k, k + 1) for k in range(4)]
-    if any("act" in m for m in BIAS):
-        cp(C("BT", 17, 18), C("IO", 0, 1))
-        ts(C("BT", 0, 16), C("IO", 0, 16), C("BT", 17, 18), ALU.subtract, -0.5, ALU.mult)
-        ts(C("BT", 0, 16), C("BT", 0, 16), 1.0, ALU.add, m1, ALU.mult)
-        ts(C("BT", 16, 17), C("DL", 0, 1), 16.0, ALU.mult)
-    ts(C("LF", 0, 128), C("ND", 0, 128), -7.5, ALU.add)
-    ts(C("LF", 128, 256), C("ND", 0, 128), -7.5, ALU.add)
-    ts(A("JW", 0, slice(0, 128)), C("LF", 0, 128), MAGIC, ALU.add, -MAGIC, ALU.add)
-    tt(A("RR", 0, slice(0, 128)), C("LF", 0, 128), A("JW", 0, slice(0, 128)), ALU.subtract)
-    Pw, Ew = C("Pb", 16, 2064), C("Ew", 0, 2048)
-    npg = [0]
+        ts(C("MM", k, 1), C("DL", 0, 1), v, ALU.mult)
+    m1, mn1, m2, mn2 = [C("MM", k, 1) for k in range(4)]
+    ms(C("SN", 0, 64, 2), 0.0)
+    ms(C("SN", 1, 64, 2), -0.5)
+    if any("pz" in m for m in PAR["BIAS"]):
+        ts(C("I2", 0, 128), io, 0.0, ALU.is_equal, 2.0, ALU.mult)
+        for k in range(32):
+            v = 2.0 ** (k % 16 + 1) * (1 if k < 16 else -1)
+            act(C("MK", k, 1), C("DL", 0, 1), AF.Identity, v)
+            for wt, days in (("WB", PAR["BIAS"][:1]), ("WF", PAR["BIAS"][1:])):
+                if any("pz" in m for m in days) and k not in (15, 16):
+                    act(C(wt, k * 128, 128), C("Ib", 0, 128), AF.Identity, v)
+    if any("act" in m for m in PAR["BIAS"]):
+        for k in range(17):
+            act(C("BT", k, 1), C("DL", 0, 1), AF.Identity, 1.0 - k / 2 if k < 16 else 16.0)
+    if PAR["EC"]:
+        ts(C("TI", 16, 1), C("IO", 0, 1), -1.0, ALU.mult)
+        ts(C("TI", 17, 1), C("TI", 16, 1), 15, ALU.bitwise_and)
+        cp(C("TF", 39, 1), C("TI", 17, 1))
+    cp(C("PT", 0, 128), C("P0", 15, 128, 16))
+    cp(C("P0", 31, 128, 16), C("PT", 0, 128))
+    for t in range(DAYS):
+        part[0] = "f%d" % t
+        for h in range(NG):
+            for r in range(2):
+                cp(fr(t, h, r * W, W), C("FC", t * 128 + h * W, W))
+            for n in (128, 256)[2 - NG:]:
+                cp(fr(t, h, n, n), fr(t, h, 0, n))
+        for d in range(t):
+            move(PAR["PUPD"], C("P%d" % t, 31 if d == 0 else 16, 128, 16), C("FC", d * 128, 128))
+    part[0] = "0"
+    for h in range(NG):
+        for r in range(2):
+            ts(C("LF", h * 128 + r * W, W), A("ND", S_, h), -7.5, ALU.add)
+        ts(jw(0, h, 0, W), C("LF", h * 128, W), MAGIC, ALU.add, -MAGIC, ALU.add)
+        tt(rr(0, h, 0, W), C("LF", h * 128, W), jw(0, h, 0, W), ALU.subtract)
 
-    def distances(t, half):
-        kb, lst = ("KO", "LO") if half == 0 else ("KA", "LA")
-        key = C(kb, 0, 128)
-        mm(key, row(512, 640), row(256, 384), True, False)
-        mm(key, row(384, 512), row(half * 128, half * 128 + 128), False, False)
+    def distances(t, h, arr):
+        part[0] = "d%d%d%d" % (t, h, arr)
+        kb = "K%d" % (h if NG == 2 else arr)
+        key, grp = C(kb, arr * W, W), (t, h, arr)
+        lst = arr_list if arr else own_list
+        mm(key, row(512, 128), row(256, W), True, False)
+        mm(key, row(384, 128), row(arr * W, W), False, False)
         low = []
-        for c in range(2):
-            kc, lo = C(kb, c * 64, c * 64 + 64), half * 128 + c * 64
-            i = mm(kc, C("Ib", 0, 128), A("RR", t, slice(lo, lo + 64)), False, False, (t, half))
-            low.append(mm(kc, row(640, 768), row(256, 320), False, False, (t, half), [i]))
-        if half == 1:
+        for c in range(W // 64):
+            a = arr * W + c * 64
+            if arr:
+                dv = A("D%d" % h, 7) if NG == 2 else A("D0", 3, c)
+                ts(dv, arr_list(t, h, c * 64), -7.5, ALU.add)
+                ts(jw(t, h, a, 64), dv, MAGIC, ALU.add, -MAGIC, ALU.add)
+                tt(rr(t, h, a, 64), dv, jw(t, h, a, 64), ALU.subtract)
+            low.append(mm(C(kb, a, 64), C("Ib", 0, 128), rr(t, h, a, 64), False, False, grp))
+            if NG == 1:
+                ts(wr(t, h, a, 64), rr(t, h, a, 64), 7.5, ALU.is_equal, -16.0, ALU.mult)
+                mm(C(kb, a, 64), C("Ib", 0, 128), wr(t, h, a, 64), False, False, grp, low[-1:])
+        if arr:
+            dv = A("D%d" % h, 7) if NG == 2 else A("D0", 3)
             for r in range(16):
-                if VOIDW:
-                    tt(C("EQ", r * 128, r * 128 + 128), A("DV", 2), C("LF", r * 8, r * 8 + 128), ALU.is_equal)
-                    mm(key, C("Ibig", 0, 128), C("EQ", r * 128, r * 128 + 128), False, False, (t, half))
-                for c in range(0 if VOIDW else 2):
-                    tt(C("EQ", r * 128 + c * 64, r * 128 + c * 64 + 64), A("DV", 2, c), C("LF", r * 8 + c * 64, r * 8 + c * 64 + 64),
-                       ALU.is_equal)
-                    mm(C(kb, c * 64, c * 64 + 64), C("Ibig", 0, 128), C("EQ", r * 128 + c * 64, r * 128 + c * 64 + 64), False, False,
-                       (t, half))
-        for q in range(4):
-            off = C(lst, t * 128 + q * 32, t * 128 + q * 32 + 32)
-            base = half * 2048 + q * 512
-            ab = C("AB", base, base + 512)
-            if half * 4 + q in ACTG[t]:
-                pg = C("PG", (npg[0] % 2) * 512, (npg[0] % 2) * 512 + 512)
-                npg[0] += 1
-                act(pg, IND(Pw, off), AF.Identity)
-                mm(C("SB", 0, 512), C("Ib", 0, 128), pg, True, False)
-                mm(C("SB", 0, 512), C("nIb", 0, 128), A("FR", t, S_), False, True)
-                act(ab, C("SB", 0, 512), AF.Abs)
-            else:
-                tt(ab, IND(Pw, off), A("FR", t, S_), ALU.subtract)
-                act(ab, ab, AF.Abs)
-            if q % 2 == 1:
-                b0 = base - 512
-                for il in range(16):
-                    mm(C(kb, (q - 1) * 32, (q + 1) * 32), C("Z", 16 - il, 144 - il), C("AB", b0 + il, b0 + 1024, 16), False, False,
-                       (t, half), [low[q // 2]])
+                eq = C("EQ", h * 1024 + r * W, W)
+                tt(eq, dv, C("LF", h * 128 + r * NB, W), ALU.is_equal)
+                mm(key, C("Ibig", 0, 128), eq, False, False, grp)
+        for c in range(W // 64):
+            pieces(t, h, arr, c, C(kb, arr * W + c * 64, 64), low[c:c + 1])
+        if not arr:
+            act(A("H", h * 2), key)
+        if PAR["EC"] and t == DAYS - 1:
+            part[0] = "c%d%d" % (h, arr)
+            for q in range(W // 32):
+                move(PAR["EC"][arr * W // 32 + q], C("EC", h * 2048 + arr * 16 * W + q * 512, 512), IND(C("Es", 16, 2048), lst(t, h, q * 32, 32)))
 
-    def sel(buf, dims, fix, rev=()):
+    def pieces(t, h, arr, c, key, low):
+        lst, grp = arr_list if arr else own_list, (t, h, arr)
+        base, how = ((h + c) * 2 + arr) * 1024, PAR["ARR" if arr else "OWN"][t][h + c]
+        for q in range(2):
+            src, ab = IND(C("P%d" % t, 16, 2048), lst(t, h, c * 64 + q * 32, 32)), C("AB", base + q * 512, 512)
+            if how[q] == "a":
+                pg = C("PG", (npg[0] % 2) * 512, 512)
+                npg[0] += 1
+                act(pg, src)
+                mm(C("SB", 0, 512), C("Ib", 0, 128), pg, True, False)
+                mm(C("SB", 0, 512), C("nIb", 0, 128), fr(t, h, 0, 512), False, True)
+                act(ab, C("SB", 0, 512), AF.Abs, 0.5)
+            else:
+                ax = C("AX", base + q * 512, 512)
+                tt(ax, src, fr(t, h, 0, 512), ALU.subtract)
+                if how[q] == "v":
+                    ts(ab, ax, 0.0, ALU.max)
+                else:
+                    act(ab, ax, AF.Abs, 0.5)
+        v = [q for q in range(2) if how[q] == "v"]
+        for il in range(16):
+            neg = low
+            if v:
+                neg = [mm(C(key[0], key[1][1].start + v[0] * 32, 32 * len(v)), C("Zn", 16 - il, 128),
+                          C("AX", base + v[0] * 512 + il, 32 * len(v), 16), False, False, grp, low)]
+            mm(key, C("Zp", 16 - il, 128), C("AB", base + il, 64, 16), False, False, grp, neg)
+
+    def sel(buf, dims, fix={}, rev=()):
         name, pre = buf
         return A(name, *(pre + tuple(fix[b] if b in fix else (R_ if b in rev else S_) for b in dims) + (S_,)))
 
-    def sort():
-        sb, ps = [("S0", ()), ("S1", ())], [("DV", (0,)), ("DV", (1,))]
+    def sort(h):
+        n = [0]
+
+        def two():
+            n[0] += 1
+            return [("H", (h * 2 + n[0] % 2,)), ("D%d" % h, (n[0] % 2,))]
+
+        def whole():
+            n[0] += 1
+            return ("Y%d" % (h * 2 + n[0] % 2), ())
+        mnx = ((0, ALU.min), (1, ALU.max))
+        x, dims = two(), [1, 4, 3, 2]
+        for side, op in mnx:
+            tt(sel(x[side], dims), A("H", h * 2), C("K%d" % h, 64, 64), op)
+        for lv in (1, 2, 3, 4):
+            y = whole()
+            yd = [lv] + [0 if b == lv else b for b in dims]
+            for side, op in mnx[:1 if lv == 4 else 2]:
+                tt(sel(y, yd, {lv: side}, [0] if side else []), sel(x[0], dims), sel(x[1], dims, {}, range(1, lv + 1)), op)
+            if lv == 4:
+                break
+            c = lv - 1
+            while c >= 0:
+                if c == 0:
+                    x, dims = two(), [b for b in yd if b != 0]
+                    for side, op in mnx:
+                        tt(sel(x[side], dims), sel(y, yd, {0: 0}), sel(y, yd, {0: 1}), op)
+                    break
+                x, dims = two(), [c] + [b for b in yd if b not in (c, c - 1)]
+                for side, op in mnx:
+                    for v in (0, 1):
+                        tt(sel(x[v], dims, {c: side}), sel(y, yd, {c: 0, c - 1: v}), sel(y, yd, {c: 1, c - 1: v}), op)
+                c -= 1
+                if c == 0:
+                    x2 = two()
+                    for side, op in mnx:
+                        tt(sel(x2[side], dims), sel(x[0], dims), sel(x[1], dims), op)
+                    x = x2
+                    break
+                y, yd = whole(), [c] + dims
+                for side, op in mnx:
+                    tt(sel(y, yd, {c: side}), sel(x[0], dims), sel(x[1], dims), op)
+                c -= 1
+        y, yd = (y[0], y[1] + (0,)), yd[1:]
+        for c in (3, 2, 1, 0):
+            z = whole()
+            z = (z[0], z[1] + (0,)) if c else ("KI", (h,))
+            zd = [b for b in yd if b != c]
+            zd.insert(3 - c, c)
+            for side, op in ((0, ALU.max), (1, ALU.min)):
+                tt(sel(z, zd, {c: side}), sel(y, yd, {c: 0}), sel(y, yd, {c: 1}), op)
+            y, yd = z, zd
+
+    def sort_wide():
+        sb, ps = [("H", (1,)), ("H", (2,))], [("D0", (0,)), ("D0", (1,))]
         seq = [(c, c == lv - 1) for lv in range(1, 5) for c in range(lv - 1, -1, -1)] + [(4, True)]
-        x0, x1, dims = ("KS", ()), None, [1, 4, 3, 2]
+        x0, x1, dims = ("H", (0,)), None, [1, 4, 3, 2]
         for s, (c, first) in enumerate(seq):
             last = c == 4
             c2 = 3 if last else seq[s + 1][0]
@@ -280,300 +422,353 @@ def build(cost):
             for side, op in ((0, ALU.min), (1, ALU.max))[:1 if last else 2]:
                 for v in (0, 1):
                     a = sel(x0, dims, {c2: 1 - v if c2 in rev else v}, rev)
-                    b = C("KA", v * 64, v * 64 + 64) if s == 0 else sel(x1, dims, {c2: v})
+                    b = C("K1", 128 + v * 64, 64) if s == 0 else sel(x1, dims, {c2: v})
                     tt(sel(ys[v], yd, {c: side}), a, b, op)
             x0, x1, dims = ys[0], ys[1], yd
-        full, zz = [3, 2, 1, 0], ("ZZ", ())
+        full, zz = [3, 2, 1, 0], ("Y0", (0,))
         for side, op in ((0, ALU.max), (1, ALU.min)):
-            tt(sel(zz, full, {3: side}), sel(x0, dims, {}), sel(x1, dims, {}), op)
-        ys = [("S1", (0,)), ("DV", (1, 0))]
+            tt(sel(zz, full, {3: side}), sel(x0, dims), sel(x1, dims), op)
+        ys = [("H", (2, 0)), ("D0", (1, 0))]
         for side, op in ((0, ALU.max), (1, ALU.min)):
             for v in (0, 1):
                 tt(sel(ys[v], [3, 2, 0], {2: side}), sel(zz, full, {2: 0, 1: v}), sel(zz, full, {2: 1, 1: v}), op)
         for side, op in ((0, ALU.max), (1, ALU.min)):
-            tt(sel(zz, full, {1: side}), sel(ys[0], [3, 2, 0], {}), sel(ys[1], [3, 2, 0], {}), op)
+            tt(sel(zz, full, {1: side}), sel(ys[0], [3, 2, 0]), sel(ys[1], [3, 2, 0]), op)
         for side, op in ((0, ALU.max), (1, ALU.min)):
-            tt(sel(("KI", ()), full, {0: side}), sel(zz, full, {0: 0}), sel(zz, full, {0: 1}), op)
+            tt(sel(("KI", (0,)), full, {0: side}), sel(zz, full, {0: 0}), sel(zz, full, {0: 1}), op)
 
-    def choose(t):
-        part[0] += 1
-        for c in range(NCH):
-            la = C("LA", t * 128 + c * 64, t * 128 + c * 64 + 64)
-            jw = A("JW", t, slice(128 + c * 64, 192 + c * 64))
-            ts(A("DV", 2, c), la, -7.5, ALU.add)
-            ts(jw, A("DV", 2, c), MAGIC, ALU.add, -MAGIC, ALU.add)
-            tt(A("RR", t, slice(128 + c * 64, 192 + c * 64)), A("DV", 2, c), jw, ALU.subtract)
-        distances(t, 0)
-        act(A("KS"), C("KO", 0, 128), AF.Identity)
-        distances(t, 1)
-        if t < DAYS - 1:
-            act(C("Pb", 31 if t == 0 else 15 + t, 2064, 16), A("FR", t, slice(0, 128)), AF.Identity)
-        sort()
-        ts(C("O32", 0, 128), A("KI"), 5, ALU.arith_shift_right, 255, ALU.bitwise_and)
-        cp(C("O16", 0, 128), C("O32", 0, 128))
-        ts(C("D32", 0, 128), A("KI"), 15, ALU.bitwise_and)
-        ts(A("RR", t + 1, slice(0, 128)), C("D32", 0, 128), -7.5, ALU.add)
-        c0 = 0
-        for n, who in LOOK[t]:
-            c1 = c0 + 8 * n
-            jg, src = C("JG", c0 * 16, c1 * 16), IND(A("JW", t, S_), C("O16", c0, c1))
-            if who == "act":
-                act(jg, src, AF.Identity)
+    def choose(t, h):
+        distances(t, h, 1)
+        part[0] = "s%d%d" % (t, h)
+        if NG == 2:
+            sort(h)
+        else:
+            sort_wide()
+        part[0] = "l%d%d" % (t, h)
+        ki, o32, o16 = A("KI", h), C("O32", h * 64, W), C("O16", h * 64, W)
+        if PAR["EC"] and t == DAYS - 1:
+            ts(o32, ki, NG - 1, ALU.arith_shift_right, 32 * W - 16, ALU.bitwise_and)
+            ts(o16, o32, C("TF", 39, 1), ALU.add)
+            return
+        ts(o32, ki, 3 + NG, ALU.arith_shift_right, 2 * W - 1, ALU.bitwise_and)
+        cp(o16, o32)
+        ts(C("D32", h * 64, W), ki, 15, ALU.bitwise_and)
+        ts(rr(t + 1, h, 0, W), C("D32", h * 64, W), -7.5, ALU.add)
+        look, c0, a = PAR["LOOK"][t][h], 0, 0
+        last, kb = t == DAYS - 1, "K%d" % (h if NG == 2 else 1)
+        for j in range(0, len(look), 2):
+            n = NB * int(look[j])
+            move(look[j + 1], C("JG", h * 1024 + c0 * 16, n * 16), IND(jw(t, h, 0, 2 * W), C("O16", h * 64 + c0, n)))
+            c0 += n
+            if last or c0 % 64 == 0:
+                lk = C(kb, 2 * W + a, c0 - a)
+                mm(lk, C("Ib", 0, 128), rr(t + 1, h, a, c0 - a), True, False)
+                for il in range(16):
+                    mm(lk, C("Dm", il * 128, 128), C("JG", h * 1024 + a * 16 + il, c0 - a, 16), False, il == 15)
+                ts(own_list(t + 1, h, a, c0 - a), lk, 7.5, ALU.add)
+                if not last:
+                    send(t + 1, [h + a // 64])
+                a = c0
+        if not last:
+            for r in range(2):
+                act(C("LF", h * 128 + r * W, W), C(kb, 2 * W, W))
+            ts(jw(t + 1, h, 0, W), C("LF", h * 128, W), MAGIC, ALU.add, -MAGIC, ALU.add)
+
+    def e_of(t, u, k, a=0, n=64):
+        return C("E", t * 2048 + unit(u)[0] * 1024 + unit(u)[1] + k * W + a, n)
+
+    def eb(t, u, k, n=64):
+        if t == 0 and PAR["BIAS"][0][0] in ("pz", "pd"):
+            return C("EB", unit(u)[0] * 1024 + unit(u)[1] + k * W, n)
+        return e_of(t, u, k, 0, n)
+
+    def errors(t, h):
+        part[0] = "e%d%d" % (t, h)
+        k0 = 0
+        ech = PAR["ECH"][t][h]
+        for n, who in [(int(ech[j]), ech[j + 1]) for j in range(0, len(ech), 2)]:
+            if PAR["EC"] and t == DAYS - 1:
+                src = IND(C("EC", h * 2048, 32 * W), C("O16", h * 64 + k0 * NB, n * NB))
             else:
-                cp(jg, src)
-            lk = C("LK", c0, c1)
-            mm(lk, C("Ib", 0, 128), A("RR", t + 1, slice(c0, c1)), True, False)
-            for il in range(16):
-                mm(lk, C("Dm", il * 128, il * 128 + 128), C("JG", c0 * 16 + il, c1 * 16, 16), False, il == 15)
-            ts(C("LO", (t + 1) * 128 + c0, (t + 1) * 128 + c1), lk, 7.5, ALU.add)
-            if t < DAYS - 1 and c1 % 64 == 0 and (c1 == 128 or not FUSE[t + 1]):
-                send(t + 1, [0, 1] if FUSE[t + 1] else [c1 // 64 - 1])
-            c0 = c1
-        if t < DAYS - 1:
-            act(C("LF", 0, 128), C("LK", 0, 128), AF.Identity)
-            act(C("LF", 128, 256), C("LK", 0, 128), AF.Identity)
-            ts(A("JW", t + 1, slice(0, 128)), C("LF", 0, 128), MAGIC, ALU.add, -MAGIC, ALU.add)
-
-    def bias(t):
-        part[0] += 1
-        e, k0, p0 = "E%d" % t, 0, part[0]
-        tri, direct = BIAS[t][0] == "tri", SUBDMA[t] == 4 and BIAS[t] == ("dve3", "dve3")
-        if tri:
-            for j, v in enumerate((0.0, 1.0, -0.5)):
-                ms(C("S3", j, 192, 3), v)
-        for n in ECH[t]:
-            act(C(e, k0 * 128, (k0 + n) * 128), IND(Ew, C("LO", (t + 1) * 128 + k0 * 8, (t + 1) * 128 + (k0 + n) * 8)), AF.Identity)
+                src = IND(C("Ew", 0, 2048), own_list(t + 1, h, k0 * NB, n * NB))
+            move(who, eb(t, h, k0, n * W), src)
             k0 += n
-        for k in range(16 if BIAS[t][0] == "whole" else 0):
-            ek, u, x, w0, w1 = C(e, k * 128, k * 128 + 128), C("U", 0, 128), C("X", 0, 128), (k % 2) * 256, (1 - k % 2) * 256
-            if k == 0:
-                ts(x, ek, 0.5, ALU.mult, m1, ALU.min)
-                ts(C("BA", w1 + 1, w1 + 256, 2), x, mn1, ALU.max)
-                continue
-            tt(u, ek, C("BA", w0 + 1, w0 + 256, 2), ALU.subtract)
-            ts(C("BA", w0, w0 + 256, 2), u, m2, ALU.min, mn2, ALU.max)
-            o, d1 = C("BA", w1, w1 + 256), C("BA", w0, w0 + 256)
-            add("dve", "tensor_tensor_scan", (o, C("SC", 0, 256), d1, 0.0, ALU.mult, ALU.add), [o], [C("SC", 0, 256), d1], vcost(256, 1))
-            if k == 15 and t < DAYS - 1:
-                cp(A("DV", 3), C("BA", w1 + 1, w1 + 256, 2))
-        for k in range(0 if BIAS[t][0] == "whole" else 16):
-            for h in range(2):
-                ek, u, x = C(e, k * 128 + h * 64, k * 128 + h * 64 + 64), C("U", h * 64, h * 64 + 64), C("X", h * 64, h * 64 + 64)
-                part[0] = p0 + h
-                mode = BIAS[t][h]
+        if eb(t, h, 0) != e_of(t, h, 0) and not PAR["SUBPE"][t]:
+            dma("pool", e_of(t, h, 0, 0, 16 * W), eb(t, h, 0, 16 * W), 3.3)
+
+    def bias(t, h):
+        mode, bk = PAR["BIAS"][t][h], "B%d" % h
+        subs = PAR["SUBS"][h] if mode == "tri" else 1
+        w = 64 // subs
+        for k in range(16):
+            for s in range(subs):
+                part[0] = "b%d%d%d" % (t, h, s)
+                ek, u, x = e_of(t, h, k, s * w, w), C("U", h * 64, 64), C("X", h * 64, 64)
                 if mode == "tri":
-                    w0, w1 = (2 * h + k % 2) * 200, (2 * h + 1 - k % 2) * 200
-                    x = C("V", w0 + 2, w0 + 193, 3)
+                    w0, w1 = [((h * 2 + s) * 2 + (k + j) % 2) * 200 for j in range(2)]
                     if k == 0:
-                        ms(C("V", w0 + 1, w0 + 193, 3), 0.0)
+                        ms(C("V", w0 + 1, w, 3), 0.0)
                     if k < 15:
-                        cp(C("V", w0 + 3, w0 + 194, 3), C(e, (k + 1) * 128 + h * 64, (k + 1) * 128 + h * 64 + 64))
+                        move(PAR["TRICP"], C("V", w0 + 3, w, 3), e_of(t, h, k + 1, s * w, w))
                     else:
-                        ms(C("V", w0 + 3, w0 + 194, 3), 0.0)
-                    ts(x, x if k > 0 else ek, m2, ALU.min, mn2, ALU.max)
-                    d1 = C("V", w0 + 1, w0 + 193)
-                    o = C("V", w1, w1 + 192) if k < 15 else C("BA", h * 192, h * 192 + 192)
-                    add("dve", "tensor_tensor_scan", (o, C("S3", 0, 192), d1, 0.0, ALU.mult, ALU.add), [o], [C("S3", 0, 192), d1],
-                        vcost(192, 1))
+                        ms(C("V", w0 + 3, w, 3), 0.0)
+                    y = C("V", w0 + 2, w, 3)
+                    ts(y, y if k > 0 else ek, m2, ALU.min, mn2, ALU.max)
+                    scan(C("V", w1, 3 * w) if k < 15 else C(bk, s * 3 * w, 3 * w), C("S3", 0, 3 * w), C("V", w0 + 1, 3 * w))
+                elif mode == "pz":
+                    z, wt = C(bk, 0, 64), "WB" if t == 0 else "WF"
+                    ts(x, u if k > 0 else eb(t, h, 0), C("MK", k, 1), ALU.min, C("MK", 16 + k, 1), ALU.max)
+                    if k < 15:
+                        mm(z, C(wt, k * 128, 128), eb(t, h, k + 1), True, k == 0)
+                    if k > 0:
+                        mm(z, C(wt, (16 + k) * 128, 128), eb(t, h, k), k == 15, False)
+                        mm(z, C("I2", 0, 128), u, False, True)
+                    tt(u, z, x, ALU.subtract)
+                    if k == 15:
+                        ts(z, u, -2.0 ** -16, ALU.mult)
+                elif mode == "pd":
+                    z, o = C(bk, 0, 64), C("V", h * 400 + 1, 64, 2)
+                    if t == DAYS - 1 and k % 2:
+                        z = A("D%d" % h, 0)
+                    pos, neg = (C("Ib", 0, 128), C("nIb", 0, 128)) if t == 0 else (C("If", 0, 128), C("nIf", 0, 128))
+                    ts(C("V", h * 400 + 200, 64, 2), o if k > 0 else eb(t, h, 0), m2, ALU.min, mn2, ALU.max)
+                    if k == 0:
+                        cp(C("V", h * 400 + 201, 64, 2), eb(t, h, 1))
+                    else:
+                        if k < 15:
+                            mm(z, pos, eb(t, h, k + 1), True, False)
+                        mm(z, neg, eb(t, h, k), k == 15, True)
+                        tt(C("V", h * 400 + 201, 64, 2), z, o, ALU.add)
+                    scan(C("V", h * 400, 128) if k < 15 else C(bk, 128, 128), C("SN", 0, 128), C("V", h * 400 + 200, 128))
                 elif mode == "act":
-                    b = C("BA", h * 128, h * 128 + 64)
+                    b = C(bk, 0, 64)
                     if k > 0:
                         tt(u, ek, b, ALU.add)
-                    act(x, u if k > 0 else ek, AF.Relu, 0.5, C("BT", k, k + 1))
+                    act(x, u if k > 0 else ek, AF.Relu, 0.5, C("BT", k, 1))
                     act(x, x, AF.Relu, -1.0, m2)
                     if k > 0:
                         tt(b, x, b, ALU.add)
                     else:
                         cp(b, x)
                     if k == 15:
-                        ts(A("DV", 3, h), b, -1.0, ALU.mult, C("BT", 16, 17), ALU.add)
+                        ts(C(bk, 64, 64), b, -1.0, ALU.mult, C("BT", 16, 1), ALU.add)
                 elif mode == "pe":
-                    b = C("BA" if h == 0 else "BB", 0, 64)
+                    b = C(bk, 0, 64)
                     if k > 0:
                         tt(u, ek, b, ALU.subtract)
                         mm(b, C("If", 0, 128), ek, True, False)
                         mm(b, C("nIf", 0, 128), u, False, False)
                     ts(x, u if k > 0 else ek, m2, ALU.min, mn2, ALU.max)
                     mm(b, C("Ih", 0, 128), x, k == 0, True)
-                    if k == 15:
-                        cp(A("DV", 3, h), b)
-                elif mode == "dve4" or k == 0:
-                    b = A("DV", 3, h) if mode == "dve4" else C("BA", 256 + h * 128 + 1, 256 + h * 128 + 128, 2)
-                    if k > 0:
-                        tt(u, ek, b, ALU.subtract)
-                    ts(x, u if k > 0 else ek, 0.5, ALU.mult, m1, ALU.min)
-                    if k > 0:
-                        ts(x, x, mn1, ALU.max)
-                        tt(b, x, b, ALU.add)
-                    else:
-                        ts(b, x, mn1, ALU.max)
+                elif k == 0:
+                    ts(x, ek, 0.5, ALU.mult, m1, ALU.min)
+                    ts(C(bk, 129, 64, 2), x, mn1, ALU.max)
                 else:
-                    w0, w1 = (k % 2) * 256 + h * 128, (1 - k % 2) * 256 + h * 128
-                    tt(u, ek, C("BA", w0 + 1, w0 + 128, 2), ALU.subtract)
-                    ts(C("BA", w0, w0 + 128, 2), u, m2, ALU.min, mn2, ALU.max)
-                    o, d1 = C("BA", w1, w1 + 128), C("BA", w0, w0 + 128)
-                    add("dve", "tensor_tensor_scan", (o, C("SC", 0, 128), d1, 0.0, ALU.mult, ALU.add), [o], [C("SC", 0, 128), d1],
-                        vcost(128, 1))
-                    if k == 15 and direct:
-                        lo, bh = t * 128 + h * 64, C("BA", w1 + 1, w1 + 128, 2)
-                        tt(C("Ew", t + h * 1024, (h + 1) * 1024, 16), C("ER", lo, lo + 64), bh, ALU.subtract)
-                        cp(C("YB", lo, lo + 64), bh)
-                    elif k == 15 and t < DAYS - 1:
-                        cp(A("DV", 3, h), C("BA", w1 + 1, w1 + 128, 2))
-        if t == DAYS - 1:
-            for h in range(2):
-                b, lo, sm = C("BA", h * 128 + 1, h * 128 + 128, 2), t * 128 + h * 64, C("SM" if h == 0 else "BB", 0, 64)
-                if tri:
-                    b = C("BA", h * 192 + 2, h * 192 + 192, 3)
-                    ts(C("YB", lo, lo + 64), b, -1.0, ALU.mult)
-                else:
-                    cp(C("YB", lo, lo + 64), b)
-                dma("act", C("yb", lo, lo + 64), C("YB", lo, lo + 64), 2.0)
-                k0 = 0
-                for n in TAILQ:
-                    for k in range(k0, k0 + n):
-                        r0 = k * 128 + h * 64
-                        tt(C("E0", h * 1024 + k * 64, h * 1024 + k * 64 + 64), C(e, r0, r0 + 64),
-                           b, ALU.add if tri else ALU.subtract)
-                    eq = C("E0", h * 1024 + k0 * 64, h * 1024 + (k0 + n) * 64)
-                    act(eq, eq, AF.Abs)
-                    act(eq, eq, AF.Exp, -1.0)
-                    for k in range(k0, k0 + n):
-                        mm(sm, C("Ih", 0, 128), C("E0", h * 1024 + k * 64, h * 1024 + k * 64 + 64), k == 0, k == 15)
-                    k0 += n
-                ts(C("YS", lo, lo + 64), sm, 2.0, ALU.mult)
-                dma("sp", C("ys", lo, lo + 64), C("YS", lo, lo + 64), 2.0)
-            return
-        b = A("DV", 3)
-        yb, ys = C("YB", t * 128, t * 128 + 128), C("YS", t * 128, t * 128 + 128)
-        if not direct:
-            tt(C("Ew", t, 2048, 16), C("ER", t * 128, t * 128 + 128), b, ALU.subtract)
-            cp(yb, b)
-        dma("sp", C("yb", t * 128, t * 128 + 128), yb, 2.0)
-        for q in range(4):
-            eq = C(e, q * 512, q * 512 + 512)
-            if q < SUBDMA[t]:
-                nb = C("NB", t * 512, t * 512 + 512)
-                for k in range(4 if q == 0 else 0):
-                    act(C("NB", t * 512 + k * 128, t * 512 + k * 128 + 128), yb, AF.Identity, -1.0)
-                add("pool", "dma_add", (eq, nb), [eq], [nb], 1.2, 4.5, "ad%d%d" % (t, q))
-                act(eq, eq, AF.Abs)
-            elif q < SUBPE[t]:
-                mm(C("BB", 0, 512), C("If", 0, 128), eq, True, False)
-                for k in range(4):
-                    mm(C("BB", k * 128, k * 128 + 128), C("nIf", 0, 128), yb, False, k == 3)
-                act(eq, C("BB", 0, 512), AF.Abs)
-            else:
-                for k in range(4 * q, 4 * q + 4):
-                    ek = C(e, k * 128, k * 128 + 128)
-                    tt(ek, ek, b, ALU.subtract)
-                act(eq, eq, AF.Abs)
-            act(eq, eq, AF.Exp, -1.0)
-            if not FOLD[t]:
-                for k in range(4 * q, 4 * q + 4):
-                    mm(C("SM", 0, 128), C("Ih", 0, 128), C(e, k * 128, k * 128 + 128), k == 0, k == 15)
-        if FOLD[t]:
-            s = add("pool", "fold", (t,), [], [C(e, 0, 2048)], 1.0, 1.0, "sent")
-            add("rx", "rx", (), [ys], [], 0.0, 9.0, "fo%d" % t, after=[s])
-        else:
-            act(ys, C("SM", 0, 128), AF.Identity, 2.0)
-        dma("sp", C("ys", t * 128, t * 128 + 128), ys, 2.0)
+                    w0, w1 = (k % 2) * 128, (1 - k % 2) * 128
+                    tt(u, ek, C(bk, w0 + 1, 64, 2), ALU.subtract)
+                    ts(C(bk, w0, 64, 2), u, m2, ALU.min, mn2, ALU.max)
+                    scan(C(bk, w1, 128), C("SC", 0, 128), C(bk, w0, 128))
+        return {"tri": (C(bk, 2, 64, 3), -1.0), "act": (C(bk, 64, 64), 1.0), "pz": (C(bk, 0, 64), 1.0), "pd": (C(bk, 129, 64, 2), -1.0), "pe": (C(bk, 0, 64), 1.0), "dve3": (C(bk, 1, 64, 2), 1.0)}[mode]
 
-    choose(0)
+    def finish(t, h, b, sign):
+        part[0] = "u%d%d" % (t, h)
+        lo = t * 128 + h * 64
+        yb, ys, less = C("YB", lo, 64), C("YS", lo, 64), ALU.subtract if sign > 0 else ALU.add
+        last = t == DAYS - 1
+        if not last:
+            if t == 0 or not PAR["EC"]:
+                tt(C("Ew", h * 1024 + t, 64, 16), C("ER", lo, 64), b, less)
+            if PAR["EC"]:
+                tt(C("Es", h * 1024 + (31 if t == 0 else 16), 64, 16), C("ER", lo, 64), b, less)
+        ts(yb, b, sign, ALU.mult)
+        dma("sp", C("yb", lo, 64), yb, 2.0)
+
+    def spread(t, h, b, sign):
+        part[0] = "x%d%d" % (t, h)
+        lo = t * 128 + h * 64
+        yb, ys, less = C("YB", lo, 64), C("YS", lo, 64), ALU.subtract if sign > 0 else ALU.add
+        last = t == DAYS - 1
+        w = 64 if last else W
+        if not last and NG == 1:
+            if h == 0:
+                return
+            h, lo = 0, t * 128
+            yb, ys = C("YB", lo, w), C("YS", lo, w)
+        sm = C("K%d" % h if last else "SM", 384, w)
+        if not last and not PAR["SUBPE"][t]:
+            nb, done = (t * 2 + h) * 1024, PAR["NACT"]
+            for r in range(done):
+                act(C("NB", nb + r * w, w), yb, AF.Identity, -1.0)
+            for r in range(done, PAR["NREP"], done):
+                dma("sp", C("NB", nb + r * w, done * w), C("NB", nb, done * w), 2.2)
+        k0 = 0
+        for n in PAR["TAILQ"] if last else [512 // w] * (w // 32):
+            if last:
+                x = C("X2", h * 1024 + k0 * 64, n * 64)
+                for k in range(k0, k0 + n):
+                    tt(C("X2", h * 1024 + k * 64, 64), e_of(t, h, k), b, less)
+            else:
+                x = e_of(t, h, k0, 0, n * w)
+                if not PAR["SUBPE"][t] and k0 % PAR["NREP"] == 0:
+                    dma("pool", e_of(t, h, k0, 0, PAR["NREP"] * w), C("NB", nb, PAR["NREP"] * w), 3.3, "dma_add")
+            if not last and PAR["SUBPE"][t]:
+                bf = eb(t, h, 0) != e_of(t, h, 0)
+                mm(C("SB", 0, n * w), C("Ib" if bf else "If", 0, 128), eb(t, h, k0, n * w), True, False)
+                for k in range(n):
+                    mm(C("SB", k * w, w), C("nIf", 0, 128), yb, False, k == n - 1)
+                act(x, C("SB", 0, n * w), AF.Abs)
+            else:
+                act(x, x, AF.Abs)
+            x0, m = x[1][1].start, n
+            if last and PAR["PAIR"]:
+                m = n // 2
+                ps = A("D%d" % h, slice((k0 % 8) // 4 * 2, (k0 % 8) // 4 * 2 + m))
+                act(ps, C(x[0], x0 + m * w, m * w), AF.Exp, -1.0)
+                act(C(x[0], x0, m * w), C(x[0], x0, m * w), AF.Exp, -1.0)
+                tt(C(x[0], x0, m * w), C(x[0], x0, m * w), ps, ALU.add)
+            else:
+                act(x, x, AF.Exp, -1.0)
+            if last or not PAR["DADD"][t]:
+                for k in range(m):
+                    mm(sm, C("If", 0, 128), C(x[0], x0 + k * w, w), k0 + k == 0, k0 + n == 16 and k == m - 1)
+            k0 += n
+        if not last and PAR["DADD"][t]:
+            m = 16
+            for _ in range(PAR["DADD"][t]):
+                m //= 2
+                dma("pool", e_of(t, h, 0, 0, m * w), e_of(t, h, m, 0, m * w), 3.3, "dma_add")
+            for k in range(m if m > 1 else 0):
+                mm(sm, C("If", 0, 128), e_of(t, h, k, 0, w), k == 0, k == m - 1)
+            if m == 1:
+                return dma("sp", C("ys", lo, w), e_of(t, h, 0, 0, w), 2.0)
+        move("v" if last else "a", ys, sm)
+        dma("sp", C("ys", lo, w), ys, 2.0)
+
+    for h in range(NG):
+        distances(0, h, 0)
+    for h in range(NG):
+        choose(0, h)
     for t in range(DAYS):
+        for h in range(NG):
+            if t + 1 < DAYS and not (PAR["EC"] and t + 1 == DAYS - 1):
+                distances(t + 1, h, 0)
+            errors(t, h)
+        bs = [bias(t, h) for h in range(2)]
+        for h in range(2):
+            finish(t, h, *bs[h])
         if t + 1 < DAYS:
-            choose(t + 1)
-        bias(t)
+            for h in range(NG):
+                if PAR["EC"] and t + 1 == DAYS - 1:
+                    distances(t + 1, h, 0)
+            for h in range(NG):
+                choose(t + 1, h)
+        for h in range(2):
+            spread(t, h, *bs[h])
+    above = []
+    for o in ops:
+        far = 0
+        for d in o["deps"]:
+            far |= above[d]
+        o["near"] = [d for d in o["deps"] if not far >> d & 1]
+        above.append(far | sum(1 << d for d in o["deps"] if not far >> d & 1))
     return ops
 
 
-def kind(o):
-    a = o["args"]
-    return "%d%s%s" % (o["part"], o["eng"], a[0][0] if a and isap(a[0]) else o["call"])
+def priced(ops, cost):
+    out = []
+    for o in ops:
+        f, c, gth, p = o["busy"]
+        b = f + (cost["FIX"] + c * cost["CY"] if c else 0.0) + gth * cost["GA"] * cost["CY"] + p * cost["PCY"]
+        out.append((b, b + (cost["HOP"] + o["lat"][1] if isap(o["lat"]) else o["lat"])))
+    return out
 
 
-def replay(ops, seq, cost):
+def replay(ops, seq, price, cost):
     free, fin, ws, wx = {}, [0.0] * len(ops), cost["WS"], cost["WX"]
     for i in seq:
         o = ops[i]
         e = o["eng"]
         t = free.get(e, 0.0) if e != "rx" else 0.0
-        for d in o["deps"]:
+        for d in o["near"]:
             a = ops[d]["eng"]
             t = max(t, fin[d] + (0.0 if (a == e == "pe" or e == "rx") else (ws if a == e else wx)))
-        free[e] = t + o["busy"]
-        fin[i] = t + o["lat"]
+        free[e] = t + price[i][0]
+        fin[i] = t + price[i][1]
     return max(fin)
 
 
 def search(ops, tries):
-    sets = [(w, build(dict(COST, **v)), dict(COST, **v)) for w, v in VARY]
-    kinds = sorted(set(kind(o) for o in ops if o["eng"] != "rx"))
-    rs = np.random.RandomState(SEED)
-
-    def length(sh):
-        schedule(ops, sh)
-        seq = sorted(range(len(ops)), key=lambda j: (ops[j]["t"], j))
-        r = [replay(o, seq, c) for _, o, c in sets]
-        return sum(x * s[0] for x, s in zip(r, sets)) / sum(s[0] for s in sets), r
-    cur = {}
-    best = length(cur)
-    for _ in range(tries):
-        sh = dict(cur)
-        for _ in range(int(rs.randint(1, 4))):
-            k = kinds[int(rs.randint(len(kinds)))]
-            sh[k] = sh.get(k, 0.0) + float(rs.randn()) * (0.5, 3.0, 10.0)[int(rs.randint(3))]
-        new = length(sh)
-        if new[0] <= best[0]:
-            cur, best = sh, new
-    return cur, best
-
-
-def schedule(ops, shift):
-    n, WS, WX = len(ops), COST["WS"], COST["WX"]
-    succ = [[] for _ in range(n)]
+    sets = [(w, priced(ops, dict(COST, **v)), dict(COST, **v)) for w, v in VARY]
+    n, price, rs = len(ops), priced(ops, COST), np.random.RandomState(SEED)
+    pred, succ = [[] for _ in ops], [[] for _ in ops]
     for i, o in enumerate(ops):
-        for d in o["deps"]:
-            succ[d].append(i)
-
-    def gap(d, i):
-        a, b = ops[d]["eng"], ops[i]["eng"]
-        return 0.0 if (a == b == "pe" or b == "rx") else (WS if a == b else WX)
-    pr = [0.0] * n
+        for d in o["near"]:
+            a, b = ops[d]["eng"], o["eng"]
+            gap = 0.0 if (a == b == "pe" or b == "rx") else COST["WS" if a == b else "WX"]
+            pred[i].append((d, gap))
+            succ[d].append((i, gap))
+    parts = sorted(set(o["part"] for o in ops))
+    of = np.array([parts.index(o["part"]) for o in ops])
+    prio = [0.0] * n
     for i in range(n - 1, -1, -1):
-        pr[i] = ops[i]["lat"] + max([gap(i, s) + pr[s] for s in succ[i]] + [0.0])
-    for i in range(n):
-        pr[i] += shift.get(kind(ops[i]), 0.0)
-    left = [len(o["deps"]) for o in ops]
-    rdy = [0.0] * n
-    ready = dict((e, []) for e in ("pe", "dve", "act", "pool", "sp", "rx"))
-    free = dict((e, 0.0) for e in ready)
-    order = dict((e, []) for e in ready)
-    for i in range(n):
-        if left[i] == 0:
-            ready[ops[i]["eng"]].append(i)
-    end = 0.0
+        prio[i] = min([prio[s] - gap for s, gap in succ[i]] + [0.0]) - price[i][1]
+    best, now, cur = None, None, np.array([PAR["SHIFT"].get(q[:2], 0.0) for q in parts])
+    for it in range(tries):
+        shift, base = cur.copy(), prio
+        if it % PAR["BACK"] == PAR["BACK"] - 1:
+            back = place(ops, price, succ, pred, [-times[i] - price[i][1] for i in range(n)], True)
+            shift, base = shift * 0, np.array([-back[i] - price[i][1] for i in range(n)])
+        elif it:
+            p = parts[rs.randint(len(parts))][:rs.randint(2, 5)]
+            shift[[j for j, q in enumerate(parts) if q.startswith(p)]] += rs.randn() * (0.4, 1.5, 5.0)[it % 3]
+        st = place(ops, price, pred, succ, list(base + shift[of]), False)
+        seq = sorted(range(n), key=lambda j: (st[j], j))
+        r = [replay(ops, seq, p, c) for _, p, c in sets]
+        score = sum(x * s[0] for x, s in zip(r, sets)) / sum(s[0] for s in sets) + PAR["EARLY"] * sum(st) / n
+        if now is None or score <= now - 0.3 * (1 - it / tries) * np.log(rs.rand()):
+            now, cur, prio, times = score, shift, base, st
+            if best is None or score < best[0]:
+                best = (score, r, st)
+    for i, o in enumerate(ops):
+        o["t"] = best[2][i]
+    return best[:2]
+
+
+def place(ops, price, pred, succ, prio, back):
+    n = len(ops)
+    left, st, rdy, begin, end = [len(p) for p in pred], [0.0] * n, [0.0] * n, {}, {}
+    rank = sorted(range(n), key=lambda i: prio[i])
+    pos = [0] * n
+    for j, i in enumerate(rank):
+        pos[i] = j
+    ready, j = [not x for x in left], 0
     for _ in range(n):
-        best = None
-        for e, r in ready.items():
-            if r:
-                t0 = max(free[e], min(rdy[i] for i in r))
-                if best is None or t0 < best[0]:
-                    best = (t0, e)
-        t0, e = best
-        i = max((j for j in ready[e] if rdy[j] <= t0 + 0.03), key=lambda j: pr[j])
-        ready[e].remove(i)
-        st = max(t0, rdy[i])
-        free[e] = st + ops[i]["busy"]
-        ops[i]["t"] = st
-        order[e].append(i)
-        end = max(end, st + ops[i]["lat"])
-        for s in succ[i]:
-            rdy[s] = max(rdy[s], st + ops[i]["lat"] + gap(i, s))
-            left[s] -= 1
-            if left[s] == 0:
-                ready[ops[s]["eng"]].append(s)
-    return order, end
+        while not ready[rank[j]]:
+            j += 1
+        i = rank[j]
+        ready[i] = False
+        (busy, lat), e, t = price[i], ops[i]["eng"], rdy[i]
+        if e != "rx":
+            off = lat - busy if back else 0.0
+            s, f = begin.setdefault(e, []), end.setdefault(e, [])
+            t += off
+            lo, hi = 0, len(f)
+            while lo < hi:
+                mid = (lo + hi) // 2
+                lo, hi = (mid + 1, hi) if f[mid] <= t else (lo, mid)
+            while lo < len(s) and s[lo] < t + busy - 1e-9:
+                t, lo = max(t, f[lo]), lo + 1
+            s.insert(lo, t)
+            f.insert(lo, t + busy)
+            t -= off
+        st[i] = t
+        for k, gap in succ[i]:
+            rdy[k] = max(rdy[k], t + lat + gap)
+            left[k] -= 1
+            if not left[k]:
+                ready[k] = True
+                j = min(j, pos[k])
+    return st
 
 
 def waits(ops, order):
@@ -618,14 +813,15 @@ PLAN = {}
 
 def plan():
     if not PLAN:
-        ops = build(COST)
-        shift, best = search(ops, TRIES)
-        order, end = schedule(ops, shift)
-        PLAN.update(best=best)
+        ops = build()
+        best = search(ops, TRIES)
+        order = dict((e, []) for e in ("pe", "dve", "act", "pool", "sp", "rx"))
+        for i in sorted(range(len(ops)), key=lambda j: (ops[j]["t"], j)):
+            order[ops[i]["eng"]].append(i)
         last = dict((ops[i]["grp"], i) for i in order["pe"] if ops[i]["grp"] is not None)
         for i in last.values():
             ops[i]["args"] = ops[i]["args"][:4] + (True,)
-        PLAN.update(ops=ops, order=order, end=end, total=waits(ops, order))
+        PLAN.update(best=best, ops=ops, order=order, total=waits(ops, order))
     return PLAN
 
 
@@ -633,53 +829,40 @@ def bits(engs):
     return sum(1 << e for e in engs)
 
 
-def helpers(T, topo, r):
+def relays_of(T, topo, r):
     src, dst = T.cores[r], T.cores[(r + 1) % len(T.cores)]
     free = sorted((c for c in topo.cores_of(src) if T.rank_of(c) is None), key=lambda c: (topo.die(c) != topo.die(src), c))
-    relays = [c for c in free if topo.may_write(c, dst)][:NCH]
-    return relays, [c for c in free if c not in relays][0]
+    return [c for c in free if topo.may_write(c, dst)][:2]
 
 
-def helper_program(g, core, T, topo):
+def relay_program(g, core, T, topo):
     for r, src in enumerate(T.cores):
-        if core not in topo.cores_of(src):
-            continue
-        relays, fold = helpers(T, topo, r)
+        relays = relays_of(T, topo, r)
         if core in relays:
-            c, dst = relays.index(core), T.cores[(r + 1) % len(T.cores)]
+            h, dst = relays.index(core), T.cores[(r + 1) % len(T.cores)]
             n_in = len(topo.engines(src, core))
             out = topo.engines(core, dst)
             rid, pid = topo.addr(dst, core)
             for t in range(DAYS):
-                ap, sem = T.LA[:, t * 128 + c * 64:t * 128 + c * 64 + 64], T.sem["ar%d%d" % (t, c)]
-                g.wait_ge(sem, n_in // NCH if FUSE[t] else n_in)
-                g.remote_dma(ap, ap, sem, T.sem.sent, pid, rid, bits(out))
+                name, key = arr_list(t, *unit(h))
+                sem = T.sem["ar%d%d" % (t, h)]
+                g.wait_ge(sem, n_in // 2 if t == 0 and PAR["FUSE0"] else n_in)
+                g.remote_dma(T[name][key], T[name][key], sem, T.sem.sent, pid, rid, bits(out))
             g.wait_ge(T.sem.sent, DAYS * len(out))
-        elif core == fold and any(FOLD):
-            n_in = len(topo.engines(src, core)) // 2
-            out = topo.engines(core, src)
-            rid, pid = topo.addr(src, core)
-            for t in range(DAYS):
-                if FOLD[t]:
-                    ap, sem = T.YS[:, t * 128:t * 128 + 128], T.sem["fo%d" % t]
-                    g.wait_ge(sem, n_in)
-                    g.remote_dma(ap, ap, sem, T.sem.sent, pid, rid, bits(out))
-            g.wait_ge(T.sem.sent, sum(FOLD) * len(out))
 
 
 def rank_program(g, core, T, topo):
     r = T.rank_of(core)
     if r is None:
-        return helper_program(g, core, T, topo)
+        return relay_program(g, core, T, topo)
     p = plan()
     ops = p["ops"]
-    relays, fold = helpers(T, topo, r)
-    before = helpers(T, topo, (r - 1) % len(T.cores))[0]
-    unit = dict((s, 16) for s in DMA_SEMS + ADD_SEMS + ["cast"])
+    relays = relays_of(T, topo, r)
+    before = relays_of(T, topo, (r - 1) % len(T.cores))
+    step = dict((s, 16) for s in DMA_SEMS + POOL_SEMS)
     for t in range(DAYS):
-        unit["fo%d" % t] = len(topo.engines(fold, core))
-        for c in range(NCH):
-            unit["ar%d%d" % (t, c)] = len(topo.engines(before[c], core))
+        for h in range(2):
+            step["ar%d%d" % (t, h)] = len(topo.engines(before[h], core))
     queue = {"pe": g.tensor, "dve": g.vector, "act": g.scalar, "pool": g, "sp": g.sync}
     sent, used = [0], []
 
@@ -690,10 +873,6 @@ def rank_program(g, core, T, topo):
             return ap(x[1]).indirect(ap(x[2]))
         return T[x[0]][x[1]]
 
-    def dst_of(c):
-        rid, pid = topo.addr(c, core)
-        return DstId(rid=rid, pnc=pid)
-
     for i in sorted(range(len(ops)), key=lambda j: (ops[j]["t"], j)):
         o = ops[i]
         if o["sem"] not in (None, "sent"):
@@ -702,29 +881,20 @@ def rank_program(g, core, T, topo):
             continue
         q, a, call = queue[o["eng"]], [ap(x) for x in o["args"]], o["call"]
         for s, v in o["wait"].items():
-            q.wait_ge(T.sem[s], v * unit.get(s, 1))
+            q.wait_ge(T.sem[s], v * step.get(s, 1))
         if call == "send":
             t, tr = a[0], []
-            for j, c in enumerate(a[1]):
-                en = topo.engines(core, relays[c])
+            for j, h in enumerate(a[1]):
+                en = topo.engines(core, relays[h])
                 en = en[j * len(en) // len(a[1]):(j + 1) * len(en) // len(a[1])]
-                lo = t * 128 + c * 64
-                tr.append(RemoteDMATransfer(dst_ids=[dst_of(relays[c])], dma_engine_mask=bits(en), remote_sem=T.sem["ar%d%d" % (t, c)],
-                                            src=T.LO[:, lo:lo + 64], dst=T.LA[:, lo:lo + 64]))
+                rid, pid = topo.addr(relays[h], core)
+                tr.append(RemoteDMATransfer(dst_ids=[DstId(rid=rid, pnc=pid)], dma_engine_mask=bits(en),
+                                            remote_sem=T.sem["ar%d%d" % (t, h)], src=ap(own_list(t, *unit(h))), dst=ap(arr_list(t, *unit(h)))))
                 sent[0] += len(en)
             g.remote_dma_fused(tr, local_sem=T.sem.sent)
             continue
-        if call == "fold":
-            t = a[0]
-            en = topo.engines(core, fold)
-            en = en[len(en) // 2:]
-            g.remote_dma_fused([RemoteDMATransfer(dst_ids=[dst_of(fold)], dma_engine_mask=bits(en), remote_sem=T.sem["fo%d" % t],
-                                                  srcs=[T["E%d" % t][:, k * 128:k * 128 + 128] for k in range(16)],
-                                                  dsts=[T.YS[:, t * 128:t * 128 + 128]], alu_op=1)], local_sem=T.sem.sent)
-            sent[0] += len(en)
-            continue
         if call == "iota":
-            ins = g.iota(T.IO[:], [[1, 256]], 0, -1)
+            ins = g.iota(*a)
         elif call == "dma_start":
             ins = q.dma_start(a[0], a[1])
         elif call == "dma_add":
@@ -744,9 +914,9 @@ def rank_program(g, core, T, topo):
         else:
             ins = q.memset(*a)
         if o["tick"]:
-            ins.then_inc(T.sem[o["tick"][0]], unit.get(o["tick"][0], 1))
+            ins.then_inc(T.sem[o["tick"][0]], step.get(o["tick"][0], 1))
     g.wait_ge(T.sem.sent, sent[0])
     for s, v in p["total"].items():
         g.wait_ge(T.sem[s], v)
     for s in used:
-        g.wait_ge(T.sem[s], unit[s])
+        g.wait_ge(T.sem[s], step[s])

@@ -4,17 +4,17 @@ from concourse.mybir import AluOpType as ALU, ActivationFunctionType as AF
 
 DAYS = 3
 PAR = dict(
-    OWN=(("mm", "mm"), ("mm", "mm"), ("mm", "mm")),
-    ARR=(("ma", "ma"), ("aa", "aa"), ("aa", "aa")),
-    LOOK=(("8a8v", "8a8a"), ("8a8a", "8a8a"), ("8a8a", "8a8v")),
+    OWN=(("am", "mm"), ("am", "mm"), ("am", "mm")),
+    ARR=(("ma", "ma"), ("aa", "ma"), ("aa", "ma")),
+    LOOK=(("8a8v", "8a8v"), ("8a8v", "8a8v"), ("8a8a", "8a8v")),
     BIAS=(("pz", "pz"), ("dve3", "dve3"), ("tri", "tri")),
     TRICP="dve", SUBS=(1, 1),
     ECH=(("8a8a", "8a8a"), ("4a4a8a", "4a4a8a"), ("4a4a8a", "4a4a8a")),
-    BACK=5, SHIFT={}, SUBPE=(0, 0), PAIR=True, DADD=(0, 0), EARLY=0.5, NG=2, PUPD="a", NACT=8, EC=False, NREP=8, TAILQ=(4, 4, 4, 2, 2), FUSE0=True,
+    TWO=False, JOINT=(0, 0, 1), ACTK=16, BACK=5, SHIFT={}, SUBPE=(0, 0), PAIR=True, DADD=(0, 0), EARLY=0.5, NG=2, PUPD="a", NACT=8, EC=False, NREP=8, TAILQ=(4, 4, 4, 2, 2), FUSE0=True,
 )
-COST = dict(CY=0.001044, GA=1.55, PCY=0.000684, WS=0.21, WX=0.21, HOP=6.2, FIX=0.012)
-VARY = ((1, {}),)
-TRIES, SEED = 4000, 6
+COST = dict(CY=0.00104, GA=1.55, PCY=0.00066, WS=0.235, WX=0.245, HOP=4.5, FIX=0.01)
+VARY = ((1, {}), (1, dict(CY=0.0012, PCY=0.0008, GA=1.4, HOP=5.0, WS=0.22, WX=0.23)), (1, dict(CY=0.00083, PCY=0.00043, HOP=3.5)))
+TRIES, SEED = 2200, 7
 
 F32, BF = "float32", "bfloat16"
 SCRATCH = {
@@ -37,6 +37,7 @@ SCRATCH = {
     "E": ("sbuf", [128, 6144], F32), "EC": ("sbuf", [128, 4096], F32), "X2": ("sbuf", [128, 2048], F32),
     "U": ("sbuf", [128, 128], F32), "X": ("sbuf", [128, 128], F32), "V": ("sbuf", [128, 1600], F32), "NB": ("sbuf", [128, 4096], F32),
     "EB": ("sbuf", [128, 2048], BF), "WB": ("sbuf", [128, 4096], BF), "WF": ("sbuf", [128, 4096], F32), "I2": ("sbuf", [128, 128], F32),
+    "I16": ("sbuf", [128, 128], BF), "PL": ("sbuf", [128, 128], F32), "DT": ("sbuf", [128, 256], F32), "TT": ("sbuf", [128, 128], F32),
     "MK": ("sbuf", [128, 32], F32), "BT": ("sbuf", [128, 20], F32), "SN": ("sbuf", [128, 128], F32),
     "YB": ("sbuf", [128, 384], F32), "YS": ("sbuf", [128, 384], F32),
 }
@@ -86,8 +87,8 @@ def isap(x):
 def shapes():
     ng = PAR["NG"]
     nb = 8 // ng
-    SCRATCH.update({"ND": ("sbuf", [128, 16, ng, nb], "int32"), "H": ("sbuf", [128, 4, 2, 2, 2, 2, nb], F32),
-                    "KI": ("sbuf", [128, ng, 2, 2, 2, 2, nb], "int32")})
+    SCRATCH.update({"ND": ("sbuf", [128, 16, ng, nb], "int32"), "H": ("sbuf", [128, 8, 2, 2, 2, 2, nb], F32),
+                    "KI": ("sbuf", [128, 2 * ng, 2, 2, 2, 2, nb], "int32")})
     for j in range(4):
         SCRATCH["Y%d" % j] = ("sbuf", [128, 2, 2, 2, 2, 2, nb], F32)
     for j in range(2):
@@ -189,7 +190,7 @@ def build():
         k = "pool" if q == "pool" else "hw"
         nsem[k] += 1
         sem = (POOL_SEMS if q == "pool" else DMA_SEMS)[nsem[k] - 1]
-        return add(q, call, (out, x), [out], [x], (2.0 if q == "pool" else 0.1, 0, 0, 0), lat + (0.2 if q == "pool" else 0.3), sem, after)
+        return add(q, call, (out, x), [out], [x], (1.4 if q == "pool" else 0.1, 0, 0, 0), lat + (0.2 if q == "pool" else -0.1), sem, after)
 
     def row(a, n):
         return ("CR", (slice(0, 1), slice(a, a + n)))
@@ -229,7 +230,7 @@ def build():
         dma("sp", C(p, 15, 2048), C("pa", 0, 2048), 3.0, after=rx0)
     ts(C("Ib", 0, 128), io, 0.0, ALU.is_equal)
     ts(C("nIb", 0, 128), io, 0.0, ALU.is_equal, -1.0, ALU.mult)
-    ts(C("Ibig", 0, 128), io, 0.0, ALU.is_equal, float(2 ** 26), ALU.mult)
+    ts(C("Ibig", 0, 128), io, 0.0, ALU.is_equal, float(2 ** (30 if PAR["TWO"] else 26)), ALU.mult)
     ts(C("If", 0, 128), io, 0.0, ALU.is_equal)
     if any("pe" in m or "pd" in m for m in PAR["BIAS"]) or any(PAR["SUBPE"]):
         ts(C("Ih", 0, 128), io, 0.0, ALU.is_equal, 0.5, ALU.mult)
@@ -237,15 +238,20 @@ def build():
     ts(C("TF", 16, 8), C("IO", 0, 8, 16), 0.0, ALU.is_le)
     ts(C("TF", 24, 8), C("IO", 0, 8, 16), -15.0, ALU.is_ge)
     tt(C("TF", 32, 8), C("TF", 16, 8), C("TF", 24, 8), ALU.mult)
-    for z, v in (("Zp", 8192.0), ("Zn", -4096.0)):
+    for z, v in (("Zp", 131072.0), ("Zn", -65536.0)) if PAR["TWO"] else (("Zp", 8192.0), ("Zn", -4096.0)):
         ms(C(z, 0, 144), 0.0)
         ts(C(z, 16, 8, 16), C("TF", 32, 8), v, ALU.mult)
     ts(C("TI", 0, 16), C("IO", 0, 16), 15, ALU.bitwise_and)
     ts(C("TF", 0, 16), C("TI", 0, 16), 0.0, ALU.is_equal)
-    for il in range(16):
+    for il in range(0 if PAR["TWO"] else 16):
         ts(C("Dm", il * 128, 128), C("Ib", 0, 128), C("TF", il, 1), ALU.mult)
-    cp(row(0, 2 * W), ("IO", (slice(0, 1), slice(0, 2 * W))))
-    for k, v in enumerate((1.0, 16.0 * NG, 8.5)):
+    if PAR["TWO"]:
+        ts(("IO", (slice(0, 1), slice(128, 256))), ("IO", (slice(0, 1), slice(0, 128))), 2, ALU.arith_shift_right)
+        cp(row(0, 128), ("IO", (slice(0, 1), slice(128, 256))))
+        ts(C("I16", 0, 128), io, 0.0, ALU.is_equal, 1 / 16, ALU.mult)
+    else:
+        cp(row(0, 2 * W), ("IO", (slice(0, 1), slice(0, 2 * W))))
+    for k, v in enumerate((1.0, 2048.0 if PAR["TWO"] else 16.0 * NG, 8.5)):
         ms(row(256 + 128 * k, 128), v)
     ms(C("SC", 0, 64, 2), 0.0)
     ms(C("SC", 1, 64, 2), 0.5)
@@ -265,8 +271,8 @@ def build():
                 if any("pz" in m for m in days) and k not in (15, 16):
                     act(C(wt, k * 128, 128), C("Ib", 0, 128), AF.Identity, v)
     if any("act" in m for m in PAR["BIAS"]):
-        for k in range(17):
-            act(C("BT", k, 1), C("DL", 0, 1), AF.Identity, 1.0 - k / 2 if k < 16 else 16.0)
+        for k in range(18):
+            act(C("BT", k, 1), C("DL", 0, 1), AF.Identity, 1.0 - k / 2 if k < 16 else (16.0, float(PAR["ACTK"]))[k - 16])
     if PAR["EC"]:
         ts(C("TI", 16, 1), C("IO", 0, 1), -1.0, ALU.mult)
         ts(C("TI", 17, 1), C("TI", 16, 1), 15, ALU.bitwise_and)
@@ -283,7 +289,13 @@ def build():
         for d in range(t):
             move(PAR["PUPD"], C("P%d" % t, 31 if d == 0 else 16, 128, 16), C("FC", d * 128, 128))
     part[0] = "0"
-    for h in range(NG):
+    for h in range(NG if PAR["TWO"] else 0):
+        for r in range(2):
+            ts(C("LF", h * 128 + r * W, W), A("ND", S_, h), 16.0, ALU.mult, -120.0, ALU.add)
+        ts(jw(0, h, 0, W), C("LF", h * 128, W), 16 * MAGIC, ALU.add, -16 * MAGIC, ALU.add)
+        ts(C("TT", h * 64, 64), jw(0, h, 0, W), -17 / 16, ALU.mult, 136.0, ALU.add)
+        tt(C("DT", h * 128, 64), C("LF", h * 128, W), C("TT", h * 64, 64), ALU.add)
+    for h in range(0 if PAR["TWO"] else NG):
         for r in range(2):
             ts(C("LF", h * 128 + r * W, W), A("ND", S_, h), -7.5, ALU.add)
         ts(jw(0, h, 0, W), C("LF", h * 128, W), MAGIC, ALU.add, -MAGIC, ALU.add)
@@ -294,10 +306,23 @@ def build():
         kb = "K%d" % (h if NG == 2 else arr)
         key, grp = C(kb, arr * W, W), (t, h, arr)
         lst = arr_list if arr else own_list
-        mm(key, row(512, 128), row(256, W), True, False)
-        mm(key, row(384, 128), row(arr * W, W), False, False)
         low = []
-        for c in range(W // 64):
+        if PAR["TWO"]:
+            mm(key, row(384, 128), row(arr * W, W), True, False)
+            dv, dt = A("D%d" % h, 7), C("DT", h * 128 + arr * 64, 64)
+            if arr:
+                ts(dv, arr_list(t, h), 16.0, ALU.mult, -120.0, ALU.add)
+                ts(jw(t, h, 64, 64), dv, 16 * MAGIC, ALU.add, -16 * MAGIC, ALU.add)
+                if PAR["TWO"] == "a":
+                    act(C("TT", h * 64, 64), jw(t, h, 64, 64), AF.Identity, -17 / 16, 136.0)
+                else:
+                    ts(C("TT", h * 64, 64), jw(t, h, 64, 64), -17 / 16, ALU.mult, 136.0, ALU.add)
+                tt(dt, dv, C("TT", h * 64, 64), ALU.add)
+            low.append(mm(key, C("I16", 0, 128), jw(t, h, arr * 64, 64), False, False, grp))
+        else:
+            mm(key, row(512, 128), row(256, W), True, False)
+            mm(key, row(384, 128), row(arr * W, W), False, False)
+        for c in range(0 if PAR["TWO"] else W // 64):
             a = arr * W + c * 64
             if arr:
                 dv = A("D%d" % h, 7) if NG == 2 else A("D0", 3, c)
@@ -316,7 +341,11 @@ def build():
                 mm(key, C("Ibig", 0, 128), eq, False, False, grp)
         for c in range(W // 64):
             pieces(t, h, arr, c, C(kb, arr * W + c * 64, 64), low[c:c + 1])
-        if not arr:
+        if PAR["TWO"]:
+            tt(C(kb, 128, 64) if arr else A("H", h * 4 + 2), key, dt, ALU.add)
+            if not arr:
+                act(A("H", h * 4), key)
+        elif not arr:
             act(A("H", h * 2), key)
         if PAR["EC"] and t == DAYS - 1:
             part[0] = "c%d%d" % (h, arr)
@@ -437,12 +466,127 @@ def build():
         for side, op in ((0, ALU.max), (1, ALU.min)):
             tt(sel(("KI", (0,)), full, {0: side}), sel(zz, full, {0: 0}), sel(zz, full, {0: 1}), op)
 
-    def choose(t, h):
+    def sort_both():
+        n = [0]
+
+        def two(*more):
+            n[0] += 1
+            j = n[0] % 2
+            return [("H", (slice(j, 4, 2),) + more), ("D0", (slice(2 * j, 2 * j + 2),) + more)]
+        mnx, mxn = ((0, ALU.min), (1, ALU.max)), ((0, ALU.max), (1, ALU.min))
+        x, dims = two(), [1, 4, 3, 2]
+        for h in range(2):
+            for side, op in mnx:
+                tt(A(*(("H", h * 2 + 1), ("D0", 2 + h))[side]), A("H", h * 2), C("K%d" % h, 64, 64), op)
+        for lv in (1, 2, 3, 4):
+            y, c2 = two(*((0,) if lv == 4 else ())), lv - 1
+            yd = ([] if lv == 4 else [lv]) + [0 if b == lv else b for b in dims if (b != c2 if c2 else b != lv)]
+            for side, op in mnx[:1 if lv == 4 else 2]:
+                for v in (0, 1):
+                    if c2:
+                        fx, fp, rv = {c2: v}, {c2: 1 - v}, [0] if side else []
+                    else:
+                        fx, fp, rv = {lv: v ^ side}, {lv: 1 - (v ^ side)}, []
+                    tt(sel(y[v], yd, {lv: side}, rv), sel(x[0], dims, fx), sel(x[1], dims, fp, range(1, lv + 1)), op)
+            x, dims = y, yd
+            for c in range(c2, -1, -1) if lv < 4 else ():
+                y = two()
+                yd = [c] + [b for b in dims if b != c - 1] if c else dims
+                for side, op in mnx:
+                    if c == 0:
+                        tt(sel(y[side], yd), sel(x[0], dims), sel(x[1], dims), op)
+                    for v in (0, 1) if c else ():
+                        tt(sel(y[v], yd, {c: side}), sel(x[0], dims, {c - 1: v}), sel(x[1], dims, {c - 1: v}), op)
+                x, dims = y, yd
+        z, zd = ("Y0", (S_,)), [3] + dims
+        for side, op in mxn:
+            tt(sel(z, zd, {3: side}), sel(x[0], dims), sel(x[1], dims), op)
+        y = two(0)
+        for side, op in mxn:
+            for v in (0, 1):
+                tt(sel(y[v], [3, 2, 0], {2: side}), sel(z, zd, {2: 0, 1: v}), sel(z, zd, {2: 1, 1: v}), op)
+        for side, op in mxn:
+            tt(sel(z, [3, 2, 1, 0], {1: side}), sel(y[0], [3, 2, 0]), sel(y[1], [3, 2, 0]), op)
+        for h in range(2):
+            for side, op in mxn:
+                tt(sel(("KI", (h,)), [3, 2, 1, 0], {0: side}), sel(("Y0", (h,)), [3, 2, 1, 0], {0: 0}), sel(("Y0", (h,)), [3, 2, 1, 0], {0: 1}), op)
+
+    def sort_two(h):
+        n = [0]
+
+        def two(*more):
+            n[0] += 1
+            j = n[0] % 2
+            return [("H", (slice(4 * h + j, 4 * h + 4, 2),) + more), ("D%d" % h, (slice(2 * j, 2 * j + 2),) + more)]
+        mnx, mxn = ((0, ALU.min), (1, ALU.max)), ((0, ALU.max), (1, ALU.min))
+        x, dims = two(), [1, 4, 3, 2]
+        for side, op in mnx:
+            tt(sel(x[side], dims), A("H", slice(4 * h, 4 * h + 4, 2)), C("K%d" % h, 64, 128), op)
+        for lv in (1, 2, 3, 4):
+            y, c2 = two(*((0,) if lv == 4 else ())), lv - 1
+            yd = ([] if lv == 4 else [lv]) + [0 if b == lv else b for b in dims if (b != c2 if c2 else b != lv)]
+            for side, op in mnx[:1 if lv == 4 else 2]:
+                for v in (0, 1):
+                    if c2:
+                        fx, fp, rv = {c2: v}, {c2: 1 - v}, [0] if side else []
+                    else:
+                        fx, fp, rv = {lv: v ^ side}, {lv: 1 - (v ^ side)}, []
+                    tt(sel(y[v], yd, {lv: side}, rv), sel(x[0], dims, fx), sel(x[1], dims, fp, range(1, lv + 1)), op)
+            x, dims = y, yd
+            for c in range(c2, -1, -1) if lv < 4 else ():
+                y = two()
+                yd = [c] + [b for b in dims if b != c - 1] if c else dims
+                for side, op in mnx:
+                    if c == 0:
+                        tt(sel(y[side], yd), sel(x[0], dims), sel(x[1], dims), op)
+                    for v in (0, 1) if c else ():
+                        tt(sel(y[v], yd, {c: side}), sel(x[0], dims, {c - 1: v}), sel(x[1], dims, {c - 1: v}), op)
+                x, dims = y, yd
+        z, zd, full = ("Y%d" % h, (S_,)), [3] + dims, [3, 2, 1, 0]
+        for side, op in mxn:
+            tt(sel(z, zd, {3: side}), sel(x[0], dims), sel(x[1], dims), op)
+        y = two(0)
+        for side, op in mxn:
+            for v in (0, 1):
+                tt(sel(y[v], [3, 2, 0], {2: side}), sel(z, zd, {2: 0, 1: v}), sel(z, zd, {2: 1, 1: v}), op)
+        for side, op in mxn:
+            tt(sel(z, full, {1: side}), sel(y[0], [3, 2, 0]), sel(y[1], [3, 2, 0]), op)
+        for side, op in mxn:
+            tt(sel(("KI", (slice(2 * h, 2 * h + 2),)), full, {0: side}), sel(z, full, {0: 0}), sel(z, full, {0: 1}), op)
+
+    def choose_two(t, h):
         distances(t, h, 1)
         part[0] = "s%d%d" % (t, h)
-        if NG == 2:
+        sort_two(h)
+        part[0] = "l%d%d" % (t, h)
+        oa, ob, pl = C("O32", h * 64, 64), C("D32", h * 64, 64), C("PL", h * 64, 64)
+        ts(oa, A("KI", 2 * h), 2032, ALU.bitwise_and)
+        ts(ob, A("KI", 2 * h + 1), 4, ALU.arith_shift_right, 15, ALU.bitwise_and)
+        tt(pl, oa, ob, ALU.add)
+        cp(own_list(t + 1, h), pl)
+        if t < DAYS - 1:
+            send(t + 1, [h])
+            for r in range(2):
+                act(C("LF", h * 128 + r * 64, 64), pl, AF.Identity, 16.0, -120.0)
+            ts(jw(t + 1, h, 0, 64), oa, 16.0, ALU.mult)
+            ts(A("D%d" % h, 6), ob, 16.0, ALU.mult, 16.0, ALU.add)
+            tt(C("DT", h * 128, 64), A("D%d" % h, 6), oa, ALU.subtract)
+
+    def choose(t, h):
+        if PAR["TWO"]:
+            return choose_two(t, h)
+        if not (PAR["JOINT"][t] and h):
+            distances(t, h, 1)
+        if PAR["JOINT"][t]:
+            if not h:
+                distances(t, 1, 1)
+                part[0] = "s%d0" % t
+                sort_both()
+        elif NG == 2:
+            part[0] = "s%d%d" % (t, h)
             sort(h)
         else:
+            part[0] = "s%d%d" % (t, h)
             sort_wide()
         part[0] = "l%d%d" % (t, h)
         ki, o32, o16 = A("KI", h), C("O32", h * 64, W), C("O16", h * 64, W)
@@ -517,6 +661,8 @@ def build():
                     scan(C("V", w1, 3 * w) if k < 15 else C(bk, s * 3 * w, 3 * w), C("S3", 0, 3 * w), C("V", w0 + 1, 3 * w))
                 elif mode == "pz":
                     z, wt = C(bk, 0, 64), "WB" if t == 0 else "WF"
+                    if t == DAYS - 1 and k % 2 == 0:
+                        z = A("D%d" % (1 - h if PAR["JOINT"][t] else h), 0) if h == 0 or not PAR["JOINT"][t] else A("D1", 0)
                     ts(x, u if k > 0 else eb(t, h, 0), C("MK", k, 1), ALU.min, C("MK", 16 + k, 1), ALU.max)
                     if k < 15:
                         mm(z, C(wt, k * 128, 128), eb(t, h, k + 1), True, k == 0)
@@ -540,8 +686,10 @@ def build():
                         mm(z, neg, eb(t, h, k), k == 15, True)
                         tt(C("V", h * 400 + 201, 64, 2), z, o, ALU.add)
                     scan(C("V", h * 400, 128) if k < 15 else C(bk, 128, 128), C("SN", 0, 128), C("V", h * 400 + 200, 128))
-                elif mode == "act":
-                    b = C(bk, 0, 64)
+                elif mode == "act" and k >= PAR["ACTK"]:
+                    b = C(bk, 256, 64)
+                    if k == PAR["ACTK"] and k:
+                        ts(b, C(bk, (k % 2) * 128 + 1, 64, 2), -1.0, ALU.mult, C("BT", 17, 1), ALU.add)
                     if k > 0:
                         tt(u, ek, b, ALU.add)
                     act(x, u if k > 0 else ek, AF.Relu, 0.5, C("BT", k, 1))
@@ -551,7 +699,7 @@ def build():
                     else:
                         cp(b, x)
                     if k == 15:
-                        ts(C(bk, 64, 64), b, -1.0, ALU.mult, C("BT", 16, 1), ALU.add)
+                        ts(C(bk, 320, 64), b, -1.0, ALU.mult, C("BT", 16, 1), ALU.add)
                 elif mode == "pe":
                     b = C(bk, 0, 64)
                     if k > 0:
@@ -568,7 +716,7 @@ def build():
                     tt(u, ek, C(bk, w0 + 1, 64, 2), ALU.subtract)
                     ts(C(bk, w0, 64, 2), u, m2, ALU.min, mn2, ALU.max)
                     scan(C(bk, w1, 128), C("SC", 0, 128), C(bk, w0, 128))
-        return {"tri": (C(bk, 2, 64, 3), -1.0), "act": (C(bk, 64, 64), 1.0), "pz": (C(bk, 0, 64), 1.0), "pd": (C(bk, 129, 64, 2), -1.0), "pe": (C(bk, 0, 64), 1.0), "dve3": (C(bk, 1, 64, 2), 1.0)}[mode]
+        return {"tri": (C(bk, 2, 64, 3), -1.0), "act": (C(bk, 320, 64), 1.0), "pz": (C(bk, 0, 64), 1.0), "pd": (C(bk, 129, 64, 2), -1.0), "pe": (C(bk, 0, 64), 1.0), "dve3": (C(bk, 1, 64, 2), 1.0)}[mode]
 
     def finish(t, h, b, sign):
         part[0] = "u%d%d" % (t, h)

@@ -4,44 +4,51 @@ from concourse.mybir import AluOpType as ALU, ActivationFunctionType as AF
 
 DAYS = 3
 PAR = dict(
-    OWN=(("am", "mm"), ("am", "mm"), ("am", "mm")),
-    ARR=(("ma", "ma"), ("aa", "ma"), ("aa", "ma")),
-    LOOK=(("8a8v", "8a8v"), ("8a8v", "8a8v"), ("8a8a", "8a8v")),
-    BIAS=(("pz", "pz"), ("dve3", "dve3"), ("tri", "tri")),
-    TRICP="dve", SUBS=(1, 1),
-    ECH=(("8a8a", "8a8a"), ("4a4a8a", "4a4a8a"), ("4a4a8a", "4a4a8a")),
-    TWO=False, JOINT=(0, 0, 1), ACTK=16, BACK=5, SHIFT={}, SUBPE=(0, 0), PAIR=True, DADD=(0, 0), EARLY=0.5, NG=2, PUPD="a", NACT=8, EC=False, NREP=8, TAILQ=(4, 4, 4, 2, 2), FUSE0=True,
+    OWN=(("8a8m", "8a8m"), ("8a8m", "8a8m"), ("8a8m", "8a8m")),
+    ARR=(("8m8a", "8m8a"), ("8m8a", "8m8a"), ("8m8a", "8m8a")), CUT=(1, 2),
+    TWO=(1, 0, 0), JOINT=(0, 0, 1),
+    LOOK=(("8a8a", "8a8v"), ("8a8a", "8a8v"), ("4v4a8a", "4v4a8a")),
+    ECH=(("4a4a8a", "4a4a8a"), ("4a4a4a4a", "4a4a4a4a"), ("4a4a8a", "4a4a8a")),
+    BIAS=(("8p8p", "8p8p"), ("5d5d6p", "5d5d6p"), ("8t8t", "8t8t")), BANK2=(10, 10, 0),
+    NACT=(4, 16), DADD=(2, 0, 0), TAILQ=("4p4q4p2n2q", "4p4q4p2n2q"),
+    WQ=("vvg", "a"), FQ="vss",
+    BACK=5, EARLY=0.5, LAG=2.0, MORE=0.5, TEMP=0.15, SAFE=(3.0, 1.0, 0.0), TRICP="vv", SPQ=("8n8n", "8n8n"),
 )
-COST = dict(CY=0.00104, GA=1.55, PCY=0.00066, WS=0.235, WX=0.245, HOP=4.5, FIX=0.01)
-VARY = ((1, {}), (1, dict(CY=0.0012, PCY=0.0008, GA=1.4, HOP=5.0, WS=0.22, WX=0.23)), (1, dict(CY=0.00083, PCY=0.00043, HOP=3.5)))
-TRIES, SEED = 2200, 7
+COST = dict(CY=0.00096, GA=1.5, PCY=0.0006, WS=0.235, WX=0.245, HOP=3.7, FIX=0.01, LS=0.9, PF=1.15)
+VARY = ((0.927, dict(CY=0.0009, GA=1.55, PCY=0.0008, HOP=3.5, LS=0.8, PF=1.0)),
+        (0.916, dict(CY=0.0009, GA=1.55, PCY=0.0005, HOP=5.2, LS=1.15, PF=1.6)),
+        (1.059, dict(CY=0.00083, GA=1.55, PCY=0.00043, HOP=2.8, LS=0.7, PF=1.0)),
+        (0.813, dict(CY=0.0012, GA=1.9, PCY=0.00065, HOP=3.5, LS=0.8, PF=1.0)),
+        (0.935, dict(CY=0.00105, GA=1.15, PCY=0.00055, HOP=3.5, LS=0.8, PF=1.0, WS=0.27, WX=0.2)))
+TRIES, SEED = 22000, 7
 
 F32, BF = "float32", "bfloat16"
 SCRATCH = {
     "K0": ("psum", [128, 512], F32), "K1": ("psum", [128, 512], F32), "B0": ("psum", [128, 512], F32), "B1": ("psum", [128, 512], F32),
-    "D0": ("psum", [128, 8, 2, 2, 2, 2, 4], F32), "D1": ("psum", [128, 8, 2, 2, 2, 2, 4], F32),
-    "SB": ("psum", [128, 512], F32), "SM": ("psum", [128, 512], F32),
+    "D": ("psum", [128, 8, 2, 2, 2, 2, 4], F32), "SB0": ("psum", [128, 512], F32), "SB1": ("psum", [128, 512], F32),
+    "SM": ("psum", [128, 512], F32),
     "ND": ("sbuf", [128, 16, 2, 4], "int32"), "P0": ("sbuf", [128, 2064], BF), "P1": ("sbuf", [128, 2064], BF),
-    "P2": ("sbuf", [128, 2064], BF), "PT": ("sbuf", [128, 128], BF), "Ew": ("sbuf", [128, 2048], F32), "Es": ("sbuf", [128, 2064], F32),
+    "P2": ("sbuf", [128, 2064], BF), "PT": ("sbuf", [128, 128], BF), "Ew": ("sbuf", [128, 2048], F32),
     "FC": ("sbuf", [128, 384], BF), "FR": ("sbuf", [128, 3072], BF), "ER": ("sbuf", [128, 384], BF), "DL": ("sbuf", [128, 4], F32),
-    "MM": ("sbuf", [128, 4], F32), "IO": ("sbuf", [128, 256], "int32"), "TI": ("sbuf", [128, 24], "int32"), "TF": ("sbuf", [128, 40], F32),
-    "Ib": ("sbuf", [128, 128], BF), "nIb": ("sbuf", [128, 128], BF), "Ibig": ("sbuf", [128, 128], BF), "Ih": ("sbuf", [128, 128], F32),
-    "If": ("sbuf", [128, 128], F32), "nIf": ("sbuf", [128, 128], F32), "Zp": ("sbuf", [128, 144], BF), "Zn": ("sbuf", [128, 144], BF),
-    "Dm": ("sbuf", [128, 2048], BF), "CR": ("sbuf", [128, 640], BF), "WR": ("sbuf", [128, 768], BF), "SC": ("sbuf", [128, 128], F32), "S3": ("sbuf", [128, 192], F32),
-    "AX": ("sbuf", [128, 4096], BF), "AB": ("sbuf", [128, 4096], BF), "PG": ("sbuf", [128, 1024], BF), "EQ": ("sbuf", [128, 2048], BF),
+    "MM": ("sbuf", [128, 4], F32), "IO": ("sbuf", [128, 128], "int32"), "TF": ("sbuf", [128, 40], F32),
+    "Ib": ("sbuf", [128, 128], BF), "Ibig": ("sbuf", [128, 128], BF), "If": ("sbuf", [128, 128], F32), "Zero": ("sbuf", [128, 128], BF),
+    "Zp0": ("sbuf", [128, 144], BF), "Zp1": ("sbuf", [128, 144], BF), "I16": ("sbuf", [128, 128], BF), "TR0": ("sbuf", [128, 128], "int32"),
+    "PL": ("sbuf", [128, 128], F32), "DT": ("sbuf", [128, 256], F32), "TT": ("sbuf", [128, 128], F32),
+    "Dm": ("sbuf", [128, 2048], BF), "CR": ("sbuf", [128, 768], BF), "SC": ("sbuf", [128, 128], F32), "S3": ("sbuf", [128, 192], F32),
+    "AX": ("sbuf", [128, 4096], BF), "AB": ("sbuf", [128, 4096], BF), "PG": ("sbuf", [128, 2048], BF), "EQ": ("sbuf", [128, 2048], BF),
     "JG": ("sbuf", [128, 2048], BF), "JW": ("sbuf", [128, 768], BF), "RR": ("sbuf", [128, 1024], BF), "LF": ("sbuf", [128, 256], F32),
     "LL": ("sbuf", [128, 1024], "uint16"),
-    "H": ("sbuf", [128, 4, 2, 2, 2, 2, 4], F32), "Y0": ("sbuf", [128, 2, 2, 2, 2, 2, 4], F32),
-    "Y1": ("sbuf", [128, 2, 2, 2, 2, 2, 4], F32), "Y2": ("sbuf", [128, 2, 2, 2, 2, 2, 4], F32), "Y3": ("sbuf", [128, 2, 2, 2, 2, 2, 4], F32), "KI": ("sbuf", [128, 2, 2, 2, 2, 2, 4], "int32"),
+    "H": ("sbuf", [128, 8, 2, 2, 2, 2, 4], F32), "Y0": ("sbuf", [128, 2, 2, 2, 2, 2, 4], F32),
+    "Y1": ("sbuf", [128, 2, 2, 2, 2, 2, 4], F32), "Y2": ("sbuf", [128, 2, 2, 2, 2, 2, 4], F32), "Y3": ("sbuf", [128, 2, 2, 2, 2, 2, 4], F32),
+    "KI": ("sbuf", [128, 4, 2, 2, 2, 2, 4], "int32"),
     "O32": ("sbuf", [128, 128], "int32"), "D32": ("sbuf", [128, 128], "int32"), "O16": ("sbuf", [128, 128], "uint16"),
-    "E": ("sbuf", [128, 6144], F32), "EC": ("sbuf", [128, 4096], F32), "X2": ("sbuf", [128, 2048], F32),
-    "U": ("sbuf", [128, 128], F32), "X": ("sbuf", [128, 128], F32), "V": ("sbuf", [128, 1600], F32), "NB": ("sbuf", [128, 4096], F32),
-    "EB": ("sbuf", [128, 2048], BF), "WB": ("sbuf", [128, 4096], BF), "WF": ("sbuf", [128, 4096], F32), "I2": ("sbuf", [128, 128], F32),
-    "I16": ("sbuf", [128, 128], BF), "PL": ("sbuf", [128, 128], F32), "DT": ("sbuf", [128, 256], F32), "TT": ("sbuf", [128, 128], F32),
-    "MK": ("sbuf", [128, 32], F32), "BT": ("sbuf", [128, 20], F32), "SN": ("sbuf", [128, 128], F32),
+    "E": ("sbuf", [128, 4096], F32), "EB": ("sbuf", [128, 2048], BF), "V": ("sbuf", [128, 800], F32),
+    "X2": ("sbuf", [128, 2048], F32), "NB": ("sbuf", [128, 4096], F32), "NC": ("sbuf", [128, 2, 1024], F32),
+    "U": ("sbuf", [128, 128], F32), "X": ("sbuf", [128, 128], F32),
+    "WF": ("sbuf", [128, 4096], F32), "WB": ("sbuf", [128, 4096], BF), "I2": ("sbuf", [128, 128], F32), "MK": ("sbuf", [128, 32], F32),
     "YB": ("sbuf", [128, 384], F32), "YS": ("sbuf", [128, 384], F32),
 }
-DMA_SEMS = ["d%d" % i for i in range(40)]
+DMA_SEMS = ["d%d" % i for i in range(60)]
 POOL_SEMS = ["p%d" % i for i in range(30)]
 SEMAPHORES = ["pe", "dve", "act", "pool", "sent"] + DMA_SEMS + POOL_SEMS + ["ar%d%d" % (t, h) for t in range(DAYS) for h in range(2)]
 EXT = {"pa": [128, 2048], "ea": [128, 2048], "nd": [128, 128], "fc": [128, 384], "er": [128, 384], "dl": [128, 1],
@@ -84,22 +91,12 @@ def isap(x):
     return isinstance(x, tuple)
 
 
-def shapes():
-    ng = PAR["NG"]
-    nb = 8 // ng
-    SCRATCH.update({"ND": ("sbuf", [128, 16, ng, nb], "int32"), "H": ("sbuf", [128, 8, 2, 2, 2, 2, nb], F32),
-                    "KI": ("sbuf", [128, 2 * ng, 2, 2, 2, 2, nb], "int32")})
-    for j in range(4):
-        SCRATCH["Y%d" % j] = ("sbuf", [128, 2, 2, 2, 2, 2, nb], F32)
-    for j in range(2):
-        SCRATCH["D%d" % j] = ("psum", [128, 32 // nb, 2, 2, 2, 2, nb], F32)
-
-
-shapes()
-
-
-def unit(u):
-    return (u, 0) if PAR["NG"] == 2 else (0, 64 * u)
+def pieces(s):
+    out, k = [], 0
+    for j in range(0, len(s), 2):
+        out.append((k, int(s[j]), s[j + 1]))
+        k += int(s[j])
+    return out
 
 
 def own_list(t, h, a=0, n=64):
@@ -107,17 +104,20 @@ def own_list(t, h, a=0, n=64):
 
 
 def arr_list(t, h, a=0, n=64):
-    return C("LL", t * 256 + h * 128 + 128 // PAR["NG"] + a, n)
+    return C("LL", t * 256 + h * 128 + 64 + a, n)
 
 
 def build():
-    ops, hist, bank, nsem, part, npg = [], {}, {}, {"hw": 0, "pool": 0}, [""], [0]
-    NG = PAR["NG"]
-    W, NB = 128 // NG, 8 // NG
+    ops, hist, bank, nsem, part, held = [], {}, {}, {"hw": 0, "pool": 0}, [""], []
 
-    def add(eng, call, args, outs, ins, busy, lat=0.0, sem=None, after=(), grp=None):
+    def add(eng, call, args, outs, ins, busy, lat=0.0, sem=None, after=(), grp=None, behind=None):
+        if held:
+            held.append((call, args, outs, ins, busy))
+            return None
         i = len(ops)
         deps = dict((d, True) for d in after)
+        if behind is not None:
+            deps[behind] = False
         flat = []
         for x in ins:
             flat += [x[1], x[2]] if x[0] == "*" else [x]
@@ -144,18 +144,28 @@ def build():
             b[1].append(i)
         if grp is not None:
             deps = dict((d, True) for d in deps if ops[d]["grp"] != grp or d in after)
-        ops.append(dict(grp=grp, part=part[0], eng=eng, call=call, args=args, deps=sorted(deps), busy=busy, lat=lat, sem=sem))
+        ops.append(dict(grp=grp, part=part[0], eng=eng, call=call, args=args, deps=sorted(d for d in deps if deps[d]),
+                        soft=[d for d in deps if not deps[d]], busy=busy, lat=lat, sem=sem))
         return i
+
+    def begin():
+        held.append(None)
+
+    def end(eng, grp=None):
+        calls = held[1:]
+        del held[:]
+        return add(eng, "many", [c[:2] for c in calls], [x for c in calls for x in c[2]], [x for c in calls for x in c[3]],
+                   tuple(sum(c[4][j] for c in calls) for j in range(5)), grp=grp[0] if grp else None, after=grp[1] if grp else ())
 
     def n_of(ap):
         return 16 * len(elems(ap[2])) if ap[0] == "*" else len(elems(ap))
 
     def cyc(n):
-        return (0.0, max(64, n), 0, 0)
+        return (0.0, max(64, n), 0, 0, 1)
 
     def one(out, x):
         if x[0] == "*":
-            return (0.05, 0, n_of(x), 0)
+            return (0.05, 0, n_of(x), 0, 0)
         return cyc(n_of(x) * (0.5 if width(out) == 2 and width(x) == 2 else 1))
 
     def cp(out, x):
@@ -176,28 +186,28 @@ def build():
         return add("dve", "memset", (out, v), [out], [], cyc(n_of(out) * width(out) / 4))
 
     def act(out, x, f=AF.Identity, scale=1.0, bias=0.0):
-        c = (0.065, 0, n_of(x), 0) if x[0] == "*" else cyc(n_of(x))
-        return add("act", "activation", (out, x, f, scale, bias), [out], [x] + [s for s in (bias,) if isap(s)], c)
+        c = (0.065, 0, n_of(x), 0, 0) if x[0] == "*" else cyc(n_of(x))
+        return add("act", "activation", (out, x, f, scale, bias), [out], [x], c)
 
     def move(who, out, x):
-        return act(out, x) if who in ("a", "act") else cp(out, x)
+        return act(out, x) if who == "a" else cp(out, x)
 
-    def mm(out, l, r, start, stop, grp=None, after=()):
-        c = (0.0, 0, 0, max(64, n_of(r)) * (4 if width(r) == 4 else 1))
-        return add("pe", "matmul", (out, l, r, start, stop), [out], [l, r], c, grp=grp, after=after)
+    def mm(out, l, r, start, stop, grp=None):
+        c = (0.0, 0, 0, max(64, n_of(r)) * (4 if width(r) == 4 else 1), 0)
+        return add("pe", "matmul", (out, l, r, start, stop), [out], [l, r], c, grp=grp)
 
     def dma(q, out, x, lat, call="dma_start", after=()):
         k = "pool" if q == "pool" else "hw"
         nsem[k] += 1
         sem = (POOL_SEMS if q == "pool" else DMA_SEMS)[nsem[k] - 1]
-        return add(q, call, (out, x), [out], [x], (1.4 if q == "pool" else 0.1, 0, 0, 0), lat + (0.2 if q == "pool" else -0.1), sem, after)
+        return add(q, call, (out, x), [out], [x], (1.4 if q == "pool" else 0.1, 0, 0, 0, 0), lat + (0.2 if q == "pool" else -0.1), sem, after)
 
-    def row(a, n):
-        return ("CR", (slice(0, 1), slice(a, a + n)))
+    def row(a, n, buf="CR"):
+        return (buf, (slice(0, 1), slice(a, a + n)))
 
     def send(t, hs):
-        s = add("pool", "send", (t, hs), [], [own_list(t, *unit(c)) for c in hs], (1.0, 0, 0, 0), 0.0, "sent")
-        return [add("rx", "rx", (arr_list(t, *unit(c)), own_list(t, *unit(c))), [arr_list(t, *unit(c))], [], (0.0, 0, 0, 0),
+        s = add("pool", "send", (t, hs), [], [own_list(t, c) for c in hs], (1.0, 0, 0, 0, 0), 0.0, "sent")
+        return [add("rx", "rx", (arr_list(t, c), own_list(t, c)), [arr_list(t, c)], [], (0.0, 0, 0, 0, 0),
                     ("hop", 2.0 if t == 0 else 0.0), "ar%d%d" % (t, c), after=[s]) for c in hs]
 
     def fr(t, h, a, n):
@@ -205,9 +215,6 @@ def build():
 
     def rr(t, h, a, n):
         return C("RR", t * 256 + h * 128 + a, n)
-
-    def wr(t, h, a, n):
-        return C("WR", t * 256 + h * 128 + a, n)
 
     def jw(t, h, a, n):
         return C("JW", t * 256 + h * 128 + a, n)
@@ -218,182 +225,159 @@ def build():
     dma("sp", C("FC", 0, 384), C("fc", 0, 384), 2.2)
     dma("sp", C("DL", 0, 1), A("dl", S_), 2.2)
     dma("sp", C("ER", 0, 384), C("er", 0, 384), 2.2)
-    add("pool", "iota", (C("IO", 0, 2 * W), [[1, 2 * W]], 0, -1), [C("IO", 0, 2 * W)], [], (0.6, 0, 0, 0))
-    io = C("IO", 0, 128)
-    for h in range(NG):
-        first = cp(own_list(0, h, 0, W), A("ND", S_, h))
-    rx0 = send(0, [0, 1]) if PAR["FUSE0"] else send(0, [0]) + send(0, [1])
+    add("pool", "iota", (C("IO", 0, 128), [[1, 128]], 0, -1), [C("IO", 0, 128)], [], (0.4, 0, 0, 0, 0))
+    for h in range(2):
+        cp(own_list(0, h), A("ND", S_, h))
+    rx0 = send(0, [0, 1])
     dma("pool", C("Ew", 0, 2048), C("ea", 0, 2048), 5.0, after=rx0)
-    if PAR["EC"]:
-        dma("sp", C("Es", 15, 2048), C("Ew", 0, 2048), 3.5, after=rx0)
     for p in ("P1", "P2"):
         dma("sp", C(p, 15, 2048), C("pa", 0, 2048), 3.0, after=rx0)
-    ts(C("Ib", 0, 128), io, 0.0, ALU.is_equal)
-    ts(C("nIb", 0, 128), io, 0.0, ALU.is_equal, -1.0, ALU.mult)
-    ts(C("Ibig", 0, 128), io, 0.0, ALU.is_equal, float(2 ** (30 if PAR["TWO"] else 26)), ALU.mult)
-    ts(C("If", 0, 128), io, 0.0, ALU.is_equal)
-    if any("pe" in m or "pd" in m for m in PAR["BIAS"]) or any(PAR["SUBPE"]):
-        ts(C("Ih", 0, 128), io, 0.0, ALU.is_equal, 0.5, ALU.mult)
-        ts(C("nIf", 0, 128), io, 0.0, ALU.is_equal, -1.0, ALU.mult)
+    ts(C("Ib", 0, 128), C("IO", 0, 128), 0.0, ALU.is_equal)
+
+    def select(out, x, pattern, op, fill, base, mult):
+        return add("pool", "affine_select", (out, x, pattern, op, fill, base, mult), [out], [x], (0.17, 2 * n_of(x), 0, 0, 0), behind=rx0[0] - 1)
+
+    def diag(who, out, v):
+        if who == "g":
+            return select(out, C("Zero", 0, 128), [[1, 128]], ALU.not_equal, v, 0, -1)
+        return act(out, C("Ib", 0, 128), AF.Identity, v) if who == "a" else ts(out, C("Ib", 0, 128), v, ALU.mult)
+
+    ms(C("Zero", 0, 128), 0.0)
+    for name, v in (("Ibig", 2.0 ** 30), ("I16", 1 / 16), ("If", 1.0), ("I2", 2.0)):
+        diag("a", C(name, 0, 128), v)
     ts(C("TF", 16, 8), C("IO", 0, 8, 16), 0.0, ALU.is_le)
     ts(C("TF", 24, 8), C("IO", 0, 8, 16), -15.0, ALU.is_ge)
     tt(C("TF", 32, 8), C("TF", 16, 8), C("TF", 24, 8), ALU.mult)
-    for z, v in (("Zp", 131072.0), ("Zn", -65536.0)) if PAR["TWO"] else (("Zp", 8192.0), ("Zn", -4096.0)):
-        ms(C(z, 0, 144), 0.0)
-        ts(C(z, 16, 8, 16), C("TF", 32, 8), v, ALU.mult)
-    ts(C("TI", 0, 16), C("IO", 0, 16), 15, ALU.bitwise_and)
-    ts(C("TF", 0, 16), C("TI", 0, 16), 0.0, ALU.is_equal)
-    for il in range(0 if PAR["TWO"] else 16):
-        ts(C("Dm", il * 128, 128), C("Ib", 0, 128), C("TF", il, 1), ALU.mult)
-    if PAR["TWO"]:
-        ts(("IO", (slice(0, 1), slice(128, 256))), ("IO", (slice(0, 1), slice(0, 128))), 2, ALU.arith_shift_right)
-        cp(row(0, 128), ("IO", (slice(0, 1), slice(128, 256))))
-        ts(C("I16", 0, 128), io, 0.0, ALU.is_equal, 1 / 16, ALU.mult)
-    else:
-        cp(row(0, 2 * W), ("IO", (slice(0, 1), slice(0, 2 * W))))
-    for k, v in enumerate((1.0, 2048.0 if PAR["TWO"] else 16.0 * NG, 8.5)):
+    for two in set(PAR["TWO"]):
+        ms(C("Zp%d" % two, 0, 144), 0.0)
+        ts(C("Zp%d" % two, 16, 8, 16), C("TF", 32, 8), 8192.0 * 16 ** two, ALU.mult)
+    ts(row(0, 128, "TR0"), row(0, 128, "IO"), 2, ALU.arith_shift_right)
+    cp(row(128, 128), row(0, 128, "TR0"))
+    ms(row(640, 128), 2048.0)
+    for il in range(16):
+        select(C("Dm", il * 128, 128), C("Ib", 0, 128), [[0, 8], [1, 16]], ALU.is_equal, 0.0, -il, 0)
+    cp(row(0, 128), row(0, 128, "IO"))
+    for k, v in enumerate((1.0, 32.0, 8.5)):
         ms(row(256 + 128 * k, 128), v)
     ms(C("SC", 0, 64, 2), 0.0)
     ms(C("SC", 1, 64, 2), 0.5)
     for j, v in enumerate((0.0, 1.0, -0.5)):
         ms(C("S3", j, 64, 3), v)
-    for k, v in enumerate((1.0, -1.0, 2.0, -2.0)):
-        ts(C("MM", k, 1), C("DL", 0, 1), v, ALU.mult)
-    m1, mn1, m2, mn2 = [C("MM", k, 1) for k in range(4)]
-    ms(C("SN", 0, 64, 2), 0.0)
-    ms(C("SN", 1, 64, 2), -0.5)
-    if any("pz" in m for m in PAR["BIAS"]):
-        ts(C("I2", 0, 128), io, 0.0, ALU.is_equal, 2.0, ALU.mult)
-        for k in range(32):
-            v = 2.0 ** (k % 16 + 1) * (1 if k < 16 else -1)
-            act(C("MK", k, 1), C("DL", 0, 1), AF.Identity, v)
-            for wt, days in (("WB", PAR["BIAS"][:1]), ("WF", PAR["BIAS"][1:])):
-                if any("pz" in m for m in days) and k not in (15, 16):
-                    act(C(wt, k * 128, 128), C("Ib", 0, 128), AF.Identity, v)
-    if any("act" in m for m in PAR["BIAS"]):
-        for k in range(18):
-            act(C("BT", k, 1), C("DL", 0, 1), AF.Identity, 1.0 - k / 2 if k < 16 else (16.0, float(PAR["ACTK"]))[k - 16])
-    if PAR["EC"]:
-        ts(C("TI", 16, 1), C("IO", 0, 1), -1.0, ALU.mult)
-        ts(C("TI", 17, 1), C("TI", 16, 1), 15, ALU.bitwise_and)
-        cp(C("TF", 39, 1), C("TI", 17, 1))
+    act(C("MK", 0, 1), C("DL", 0, 1), AF.Identity, 2.0)
+    for n in (1, 2, 4, 8):
+        act(C("MK", n, n), C("MK", 0, n), AF.Identity, 2.0 ** n)
+    act(C("MK", 16, 16), C("MK", 0, 16), AF.Identity, -1.0)
+    act(C("MM", 0, 1), C("DL", 0, 1), AF.Identity, -1.0)
+    m1, mn1, m2, mn2 = C("DL", 0, 1), C("MM", 0, 1), C("MK", 0, 1), C("MK", 16, 1)
+    made = set()
+
+    def power(t, k, sign):
+        out = C("WF" if t else "WB", (k - 1 + 16 * (sign < 0)) * 128, 128)
+        if (t > 0, k, sign) not in made:
+            made.add((t > 0, k, sign))
+            now, part[0] = part[0], "w%d" % (t > 0)
+            diag(PAR["WQ"][t > 0][k % len(PAR["WQ"][t > 0])], out, sign * 2.0 ** k)
+            part[0] = now
+        return out
+
     cp(C("PT", 0, 128), C("P0", 15, 128, 16))
     cp(C("P0", 31, 128, 16), C("PT", 0, 128))
     for t in range(DAYS):
         part[0] = "f%d" % t
-        for h in range(NG):
+        for h in range(2):
+            who = PAR["FQ"][t]
             for r in range(2):
-                cp(fr(t, h, r * W, W), C("FC", t * 128 + h * W, W))
-            for n in (128, 256)[2 - NG:]:
-                cp(fr(t, h, n, n), fr(t, h, 0, n))
+                if who == "v":
+                    ts(fr(t, h, r * 64, 64), C("FC", t * 128 + h * 64, 64), -1.0, ALU.mult)
+                else:
+                    act(fr(t, h, r * 64, 64), C("FC", t * 128 + h * 64, 64), AF.Identity, -1.0)
+            for n in (128, 256):
+                if who == "s":
+                    dma("sp", fr(t, h, n, n), fr(t, h, 0, n), 2.2)
+                else:
+                    move(who, fr(t, h, n, n), fr(t, h, 0, n))
         for d in range(t):
-            move(PAR["PUPD"], C("P%d" % t, 31 if d == 0 else 16, 128, 16), C("FC", d * 128, 128))
+            act(C("P%d" % t, 31 if d == 0 else 16, 128, 16), C("FC", d * 128, 128))
     part[0] = "0"
-    for h in range(NG if PAR["TWO"] else 0):
-        for r in range(2):
-            ts(C("LF", h * 128 + r * W, W), A("ND", S_, h), 16.0, ALU.mult, -120.0, ALU.add)
-        ts(jw(0, h, 0, W), C("LF", h * 128, W), 16 * MAGIC, ALU.add, -16 * MAGIC, ALU.add)
-        ts(C("TT", h * 64, 64), jw(0, h, 0, W), -17 / 16, ALU.mult, 136.0, ALU.add)
-        tt(C("DT", h * 128, 64), C("LF", h * 128, W), C("TT", h * 64, 64), ALU.add)
-    for h in range(0 if PAR["TWO"] else NG):
-        for r in range(2):
-            ts(C("LF", h * 128 + r * W, W), A("ND", S_, h), -7.5, ALU.add)
-        ts(jw(0, h, 0, W), C("LF", h * 128, W), MAGIC, ALU.add, -MAGIC, ALU.add)
-        tt(rr(0, h, 0, W), C("LF", h * 128, W), jw(0, h, 0, W), ALU.subtract)
+
+    def fields(t, h, a, src, out):
+        s = 16.0 if PAR["TWO"][t] else 1.0
+        ts(out, src, s, ALU.mult, -7.5 * s, ALU.add)
+        ts(jw(t, h, a, 64), out, s * MAGIC, ALU.add, -s * MAGIC, ALU.add)
+        if PAR["TWO"][t]:
+            act(C("TT", h * 64, 64), jw(t, h, a, 64), AF.Identity, -17 / 16, 136.0)
+            tt(C("DT", h * 128 + a, 64), out, C("TT", h * 64, 64), ALU.add)
+        else:
+            tt(rr(t, h, a, 64), out, jw(t, h, a, 64), ALU.subtract)
+
+    for h in range(2):
+        fields(0, h, 0, A("ND", S_, h), C("LF", h * 128, 64))
+        cp(C("LF", h * 128 + 64, 64), C("LF", h * 128, 64))
 
     def distances(t, h, arr):
         part[0] = "d%d%d%d" % (t, h, arr)
-        kb = "K%d" % (h if NG == 2 else arr)
-        key, grp = C(kb, arr * W, W), (t, h, arr)
-        lst = arr_list if arr else own_list
-        low = []
-        if PAR["TWO"]:
-            mm(key, row(384, 128), row(arr * W, W), True, False)
-            dv, dt = A("D%d" % h, 7), C("DT", h * 128 + arr * 64, 64)
-            if arr:
-                ts(dv, arr_list(t, h), 16.0, ALU.mult, -120.0, ALU.add)
-                ts(jw(t, h, 64, 64), dv, 16 * MAGIC, ALU.add, -16 * MAGIC, ALU.add)
-                if PAR["TWO"] == "a":
-                    act(C("TT", h * 64, 64), jw(t, h, 64, 64), AF.Identity, -17 / 16, 136.0)
-                else:
-                    ts(C("TT", h * 64, 64), jw(t, h, 64, 64), -17 / 16, ALU.mult, 136.0, ALU.add)
-                tt(dt, dv, C("TT", h * 64, 64), ALU.add)
-            low.append(mm(key, C("I16", 0, 128), jw(t, h, arr * 64, 64), False, False, grp))
+        key, grp, a, two = C("K%d" % h, arr * 64, 64), (t, h, arr), arr * 64, PAR["TWO"][t]
+        lst, dv = arr_list if arr else own_list, A("D", 4 * h)
+        if two:
+            mm(key, row(640, 128), row(128 + a, 64), True, False)
         else:
-            mm(key, row(512, 128), row(256, W), True, False)
-            mm(key, row(384, 128), row(arr * W, W), False, False)
-        for c in range(0 if PAR["TWO"] else W // 64):
-            a = arr * W + c * 64
-            if arr:
-                dv = A("D%d" % h, 7) if NG == 2 else A("D0", 3, c)
-                ts(dv, arr_list(t, h, c * 64), -7.5, ALU.add)
-                ts(jw(t, h, a, 64), dv, MAGIC, ALU.add, -MAGIC, ALU.add)
-                tt(rr(t, h, a, 64), dv, jw(t, h, a, 64), ALU.subtract)
-            low.append(mm(C(kb, a, 64), C("Ib", 0, 128), rr(t, h, a, 64), False, False, grp))
-            if NG == 1:
-                ts(wr(t, h, a, 64), rr(t, h, a, 64), 7.5, ALU.is_equal, -16.0, ALU.mult)
-                mm(C(kb, a, 64), C("Ib", 0, 128), wr(t, h, a, 64), False, False, grp, low[-1:])
+            begin()
+            mm(key, row(512, 128), row(256, 64), True, False)
+            mm(key, row(384, 128), row(a, 64), False, False)
+            end("pe")
         if arr:
-            dv = A("D%d" % h, 7) if NG == 2 else A("D0", 3)
-            for r in range(16):
-                eq = C("EQ", h * 1024 + r * W, W)
-                tt(eq, dv, C("LF", h * 128 + r * NB, W), ALU.is_equal)
-                mm(key, C("Ibig", 0, 128), eq, False, False, grp)
-        for c in range(W // 64):
-            pieces(t, h, arr, c, C(kb, arr * W + c * 64, 64), low[c:c + 1])
-        if PAR["TWO"]:
-            tt(C(kb, 128, 64) if arr else A("H", h * 4 + 2), key, dt, ALU.add)
-            if not arr:
-                act(A("H", h * 4), key)
-        elif not arr:
-            act(A("H", h * 2), key)
-        if PAR["EC"] and t == DAYS - 1:
-            part[0] = "c%d%d" % (h, arr)
-            for q in range(W // 32):
-                move(PAR["EC"][arr * W // 32 + q], C("EC", h * 2048 + arr * 16 * W + q * 512, 512), IND(C("Es", 16, 2048), lst(t, h, q * 32, 32)))
-
-    def pieces(t, h, arr, c, key, low):
-        lst, grp = arr_list if arr else own_list, (t, h, arr)
-        base, how = ((h + c) * 2 + arr) * 1024, PAR["ARR" if arr else "OWN"][t][h + c]
-        for q in range(2):
-            src, ab = IND(C("P%d" % t, 16, 2048), lst(t, h, c * 64 + q * 32, 32)), C("AB", base + q * 512, 512)
-            if how[q] == "a":
-                pg = C("PG", (npg[0] % 2) * 512, 512)
-                npg[0] += 1
+            fields(t, h, a, arr_list(t, h), dv)
+        low = [mm(key, C("I16" if two else "Ib", 0, 128), (jw if two else rr)(t, h, a, 64), False, False, grp)]
+        for q in range(4 if arr else 0):
+            eq = [C("EQ", h * 1024 + r * 64, 64) for r in range(4 * q, 4 * q + 4)]
+            for r in range(4):
+                tt(eq[r], dv, C("LF", h * 128 + (4 * q + r) * 4, 64), ALU.is_equal)
+            begin()
+            for r in range(4):
+                mm(key, C("Ibig", 0, 128), eq[r], False, False)
+            end("pe", (grp, ()))
+        base = (h * 2 + arr) * 1024
+        cut = PAR["CUT"][arr]
+        for k, n, form in pieces(PAR["ARR" if arr else "OWN"][t][h]):
+            src = IND(C("P%d" % t, 16, 2048), lst(t, h, k * 4, n * 4))
+            if form == "a":
+                pg, buf, x0 = C("PG", h * 1024 + k * 64, n * 64), "SB%d" % h, 0
                 act(pg, src)
-                mm(C("SB", 0, 512), C("Ib", 0, 128), pg, True, False)
-                mm(C("SB", 0, 512), C("nIb", 0, 128), fr(t, h, 0, 512), False, True)
-                act(ab, C("SB", 0, 512), AF.Abs, 0.5)
+                begin()
+                mm(C(buf, 0, n * 64), C("Ib", 0, 128), fr(t, h, 0, n * 64), True, False)
+                mm(C(buf, 0, n * 64), C("Ib", 0, 128), pg, False, True)
+                end("pe")
             else:
-                ax = C("AX", base + q * 512, 512)
-                tt(ax, src, fr(t, h, 0, 512), ALU.subtract)
-                if how[q] == "v":
-                    ts(ab, ax, 0.0, ALU.max)
-                else:
-                    act(ab, ax, AF.Abs, 0.5)
-        v = [q for q in range(2) if how[q] == "v"]
-        for il in range(16):
-            neg = low
-            if v:
-                neg = [mm(C(key[0], key[1][1].start + v[0] * 32, 32 * len(v)), C("Zn", 16 - il, 128),
-                          C("AX", base + v[0] * 512 + il, 32 * len(v), 16), False, False, grp, low)]
-            mm(key, C("Zp", 16 - il, 128), C("AB", base + il, 64, 16), False, False, grp, neg)
+                buf, x0 = "AX", base + k * 64
+                tt(C(buf, x0, n * 64), src, fr(t, h, 0, n * 64), ALU.add)
+            for j in range(cut):
+                act(C("AB", base + k * 64 + j, n * 64 // cut, cut), C(buf, x0 + j, n * 64 // cut, cut), AF.Abs, 0.5)
+        for q in range(4):
+            begin()
+            for il in range(q // 2 + q % 2 * 8, q // 2 + q % 2 * 8 + 8, 2):
+                mm(key, C("Zp%d" % two, 16 - il, 128), C("AB", base + il, 64, 16), False, False)
+            end("pe", (grp, low))
+        if two:
+            tt(C(key[0], 128, 64) if arr else A("H", h * 4 + 2), key, C("DT", h * 128 + a, 64), ALU.add)
+        if not arr:
+            act(A("H", h * (4 if two else 2)), key)
 
     def sel(buf, dims, fix={}, rev=()):
         name, pre = buf
         return A(name, *(pre + tuple(fix[b] if b in fix else (R_ if b in rev else S_) for b in dims) + (S_,)))
+
+    mnx, mxn, full = ((0, ALU.min), (1, ALU.max)), ((0, ALU.max), (1, ALU.min)), [3, 2, 1, 0]
 
     def sort(h):
         n = [0]
 
         def two():
             n[0] += 1
-            return [("H", (h * 2 + n[0] % 2,)), ("D%d" % h, (n[0] % 2,))]
+            return [("H", (h * 2 + n[0] % 2,)), ("D", (h * 2 + n[0] % 2,))]
 
         def whole():
             n[0] += 1
             return ("Y%d" % (h * 2 + n[0] % 2), ())
-        mnx = ((0, ALU.min), (1, ALU.max))
         x, dims = two(), [1, 4, 3, 2]
         for side, op in mnx:
             tt(sel(x[side], dims), A("H", h * 2), C("K%d" % h, 64, 64), op)
@@ -432,52 +416,11 @@ def build():
             z = (z[0], z[1] + (0,)) if c else ("KI", (h,))
             zd = [b for b in yd if b != c]
             zd.insert(3 - c, c)
-            for side, op in ((0, ALU.max), (1, ALU.min)):
+            for side, op in mxn:
                 tt(sel(z, zd, {c: side}), sel(y, yd, {c: 0}), sel(y, yd, {c: 1}), op)
             y, yd = z, zd
 
-    def sort_wide():
-        sb, ps = [("H", (1,)), ("H", (2,))], [("D0", (0,)), ("D0", (1,))]
-        seq = [(c, c == lv - 1) for lv in range(1, 5) for c in range(lv - 1, -1, -1)] + [(4, True)]
-        x0, x1, dims = ("H", (0,)), None, [1, 4, 3, 2]
-        for s, (c, first) in enumerate(seq):
-            last = c == 4
-            c2 = 3 if last else seq[s + 1][0]
-            rev = [b for b in range(c)] if first else []
-            yd = [2, 1, 0] if last else sorted([b for b in dims if b != c2] + [c], reverse=True)
-            ys = [sb[s % 2], ps[s % 2]]
-            if last:
-                ys = [(y[0], y[1] + (0,)) for y in ys]
-            for side, op in ((0, ALU.min), (1, ALU.max))[:1 if last else 2]:
-                for v in (0, 1):
-                    a = sel(x0, dims, {c2: 1 - v if c2 in rev else v}, rev)
-                    b = C("K1", 128 + v * 64, 64) if s == 0 else sel(x1, dims, {c2: v})
-                    tt(sel(ys[v], yd, {c: side}), a, b, op)
-            x0, x1, dims = ys[0], ys[1], yd
-        full, zz = [3, 2, 1, 0], ("Y0", (0,))
-        for side, op in ((0, ALU.max), (1, ALU.min)):
-            tt(sel(zz, full, {3: side}), sel(x0, dims), sel(x1, dims), op)
-        ys = [("H", (2, 0)), ("D0", (1, 0))]
-        for side, op in ((0, ALU.max), (1, ALU.min)):
-            for v in (0, 1):
-                tt(sel(ys[v], [3, 2, 0], {2: side}), sel(zz, full, {2: 0, 1: v}), sel(zz, full, {2: 1, 1: v}), op)
-        for side, op in ((0, ALU.max), (1, ALU.min)):
-            tt(sel(zz, full, {1: side}), sel(ys[0], [3, 2, 0]), sel(ys[1], [3, 2, 0]), op)
-        for side, op in ((0, ALU.max), (1, ALU.min)):
-            tt(sel(("KI", (0,)), full, {0: side}), sel(zz, full, {0: 0}), sel(zz, full, {0: 1}), op)
-
-    def sort_both():
-        n = [0]
-
-        def two(*more):
-            n[0] += 1
-            j = n[0] % 2
-            return [("H", (slice(j, 4, 2),) + more), ("D0", (slice(2 * j, 2 * j + 2),) + more)]
-        mnx, mxn = ((0, ALU.min), (1, ALU.max)), ((0, ALU.max), (1, ALU.min))
-        x, dims = two(), [1, 4, 3, 2]
-        for h in range(2):
-            for side, op in mnx:
-                tt(A(*(("H", h * 2 + 1), ("D0", 2 + h))[side]), A("H", h * 2), C("K%d" % h, 64, 64), op)
+    def network(two, x, dims, yz):
         for lv in (1, 2, 3, 4):
             y, c2 = two(*((0,) if lv == 4 else ())), lv - 1
             yd = ([] if lv == 4 else [lv]) + [0 if b == lv else b for b in dims if (b != c2 if c2 else b != lv)]
@@ -498,51 +441,7 @@ def build():
                     for v in (0, 1) if c else ():
                         tt(sel(y[v], yd, {c: side}), sel(x[0], dims, {c - 1: v}), sel(x[1], dims, {c - 1: v}), op)
                 x, dims = y, yd
-        z, zd = ("Y0", (S_,)), [3] + dims
-        for side, op in mxn:
-            tt(sel(z, zd, {3: side}), sel(x[0], dims), sel(x[1], dims), op)
-        y = two(0)
-        for side, op in mxn:
-            for v in (0, 1):
-                tt(sel(y[v], [3, 2, 0], {2: side}), sel(z, zd, {2: 0, 1: v}), sel(z, zd, {2: 1, 1: v}), op)
-        for side, op in mxn:
-            tt(sel(z, [3, 2, 1, 0], {1: side}), sel(y[0], [3, 2, 0]), sel(y[1], [3, 2, 0]), op)
-        for h in range(2):
-            for side, op in mxn:
-                tt(sel(("KI", (h,)), [3, 2, 1, 0], {0: side}), sel(("Y0", (h,)), [3, 2, 1, 0], {0: 0}), sel(("Y0", (h,)), [3, 2, 1, 0], {0: 1}), op)
-
-    def sort_two(h):
-        n = [0]
-
-        def two(*more):
-            n[0] += 1
-            j = n[0] % 2
-            return [("H", (slice(4 * h + j, 4 * h + 4, 2),) + more), ("D%d" % h, (slice(2 * j, 2 * j + 2),) + more)]
-        mnx, mxn = ((0, ALU.min), (1, ALU.max)), ((0, ALU.max), (1, ALU.min))
-        x, dims = two(), [1, 4, 3, 2]
-        for side, op in mnx:
-            tt(sel(x[side], dims), A("H", slice(4 * h, 4 * h + 4, 2)), C("K%d" % h, 64, 128), op)
-        for lv in (1, 2, 3, 4):
-            y, c2 = two(*((0,) if lv == 4 else ())), lv - 1
-            yd = ([] if lv == 4 else [lv]) + [0 if b == lv else b for b in dims if (b != c2 if c2 else b != lv)]
-            for side, op in mnx[:1 if lv == 4 else 2]:
-                for v in (0, 1):
-                    if c2:
-                        fx, fp, rv = {c2: v}, {c2: 1 - v}, [0] if side else []
-                    else:
-                        fx, fp, rv = {lv: v ^ side}, {lv: 1 - (v ^ side)}, []
-                    tt(sel(y[v], yd, {lv: side}, rv), sel(x[0], dims, fx), sel(x[1], dims, fp, range(1, lv + 1)), op)
-            x, dims = y, yd
-            for c in range(c2, -1, -1) if lv < 4 else ():
-                y = two()
-                yd = [c] + [b for b in dims if b != c - 1] if c else dims
-                for side, op in mnx:
-                    if c == 0:
-                        tt(sel(y[side], yd), sel(x[0], dims), sel(x[1], dims), op)
-                    for v in (0, 1) if c else ():
-                        tt(sel(y[v], yd, {c: side}), sel(x[0], dims, {c - 1: v}), sel(x[1], dims, {c - 1: v}), op)
-                x, dims = y, yd
-        z, zd, full = ("Y%d" % h, (S_,)), [3] + dims, [3, 2, 1, 0]
+        z, zd = (yz, (S_,)), [3] + dims
         for side, op in mxn:
             tt(sel(z, zd, {3: side}), sel(x[0], dims), sel(x[1], dims), op)
         y = two(0)
@@ -551,11 +450,38 @@ def build():
                 tt(sel(y[v], [3, 2, 0], {2: side}), sel(z, zd, {2: 0, 1: v}), sel(z, zd, {2: 1, 1: v}), op)
         for side, op in mxn:
             tt(sel(z, full, {1: side}), sel(y[0], [3, 2, 0]), sel(y[1], [3, 2, 0]), op)
+
+    def sort_both():
+        n = [0]
+
+        def two(*more):
+            n[0] += 1
+            j = n[0] % 2
+            return [("H", (slice(j, 4, 2),) + more), ("D", (slice(2 * j, 2 * j + 2),) + more)]
+        x, dims = two(), [1, 4, 3, 2]
+        for h in range(2):
+            for side, op in mnx:
+                tt(A(*(("H", h * 2 + 1), ("D", 2 + h))[side]), A("H", h * 2), C("K%d" % h, 64, 64), op)
+        network(two, x, dims, "Y0")
+        for h in range(2):
+            for side, op in mxn:
+                tt(sel(("KI", (h,)), full, {0: side}), sel(("Y0", (h,)), full, {0: 0}), sel(("Y0", (h,)), full, {0: 1}), op)
+
+    def sort_two(h):
+        n = [0]
+
+        def two(*more):
+            n[0] += 1
+            j = n[0] % 2
+            return [("H", (slice(4 * h + j, 4 * h + 4, 2),) + more), ("D", (slice(4 * h + 2 * j, 4 * h + 2 * j + 2),) + more)]
+        x, dims, y = two(), [1, 4, 3, 2], ("Y%d" % h, (S_,))
+        for side, op in mnx:
+            tt(sel(x[side], dims), A("H", slice(4 * h, 4 * h + 4, 2)), C("K%d" % h, 64, 128), op)
+        network(two, x, dims, y[0])
         for side, op in mxn:
-            tt(sel(("KI", (slice(2 * h, 2 * h + 2),)), full, {0: side}), sel(z, full, {0: 0}), sel(z, full, {0: 1}), op)
+            tt(sel(("KI", (slice(2 * h, 2 * h + 2),)), full, {0: side}), sel(y, full, {0: 0}), sel(y, full, {0: 1}), op)
 
     def choose_two(t, h):
-        distances(t, h, 1)
         part[0] = "s%d%d" % (t, h)
         sort_two(h)
         part[0] = "l%d%d" % (t, h)
@@ -566,249 +492,198 @@ def build():
         cp(own_list(t + 1, h), pl)
         if t < DAYS - 1:
             send(t + 1, [h])
+            s = 16.0 if PAR["TWO"][t + 1] else 1.0
+            begin()
             for r in range(2):
-                act(C("LF", h * 128 + r * 64, 64), pl, AF.Identity, 16.0, -120.0)
-            ts(jw(t + 1, h, 0, 64), oa, 16.0, ALU.mult)
-            ts(A("D%d" % h, 6), ob, 16.0, ALU.mult, 16.0, ALU.add)
-            tt(C("DT", h * 128, 64), A("D%d" % h, 6), oa, ALU.subtract)
+                act(C("LF", h * 128 + r * 64, 64), pl, AF.Identity, s, -7.5 * s)
+            end("act")
+            ts(jw(t + 1, h, 0, 64), oa, s, ALU.mult)
+            if PAR["TWO"][t + 1]:
+                ts(A("D", 4 * h + 1), ob, 16.0, ALU.mult, 16.0, ALU.add)
+                tt(C("DT", h * 128, 64), A("D", 4 * h + 1), oa, ALU.subtract)
+            else:
+                ts(rr(t + 1, h, 0, 64), ob, -7.5, ALU.add)
 
     def choose(t, h):
-        if PAR["TWO"]:
+        if PAR["TWO"][t]:
             return choose_two(t, h)
-        if not (PAR["JOINT"][t] and h):
-            distances(t, h, 1)
-        if PAR["JOINT"][t]:
-            if not h:
-                distances(t, 1, 1)
-                part[0] = "s%d0" % t
-                sort_both()
-        elif NG == 2:
+        if not PAR["JOINT"][t]:
             part[0] = "s%d%d" % (t, h)
             sort(h)
-        else:
-            part[0] = "s%d%d" % (t, h)
-            sort_wide()
+        elif not h:
+            part[0] = "s%d0" % t
+            sort_both()
         part[0] = "l%d%d" % (t, h)
-        ki, o32, o16 = A("KI", h), C("O32", h * 64, W), C("O16", h * 64, W)
-        if PAR["EC"] and t == DAYS - 1:
-            ts(o32, ki, NG - 1, ALU.arith_shift_right, 32 * W - 16, ALU.bitwise_and)
-            ts(o16, o32, C("TF", 39, 1), ALU.add)
-            return
-        ts(o32, ki, 3 + NG, ALU.arith_shift_right, 2 * W - 1, ALU.bitwise_and)
+        ki, o32, o16 = A("KI", h), C("O32", h * 64, 64), C("O16", h * 64, 64)
+        ts(o32, ki, 5, ALU.arith_shift_right, 127, ALU.bitwise_and)
         cp(o16, o32)
-        ts(C("D32", h * 64, W), ki, 15, ALU.bitwise_and)
-        ts(rr(t + 1, h, 0, W), C("D32", h * 64, W), -7.5, ALU.add)
-        look, c0, a = PAR["LOOK"][t][h], 0, 0
-        last, kb = t == DAYS - 1, "K%d" % (h if NG == 2 else 1)
-        for j in range(0, len(look), 2):
-            n = NB * int(look[j])
-            move(look[j + 1], C("JG", h * 1024 + c0 * 16, n * 16), IND(jw(t, h, 0, 2 * W), C("O16", h * 64 + c0, n)))
-            c0 += n
-            if last or c0 % 64 == 0:
-                lk = C(kb, 2 * W + a, c0 - a)
+        ts(C("D32", h * 64, 64), ki, 15, ALU.bitwise_and)
+        ts(rr(t + 1, h, 0, 64), C("D32", h * 64, 64), -7.5, ALU.add)
+        last, kb, a = t == DAYS - 1, "K%d" % h, 0
+        for k, n, who in pieces(PAR["LOOK"][t][h]):
+            move(who, C("JG", h * 1024 + k * 64, n * 64), IND(jw(t, h, 0, 128), C("O16", h * 64 + k * 4, n * 4)))
+            c0 = (k + n) * 4
+            if last or c0 == 64:
+                lk = C(kb, 128 + a, c0 - a)
                 mm(lk, C("Ib", 0, 128), rr(t + 1, h, a, c0 - a), True, False)
-                for il in range(16):
-                    mm(lk, C("Dm", il * 128, 128), C("JG", h * 1024 + a * 16 + il, c0 - a, 16), False, il == 15)
+                for q in range(0, 16, 4):
+                    begin()
+                    for il in range(q, q + 4):
+                        mm(lk, C("Dm", il * 128, 128), C("JG", h * 1024 + a * 16 + il, c0 - a, 16), False, il == 15)
+                    end("pe")
                 ts(own_list(t + 1, h, a, c0 - a), lk, 7.5, ALU.add)
-                if not last:
-                    send(t + 1, [h + a // 64])
                 a = c0
         if not last:
+            send(t + 1, [h])
+            begin()
             for r in range(2):
-                act(C("LF", h * 128 + r * W, W), C(kb, 2 * W, W))
-            ts(jw(t + 1, h, 0, W), C("LF", h * 128, W), MAGIC, ALU.add, -MAGIC, ALU.add)
+                act(C("LF", h * 128 + r * 64, 64), C(kb, 128, 64))
+            end("act")
+            ts(jw(t + 1, h, 0, 64), C("LF", h * 128, 64), MAGIC, ALU.add, -MAGIC, ALU.add)
 
-    def e_of(t, u, k, a=0, n=64):
-        return C("E", t * 2048 + unit(u)[0] * 1024 + unit(u)[1] + k * W + a, n)
-
-    def eb(t, u, k, n=64):
-        if t == 0 and PAR["BIAS"][0][0] in ("pz", "pd"):
-            return C("EB", unit(u)[0] * 1024 + unit(u)[1] + k * W, n)
-        return e_of(t, u, k, 0, n)
+    def e_of(t, h, k, n=1):
+        return C("E" if t else "EB", max(t - 1, 0) * 2048 + h * 1024 + k * 64, n * 64)
 
     def errors(t, h):
         part[0] = "e%d%d" % (t, h)
-        k0 = 0
-        ech = PAR["ECH"][t][h]
-        for n, who in [(int(ech[j]), ech[j + 1]) for j in range(0, len(ech), 2)]:
-            if PAR["EC"] and t == DAYS - 1:
-                src = IND(C("EC", h * 2048, 32 * W), C("O16", h * 64 + k0 * NB, n * NB))
-            else:
-                src = IND(C("Ew", 0, 2048), own_list(t + 1, h, k0 * NB, n * NB))
-            move(who, eb(t, h, k0, n * W), src)
-            k0 += n
-        if eb(t, h, 0) != e_of(t, h, 0) and not PAR["SUBPE"][t]:
-            dma("pool", e_of(t, h, 0, 0, 16 * W), eb(t, h, 0, 16 * W), 3.3)
+        for k, n, who in pieces(PAR["ECH"][t][h]):
+            move(who, e_of(t, h, k, n), IND(C("Ew", 0, 2048), own_list(t + 1, h, k * 4, n * 4)))
 
-    def bias(t, h):
-        mode, bk = PAR["BIAS"][t][h], "B%d" % h
-        subs = PAR["SUBS"][h] if mode == "tri" else 1
-        w = 64 // subs
-        for k in range(16):
-            for s in range(subs):
-                part[0] = "b%d%d%d" % (t, h, s)
-                ek, u, x = e_of(t, h, k, s * w, w), C("U", h * 64, 64), C("X", h * 64, 64)
-                if mode == "tri":
-                    w0, w1 = [((h * 2 + s) * 2 + (k + j) % 2) * 200 for j in range(2)]
-                    if k == 0:
-                        ms(C("V", w0 + 1, w, 3), 0.0)
-                    if k < 15:
-                        move(PAR["TRICP"], C("V", w0 + 3, w, 3), e_of(t, h, k + 1, s * w, w))
-                    else:
-                        ms(C("V", w0 + 3, w, 3), 0.0)
-                    y = C("V", w0 + 2, w, 3)
-                    ts(y, y if k > 0 else ek, m2, ALU.min, mn2, ALU.max)
-                    scan(C("V", w1, 3 * w) if k < 15 else C(bk, s * 3 * w, 3 * w), C("S3", 0, 3 * w), C("V", w0 + 1, 3 * w))
-                elif mode == "pz":
-                    z, wt = C(bk, 0, 64), "WB" if t == 0 else "WF"
-                    if t == DAYS - 1 and k % 2 == 0:
-                        z = A("D%d" % (1 - h if PAR["JOINT"][t] else h), 0) if h == 0 or not PAR["JOINT"][t] else A("D1", 0)
-                    ts(x, u if k > 0 else eb(t, h, 0), C("MK", k, 1), ALU.min, C("MK", 16 + k, 1), ALU.max)
-                    if k < 15:
-                        mm(z, C(wt, k * 128, 128), eb(t, h, k + 1), True, k == 0)
-                    if k > 0:
-                        mm(z, C(wt, (16 + k) * 128, 128), eb(t, h, k), k == 15, False)
-                        mm(z, C("I2", 0, 128), u, False, True)
-                    tt(u, z, x, ALU.subtract)
-                    if k == 15:
-                        ts(z, u, -2.0 ** -16, ALU.mult)
-                elif mode == "pd":
-                    z, o = C(bk, 0, 64), C("V", h * 400 + 1, 64, 2)
-                    if t == DAYS - 1 and k % 2:
-                        z = A("D%d" % h, 0)
-                    pos, neg = (C("Ib", 0, 128), C("nIb", 0, 128)) if t == 0 else (C("If", 0, 128), C("nIf", 0, 128))
-                    ts(C("V", h * 400 + 200, 64, 2), o if k > 0 else eb(t, h, 0), m2, ALU.min, mn2, ALU.max)
-                    if k == 0:
-                        cp(C("V", h * 400 + 201, 64, 2), eb(t, h, 1))
-                    else:
-                        if k < 15:
-                            mm(z, pos, eb(t, h, k + 1), True, False)
-                        mm(z, neg, eb(t, h, k), k == 15, True)
-                        tt(C("V", h * 400 + 201, 64, 2), z, o, ALU.add)
-                    scan(C("V", h * 400, 128) if k < 15 else C(bk, 128, 128), C("SN", 0, 128), C("V", h * 400 + 200, 128))
-                elif mode == "act" and k >= PAR["ACTK"]:
-                    b = C(bk, 256, 64)
-                    if k == PAR["ACTK"] and k:
-                        ts(b, C(bk, (k % 2) * 128 + 1, 64, 2), -1.0, ALU.mult, C("BT", 17, 1), ALU.add)
-                    if k > 0:
-                        tt(u, ek, b, ALU.add)
-                    act(x, u if k > 0 else ek, AF.Relu, 0.5, C("BT", k, 1))
-                    act(x, x, AF.Relu, -1.0, m2)
-                    if k > 0:
-                        tt(b, x, b, ALU.add)
-                    else:
-                        cp(b, x)
-                    if k == 15:
-                        ts(C(bk, 320, 64), b, -1.0, ALU.mult, C("BT", 16, 1), ALU.add)
-                elif mode == "pe":
-                    b = C(bk, 0, 64)
-                    if k > 0:
-                        tt(u, ek, b, ALU.subtract)
-                        mm(b, C("If", 0, 128), ek, True, False)
-                        mm(b, C("nIf", 0, 128), u, False, False)
-                    ts(x, u if k > 0 else ek, m2, ALU.min, mn2, ALU.max)
-                    mm(b, C("Ih", 0, 128), x, k == 0, True)
-                elif k == 0:
-                    ts(x, ek, 0.5, ALU.mult, m1, ALU.min)
-                    ts(C(bk, 129, 64, 2), x, mn1, ALU.max)
+    def bias(t, h, steps):
+        forms, bk = [f for _, n, f in pieces(PAR["BIAS"][t][h]) for _ in range(n)], "B%d" % h
+        k0 = forms.index("p") if "p" in forms else 16
+        u, x = C("U", h * 64, 64), C("X", h * 64, 64)
+        part[0] = "b%d%d0" % (t, h)
+        for k in steps:
+            ek = e_of(t, h, k)
+            if forms[k] == "t":
+                w0, w1 = [(h * 2 + (k + j) % 2) * 200 for j in range(2)]
+                if k == 0:
+                    ms(C("V", w0 + 1, 64, 3), 0.0)
+                if k < 15:
+                    move(PAR["TRICP"][h], C("V", w0 + 3, 64, 3), e_of(t, h, k + 1))
                 else:
-                    w0, w1 = (k % 2) * 128, (1 - k % 2) * 128
-                    tt(u, ek, C(bk, w0 + 1, 64, 2), ALU.subtract)
-                    ts(C(bk, w0, 64, 2), u, m2, ALU.min, mn2, ALU.max)
-                    scan(C(bk, w1, 128), C("SC", 0, 128), C(bk, w0, 128))
-        return {"tri": (C(bk, 2, 64, 3), -1.0), "act": (C(bk, 320, 64), 1.0), "pz": (C(bk, 0, 64), 1.0), "pd": (C(bk, 129, 64, 2), -1.0), "pe": (C(bk, 0, 64), 1.0), "dve3": (C(bk, 1, 64, 2), 1.0)}[mode]
+                    ms(C("V", w0 + 3, 64, 3), 0.0)
+                y = C("V", w0 + 2, 64, 3)
+                ts(y, y if k > 0 else ek, m2, ALU.min, mn2, ALU.max)
+                scan(C("V", w1, 192) if k < 15 else C(bk, 0, 192), C("S3", 0, 192), C("V", w0 + 1, 192))
+            elif forms[k] == "p":
+                j = k - k0
+                z = C(bk if k % 2 or k < PAR["BANK2"][t] else "SB%d" % h, 256, 64)
+                if k == k0 > 0:
+                    tt(u, ek, C(bk, (k % 2) * 128 + 1, 64, 2), ALU.subtract)
+                ts(x, u if k > 0 else ek, C("MK", j, 1), ALU.min, C("MK", 16 + j, 1), ALU.max)
+                wts = [power(t, j + 1, 1) if k < 15 else None, power(t, j + 1, -1) if k > 0 else None]
+                begin()
+                if k < 15:
+                    mm(z, wts[0], e_of(t, h, k + 1), True, k == 0)
+                if k > 0:
+                    mm(z, wts[1], ek, k == 15, False)
+                end("pe")
+                if k > 0:
+                    mm(z, C("I2", 0, 128), u, False, True)
+                tt(u, z, x, ALU.subtract)
+                if k == 15:
+                    ts(z, u, -2.0 ** (k0 - 16), ALU.mult)
+            elif k == 0:
+                ts(x, ek, 0.5, ALU.mult, m1, ALU.min)
+                ts(C(bk, 129, 64, 2), x, mn1, ALU.max)
+            else:
+                w0, w1 = (k % 2) * 128, (1 - k % 2) * 128
+                tt(u, ek, C(bk, w0 + 1, 64, 2), ALU.subtract)
+                ts(C(bk, w0, 64, 2), u, m2, ALU.min, mn2, ALU.max)
+                scan(C(bk, w1, 128), C("SC", 0, 128), C(bk, w0, 128))
+        return {"t": (C(bk, 2, 64, 3), -1.0), "d": (C(bk, 1, 64, 2), 1.0), "p": (C(bk, 256, 64), 1.0)}[forms[15]]
 
     def finish(t, h, b, sign):
         part[0] = "u%d%d" % (t, h)
         lo = t * 128 + h * 64
-        yb, ys, less = C("YB", lo, 64), C("YS", lo, 64), ALU.subtract if sign > 0 else ALU.add
-        last = t == DAYS - 1
-        if not last:
-            if t == 0 or not PAR["EC"]:
-                tt(C("Ew", h * 1024 + t, 64, 16), C("ER", lo, 64), b, less)
-            if PAR["EC"]:
-                tt(C("Es", h * 1024 + (31 if t == 0 else 16), 64, 16), C("ER", lo, 64), b, less)
-        ts(yb, b, sign, ALU.mult)
-        dma("sp", C("yb", lo, 64), yb, 2.0)
+        if t < DAYS - 1:
+            tt(C("Ew", h * 1024 + t, 64, 16), C("ER", lo, 64), b, ALU.subtract if sign > 0 else ALU.add)
+        ts(C("YB", lo, 64), b, sign, ALU.mult)
+        dma("sp", C("yb", lo, 64), C("YB", lo, 64), 2.0)
 
     def spread(t, h, b, sign):
         part[0] = "x%d%d" % (t, h)
         lo = t * 128 + h * 64
-        yb, ys, less = C("YB", lo, 64), C("YS", lo, 64), ALU.subtract if sign > 0 else ALU.add
-        last = t == DAYS - 1
-        w = 64 if last else W
-        if not last and NG == 1:
-            if h == 0:
-                return
-            h, lo = 0, t * 128
-            yb, ys = C("YB", lo, w), C("YS", lo, w)
-        sm = C("K%d" % h if last else "SM", 384, w)
-        if not last and not PAR["SUBPE"][t]:
-            nb, done = (t * 2 + h) * 1024, PAR["NACT"]
-            for r in range(done):
-                act(C("NB", nb + r * w, w), yb, AF.Identity, -1.0)
-            for r in range(done, PAR["NREP"], done):
-                dma("sp", C("NB", nb + r * w, done * w), C("NB", nb, done * w), 2.2)
-        k0 = 0
-        for n in PAR["TAILQ"] if last else [512 // w] * (w // 32):
+        yb, ys, last = C("YB", lo, 64), C("YS", lo, 64), t == DAYS - 1
+        sm = C("K%d" % h if last else "SM", 384, 64)
+        buf, x0 = ("X2", h * 1024) if last else ("NB", (t * 2 + h) * 1024)
+        if not last:
+            n = PAR["NACT"][t]
+            begin()
+            for r in range(4):
+                act(C(buf, x0 + r * 64, 64), yb, AF.Identity, -1.0)
+            end("act")
+            for r in range(4, n, 4):
+                act(C(buf, x0 + r * 64, 256), C(buf, x0, 256))
+            for r in range(n, 16, n):
+                dma("sp", C(buf, x0 + r * 64, n * 64), C(buf, x0, n * 64), 2.2)
+            dma("pool", C(buf, x0, 1024), e_of(t, h, 0, 16), 3.6, "dma_add")
+        todo = pieces(PAR["TAILQ"][h] if last else PAR["SPQ"][t])
+        for k0, n, form in todo:
+            a, m = x0 + k0 * 64, n
+            x = C(buf, a, n * 64)
             if last:
-                x = C("X2", h * 1024 + k0 * 64, n * 64)
+                begin()
                 for k in range(k0, k0 + n):
-                    tt(C("X2", h * 1024 + k * 64, 64), e_of(t, h, k), b, less)
-            else:
-                x = e_of(t, h, k0, 0, n * w)
-                if not PAR["SUBPE"][t] and k0 % PAR["NREP"] == 0:
-                    dma("pool", e_of(t, h, k0, 0, PAR["NREP"] * w), C("NB", nb, PAR["NREP"] * w), 3.3, "dma_add")
-            if not last and PAR["SUBPE"][t]:
-                bf = eb(t, h, 0) != e_of(t, h, 0)
-                mm(C("SB", 0, n * w), C("Ib" if bf else "If", 0, 128), eb(t, h, k0, n * w), True, False)
-                for k in range(n):
-                    mm(C("SB", k * w, w), C("nIf", 0, 128), yb, False, k == n - 1)
-                act(x, C("SB", 0, n * w), AF.Abs)
-            else:
-                act(x, x, AF.Abs)
-            x0, m = x[1][1].start, n
-            if last and PAR["PAIR"]:
+                    tt(C(buf, x0 + k * 64, 64), e_of(t, h, k), b, ALU.subtract if sign > 0 else ALU.add)
+                end("dve")
+            act(x, x, AF.Abs)
+            if form != "n":
                 m = n // 2
-                ps = A("D%d" % h, slice((k0 % 8) // 4 * 2, (k0 % 8) // 4 * 2 + m))
-                act(ps, C(x[0], x0 + m * w, m * w), AF.Exp, -1.0)
-                act(C(x[0], x0, m * w), C(x[0], x0, m * w), AF.Exp, -1.0)
-                tt(C(x[0], x0, m * w), C(x[0], x0, m * w), ps, ALU.add)
+                ps = C("SB%d" % h, 0, m * 64) if form == "p" else A("D", slice(4 * h, 4 * h + m))
+                begin()
+                act(ps, C(buf, a + m * 64, m * 64), AF.Exp, -1.0)
+                act(C(buf, a, m * 64), C(buf, a, m * 64), AF.Exp, -1.0)
+                end("act")
+                tt(C(buf, a, m * 64), C(buf, a, m * 64), ps, ALU.add)
             else:
-                act(x, x, AF.Exp, -1.0)
-            if last or not PAR["DADD"][t]:
-                for k in range(m):
-                    mm(sm, C("If", 0, 128), C(x[0], x0 + k * w, w), k0 + k == 0, k0 + n == 16 and k == m - 1)
-            k0 += n
-        if not last and PAR["DADD"][t]:
+                act(A("NC", h, slice(k0 * 64, (k0 + n) * 64)) if PAR["DADD"][t] else x, x, AF.Exp, -1.0)
+            if last and k0 + n == 16:
+                tt(ys, sm, C(buf, a, 64), ALU.add)
+                return dma("sp", C("ys", lo, 64), ys, 2.0)
+            for k in range(0, 0 if PAR["DADD"][t] else m, 2):
+                begin()
+                for j in range(k, min(k + 2, m)):
+                    mm(sm, C("If", 0, 128), C(buf, a + j * 64, 64), k0 + j == 0, k0 + n == (todo[-1][0] if last else 16) and j == m - 1)
+                end("pe")
+        if not PAR["DADD"][t]:
+            act(ys, sm)
+            return dma("sp", C("ys", lo, 64), ys, 2.0 + PAR["SAFE"][t])
+        if h == 1:
             m = 16
             for _ in range(PAR["DADD"][t]):
                 m //= 2
-                dma("pool", e_of(t, h, 0, 0, m * w), e_of(t, h, m, 0, m * w), 3.3, "dma_add")
-            for k in range(m if m > 1 else 0):
-                mm(sm, C("If", 0, 128), e_of(t, h, k, 0, w), k == 0, k == m - 1)
-            if m == 1:
-                return dma("sp", C("ys", lo, w), e_of(t, h, 0, 0, w), 2.0)
-        move("v" if last else "a", ys, sm)
-        dma("sp", C("ys", lo, w), ys, 2.0)
+                dma("pool", A("NC", S_, slice(0, m * 64)), A("NC", S_, slice(m * 64, m * 128)), 3.3, "dma_add")
+            for g in range(2):
+                for k in range(0, m, 2):
+                    begin()
+                    for j in (k, k + 1):
+                        mm(sm, C("If", 0, 128), A("NC", g, slice(j * 64, j * 64 + 64)), j == 0, j == m - 1)
+                    end("pe")
+                act(C("YS", t * 128 + g * 64, 64), sm)
+            dma("sp", C("ys", t * 128, 128), C("YS", t * 128, 128), 2.0 + PAR["SAFE"][t])
 
-    for h in range(NG):
-        distances(0, h, 0)
-    for h in range(NG):
+    for arr in range(2):
+        for h in range(2):
+            distances(0, h, arr)
+    for h in range(2):
         choose(0, h)
     for t in range(DAYS):
-        for h in range(NG):
-            if t + 1 < DAYS and not (PAR["EC"] and t + 1 == DAYS - 1):
+        for h in range(2):
+            if t + 1 < DAYS:
                 distances(t + 1, h, 0)
             errors(t, h)
-        bs = [bias(t, h) for h in range(2)]
+        for h in range(2):
+            bias(t, h, range(PAR["BANK2"][t]))
+            if t + 1 < DAYS:
+                distances(t + 1, h, 1)
+        bs = [bias(t, h, range(PAR["BANK2"][t], 16)) for h in range(2)]
         for h in range(2):
             finish(t, h, *bs[h])
         if t + 1 < DAYS:
-            for h in range(NG):
-                if PAR["EC"] and t + 1 == DAYS - 1:
-                    distances(t + 1, h, 0)
-            for h in range(NG):
+            for h in range(2):
                 choose(t + 1, h)
         for h in range(2):
             spread(t, h, *bs[h])
@@ -817,106 +692,176 @@ def build():
         far = 0
         for d in o["deps"]:
             far |= above[d]
-        o["near"] = [d for d in o["deps"] if not far >> d & 1]
-        above.append(far | sum(1 << d for d in o["deps"] if not far >> d & 1))
+        o["near"] = [d for d in o["deps"] + o["soft"] if not far >> d & 1]
+        for d in o["near"]:
+            far |= above[d] | 1 << d
+        above.append(far)
     return ops
 
 
 def priced(ops, cost):
     out = []
     for o in ops:
-        f, c, gth, p = o["busy"]
-        b = f + (cost["FIX"] + c * cost["CY"] if c else 0.0) + gth * cost["GA"] * cost["CY"] + p * cost["PCY"]
-        out.append((b, b + (cost["HOP"] + o["lat"][1] if isap(o["lat"]) else o["lat"])))
+        f, c, gth, p, n = o["busy"]
+        b = f * (cost["PF"] if o["eng"] == "pool" else 1.0) + n * cost["FIX"] + (c + gth * cost["GA"]) * cost["CY"] + p * cost["PCY"]
+        out.append((b, b + (cost["HOP"] + o["lat"][1] * cost["LS"] if isap(o["lat"]) else o["lat"] * cost["LS"])))
     return out
 
 
-def replay(ops, seq, price, cost):
-    free, fin, ws, wx = {}, [0.0] * len(ops), cost["WS"], cost["WX"]
-    for i in seq:
-        o = ops[i]
-        e = o["eng"]
-        t = free.get(e, 0.0) if e != "rx" else 0.0
-        for d in o["near"]:
-            a = ops[d]["eng"]
-            t = max(t, fin[d] + (0.0 if (a == e == "pe" or e == "rx") else (ws if a == e else wx)))
-        free[e] = t + price[i][0]
-        fin[i] = t + price[i][1]
-    return max(fin)
+def gap(ops, d, i, cost):
+    a, b = ops[d]["eng"], ops[i]["eng"]
+    return 0.0 if (a == b == "pe" or b == "rx" or d in ops[i]["soft"]) else cost["WS" if a == b else "WX"]
 
 
-def search(ops, tries):
-    sets = [(w, priced(ops, dict(COST, **v)), dict(COST, **v)) for w, v in VARY]
-    n, price, rs = len(ops), priced(ops, COST), np.random.RandomState(SEED)
-    pred, succ = [[] for _ in ops], [[] for _ in ops]
-    for i, o in enumerate(ops):
-        for d in o["near"]:
-            a, b = ops[d]["eng"], o["eng"]
-            gap = 0.0 if (a == b == "pe" or b == "rx") else COST["WS" if a == b else "WX"]
-            pred[i].append((d, gap))
-            succ[d].append((i, gap))
-    parts = sorted(set(o["part"] for o in ops))
-    of = np.array([parts.index(o["part"]) for o in ops])
-    prio = [0.0] * n
-    for i in range(n - 1, -1, -1):
-        prio[i] = min([prio[s] - gap for s, gap in succ[i]] + [0.0]) - price[i][1]
-    best, now, cur = None, None, np.array([PAR["SHIFT"].get(q[:2], 0.0) for q in parts])
-    for it in range(tries):
-        shift, base = cur.copy(), prio
-        if it % PAR["BACK"] == PAR["BACK"] - 1:
-            back = place(ops, price, succ, pred, [-times[i] - price[i][1] for i in range(n)], True)
-            shift, base = shift * 0, np.array([-back[i] - price[i][1] for i in range(n)])
-        elif it:
-            p = parts[rs.randint(len(parts))][:rs.randint(2, 5)]
-            shift[[j for j, q in enumerate(parts) if q.startswith(p)]] += rs.randn() * (0.4, 1.5, 5.0)[it % 3]
-        st = place(ops, price, pred, succ, list(base + shift[of]), False)
-        seq = sorted(range(n), key=lambda j: (st[j], j))
-        r = [replay(ops, seq, p, c) for _, p, c in sets]
-        score = sum(x * s[0] for x, s in zip(r, sets)) / sum(s[0] for s in sets) + PAR["EARLY"] * sum(st) / n
-        if now is None or score <= now - 0.3 * (1 - it / tries) * np.log(rs.rand()):
-            now, cur, prio, times = score, shift, base, st
-            if best is None or score < best[0]:
-                best = (score, r, st)
-    for i, o in enumerate(ops):
-        o["t"] = best[2][i]
-    return best[:2]
-
-
-def place(ops, price, pred, succ, prio, back):
-    n = len(ops)
-    left, st, rdy, begin, end = [len(p) for p in pred], [0.0] * n, [0.0] * n, {}, {}
-    rank = sorted(range(n), key=lambda i: prio[i])
-    pos = [0] * n
-    for j, i in enumerate(rank):
-        pos[i] = j
+def place(eng, busy, lat, pred, succ, prio, back, old=None, cut=0.0):
+    n = len(eng)
+    begin, end = [[] for _ in range(6)], [[] for _ in range(6)]
+    st, rdy = [0.0] * n if old is None else old.tolist(), [cut] * n
+    rank = np.argsort(prio, kind="stable")
+    if old is None:
+        left = [len(p) for p in pred]
+    else:
+        rank, left = rank[old[rank] >= cut], [0] * n
+        for i in np.nonzero((old < cut) & (old > cut - 3.0))[0].tolist():
+            if st[i] + busy[i] > cut and eng[i]:
+                begin[eng[i]], end[eng[i]] = [st[i]], [st[i] + busy[i]]
+        for i in rank.tolist():
+            for d, g in pred[i]:
+                if st[d] >= cut:
+                    left[i] += 1
+                elif st[d] + lat[d] + g > rdy[i]:
+                    rdy[i] = st[d] + lat[d] + g
+    pos = np.empty(n, int)
+    pos[rank] = np.arange(len(rank))
+    rank, pos = rank.tolist(), pos.tolist()
     ready, j = [not x for x in left], 0
-    for _ in range(n):
+    for _ in rank:
         while not ready[rank[j]]:
             j += 1
         i = rank[j]
         ready[i] = False
-        (busy, lat), e, t = price[i], ops[i]["eng"], rdy[i]
-        if e != "rx":
-            off = lat - busy if back else 0.0
-            s, f = begin.setdefault(e, []), end.setdefault(e, [])
+        b, l, e, t = busy[i], lat[i], eng[i], rdy[i]
+        if e:
+            s, f = begin[e], end[e]
+            off = l - b if back else 0.0
             t += off
-            lo, hi = 0, len(f)
-            while lo < hi:
-                mid = (lo + hi) // 2
-                lo, hi = (mid + 1, hi) if f[mid] <= t else (lo, mid)
-            while lo < len(s) and s[lo] < t + busy - 1e-9:
-                t, lo = max(t, f[lo]), lo + 1
-            s.insert(lo, t)
-            f.insert(lo, t + busy)
+            if not f or f[-1] <= t:
+                s.append(t)
+                f.append(t + b)
+            else:
+                lo, hi = 0, len(f)
+                m = hi
+                while lo < hi:
+                    mid = (lo + hi) // 2
+                    if f[mid] <= t:
+                        lo = mid + 1
+                    else:
+                        hi = mid
+                while lo < m and s[lo] < t + b - 1e-9:
+                    t = f[lo]
+                    lo += 1
+                s.insert(lo, t)
+                f.insert(lo, t + b)
             t -= off
         st[i] = t
-        for k, gap in succ[i]:
-            rdy[k] = max(rdy[k], t + lat + gap)
+        t += l
+        for k, g in succ[i]:
+            if t + g > rdy[k]:
+                rdy[k] = t + g
             left[k] -= 1
             if not left[k]:
                 ready[k] = True
-                j = min(j, pos[k])
-    return st
+                if pos[k] < j:
+                    j = pos[k]
+    return np.array(st)
+
+
+def replay(seq, eng, pred, busy, lat, old, keep):
+    free, fin = [0.0] * 6, [0.0] * len(seq) if old is None else list(old)
+    seen = 1
+    for i in seq[keep - 1::-1] if keep else ():
+        if not seen >> eng[i] & 1:
+            seen |= 1 << eng[i]
+            free[eng[i]] = fin[i] - lat[i] + busy[i]
+            if seen == 63:
+                break
+    for i in seq[keep:]:
+        e = eng[i]
+        t = free[e]
+        for d, g in pred[i]:
+            x = fin[d] + g
+            if x > t:
+                t = x
+        if e:
+            free[e] = t + busy[i]
+        fin[i] = t + lat[i]
+    return fin
+
+
+def search(ops, tries):
+    n, price, rs = len(ops), priced(ops, COST), np.random.RandomState(SEED)
+    eng = [("rx", "dve", "act", "pe", "pool", "sp").index(o["eng"]) for o in ops]
+    sets = []
+    for w, v in VARY:
+        c = dict(COST, **v)
+        p = priced(ops, c)
+        sets.append((w, [[(d, gap(ops, d, i, c)) for d in o["near"]] for i, o in enumerate(ops)], [x[0] for x in p], [x[1] for x in p]))
+    pred, succ = [[] for _ in ops], [[] for _ in ops]
+    for i, o in enumerate(ops):
+        for d in o["near"]:
+            pred[i].append((d, gap(ops, d, i, COST)))
+            succ[d].append((i, gap(ops, d, i, COST)))
+    parts = sorted(set(o["part"] for o in ops))
+    of = np.array([parts.index(o["part"]) for o in ops])
+    busy, lat = [p[0] for p in price], [p[1] for p in price]
+    alat, queue = np.array(lat), np.array(eng)
+    prio = [0.0] * n
+    for i in range(n - 1, -1, -1):
+        prio[i] = min([prio[s] - g for s, g in succ[i]] + [0.0]) - lat[i]
+    prio = np.array(prio) + np.array([PAR["LAG"] * ((q[2:3] == "1") + 3 * (q[0] == "x" and q[1] != "2")) for q in parts])[of]
+    best, now, masks, ends = None, None, {}, [None] * len(sets)
+    for it in range(tries):
+        base, cut = prio.copy(), 0.0
+        if it % PAR["BACK"] == PAR["BACK"] - 1:
+            base = -place(eng, busy, lat, succ, pred, -times - alat, True) - alat
+        elif it:
+            near = rs.rand() < 0.6
+            if near:
+                base = times.copy()
+            for _ in range(1 + (rs.rand() < PAR["MORE"])):
+                p = parts[rs.randint(len(parts))][:rs.randint(2, 5)]
+                if p not in masks:
+                    masks[p] = np.array([q.startswith(p) for q in parts])[of]
+                m = masks[p]
+                if rs.rand() < 0.5:
+                    lo, hi = times[m].min(), times[m].max()
+                    a = lo + rs.rand() * (hi - lo)
+                    m = m & ((times >= a) if rs.rand() < 0.5 else (times <= a))
+                if rs.rand() < 0.3:
+                    m = m & (queue == 1 + rs.randint(3))
+                base[m] += rs.randn() * (0.4, 1.5, 5.0)[it % 3]
+            if near:
+                m = base != times
+                if not m.any():
+                    continue
+                cut = max(0.0, np.minimum(base, times)[m].min() - 1.0)
+        st = place(eng, busy, lat, pred, succ, base, False, times if cut else None, cut)
+        bar = 1e9 if now is None else now - PAR["TEMP"] * (1 - it / tries) * np.log(rs.rand())
+        early, mine = PAR["EARLY"] * st.mean(), (st + alat).max()
+        if now is not None and mine + early > head + (bar - now) * 2 + 0.6:
+            continue
+        seq, keep = np.argsort(st, kind="stable").tolist(), int((st < cut).sum())
+        new = [replay(seq, eng, s[1], s[2], s[3], e, keep) for s, e in zip(sets, ends)]
+        r = [max(x) for x in new]
+        q = [x * s[0] for x, s in zip(r, sets)]
+        score = (sum(q) / len(q) + max(q)) / 2 + early
+        if score <= bar:
+            now, prio, times, head, ends = score, base, st, mine + early, new
+            if best is None or score < best[0]:
+                best = (score, r, st)
+    for i, o in enumerate(ops):
+        o["t"] = float(best[2][i])
+    return best[:2]
 
 
 def waits(ops, order):
@@ -928,7 +873,7 @@ def waits(ops, order):
     for e in order:
         for i in order[e]:
             if ops[i]["sem"] is None and i in inc:
-                total[e] = total.get(e, 0) + 1
+                total[e] = total.get(e, 0) + (len(ops[i]["args"]) if ops[i]["call"] == "many" else 1)
                 tick[i] = (e, total[e])
             elif ops[i]["sem"] is not None:
                 tick[i] = (ops[i]["sem"], 1)
@@ -968,7 +913,10 @@ def plan():
             order[ops[i]["eng"]].append(i)
         last = dict((ops[i]["grp"], i) for i in order["pe"] if ops[i]["grp"] is not None)
         for i in last.values():
-            ops[i]["args"] = ops[i]["args"][:4] + (True,)
+            if ops[i]["call"] == "many":
+                ops[i]["args"][-1] = ("matmul", ops[i]["args"][-1][1][:4] + (True,))
+            else:
+                ops[i]["args"] = ops[i]["args"][:4] + (True,)
         PLAN.update(best=best, ops=ops, order=order, total=waits(ops, order))
     return PLAN
 
@@ -992,11 +940,35 @@ def relay_program(g, core, T, topo):
             out = topo.engines(core, dst)
             rid, pid = topo.addr(dst, core)
             for t in range(DAYS):
-                name, key = arr_list(t, *unit(h))
+                name, key = arr_list(t, h)
                 sem = T.sem["ar%d%d" % (t, h)]
-                g.wait_ge(sem, n_in // 2 if t == 0 and PAR["FUSE0"] else n_in)
+                g.wait_ge(sem, n_in // 2 if t == 0 else n_in)
                 g.remote_dma(T[name][key], T[name][key], sem, T.sem.sent, pid, rid, bits(out))
             g.wait_ge(T.sem.sent, DAYS * len(out))
+
+
+def issue(q, call, a):
+    if call == "iota":
+        return q.iota(*a)
+    if call == "affine_select":
+        return q.affine_select(*a)
+    if call == "dma_start":
+        return q.dma_start(a[0], a[1])
+    if call == "dma_add":
+        return q.dma_start(a[0], a[1], accum_op=ALU.add)
+    if call == "activation":
+        return q.activation(a[0], a[1], a[2], bias=a[4], scale=a[3])
+    if call == "matmul":
+        return q.matmul(*a)
+    if call == "tensor_copy":
+        return q.tensor_copy(*a)
+    if call == "tensor_scalar":
+        return q.tensor_scalar(*a)
+    if call == "tensor_tensor":
+        return q.tensor_tensor(*a)
+    if call == "tensor_tensor_scan":
+        return q.tensor_tensor_scan(*a)
+    return q.memset(*a)
 
 
 def rank_program(g, core, T, topo):
@@ -1027,42 +999,24 @@ def rank_program(g, core, T, topo):
             used.append(o["sem"])
         if o["eng"] == "rx":
             continue
-        q, a, call = queue[o["eng"]], [ap(x) for x in o["args"]], o["call"]
+        q = queue[o["eng"]]
         for s, v in o["wait"].items():
             q.wait_ge(T.sem[s], v * step.get(s, 1))
-        if call == "send":
-            t, tr = a[0], []
-            for j, h in enumerate(a[1]):
+        if o["call"] == "send":
+            (t, hs), tr = o["args"], []
+            for j, h in enumerate(hs):
                 en = topo.engines(core, relays[h])
-                en = en[j * len(en) // len(a[1]):(j + 1) * len(en) // len(a[1])]
+                en = en[j * len(en) // len(hs):(j + 1) * len(en) // len(hs)]
                 rid, pid = topo.addr(relays[h], core)
                 tr.append(RemoteDMATransfer(dst_ids=[DstId(rid=rid, pnc=pid)], dma_engine_mask=bits(en),
-                                            remote_sem=T.sem["ar%d%d" % (t, h)], src=ap(own_list(t, *unit(h))), dst=ap(arr_list(t, *unit(h)))))
+                                            remote_sem=T.sem["ar%d%d" % (t, h)], src=ap(own_list(t, h)), dst=ap(arr_list(t, h))))
                 sent[0] += len(en)
             g.remote_dma_fused(tr, local_sem=T.sem.sent)
             continue
-        if call == "iota":
-            ins = g.iota(*a)
-        elif call == "dma_start":
-            ins = q.dma_start(a[0], a[1])
-        elif call == "dma_add":
-            ins = q.dma_start(a[0], a[1], accum_op=ALU.add)
-        elif call == "activation":
-            ins = q.activation(a[0], a[1], a[2], bias=a[4], scale=a[3])
-        elif call == "matmul":
-            ins = q.matmul(*a)
-        elif call == "tensor_copy":
-            ins = q.tensor_copy(*a)
-        elif call == "tensor_scalar":
-            ins = q.tensor_scalar(*a)
-        elif call == "tensor_tensor":
-            ins = q.tensor_tensor(*a)
-        elif call == "tensor_tensor_scan":
-            ins = q.tensor_tensor_scan(*a)
-        else:
-            ins = q.memset(*a)
-        if o["tick"]:
-            ins.then_inc(T.sem[o["tick"][0]], step.get(o["tick"][0], 1))
+        for call, args in o["args"] if o["call"] == "many" else [(o["call"], o["args"])]:
+            ins = issue(q, call, [ap(x) for x in args])
+            if o["tick"]:
+                ins.then_inc(T.sem[o["tick"][0]], step.get(o["tick"][0], 1))
     g.wait_ge(T.sem.sent, sent[0])
     for s, v in p["total"].items():
         g.wait_ge(T.sem[s], v)

import numpy as np
from concourse.bass import DstId, RemoteDMATransfer
from concourse.mybir import AluOpType as ALU, ActivationFunctionType as AF

DAYS = 3
PAR = dict(
    OWN=(("8a8m", "8a8m"), ("8a8m", "8a8m"), ("8a8m", "8a8m")),
    ARR=(("8m8a", "8m8a"), ("8m8a", "8m8a"), ("8m8a", "8m8a")), CUT=(1, 2),
    TWO=(1, 0, 0), JOINT=(0, 0, 1),
    LOOK=(("8a8a", "8a8v"), ("8a8a", "8a8v"), ("4v4a8a", "4v4a8a")),
    ECH=(("4a4a8a", "4a4a8a"), ("4a4a4a4a", "4a4a4a4a"), ("4a4a8a", "4a4a8a")),
    BIAS=(("8p8p", "8p8p"), ("5d5d6p", "5d5d6p"), ("8t8t", "8t8t")), BANK2=(10, 10, 0),
    NACT=(4, 16), DADD=(2, 0, 0), TAILQ=("4p4q4p2n2q", "4p4q4p2n2q"),
    WQ=("vvg", "a"), FQ="vss",
    BACK=5, EARLY=0.5, LAG=2.0, MORE=0.5, TEMP=0.15, SAFE=(3.0, 1.0, 0.0), TRICP="vv", SPQ=("8n8n", "8n8n"),
)
COST = dict(CY=0.00096, GA=1.5, PCY=0.0006, WS=0.235, WX=0.245, HOP=3.7, FIX=0.01, LS=0.9, PF=1.15)
VARY = ((0.927, dict(CY=0.0009, GA=1.55, PCY=0.0008, HOP=3.5, LS=0.8, PF=1.0)),
        (0.916, dict(CY=0.0009, GA=1.55, PCY=0.0005, HOP=5.2, LS=1.15, PF=1.6)),
        (1.059, dict(CY=0.00083, GA=1.55, PCY=0.00043, HOP=2.8, LS=0.7, PF=1.0)),
        (0.813, dict(CY=0.0012, GA=1.9, PCY=0.00065, HOP=3.5, LS=0.8, PF=1.0)),
        (0.935, dict(CY=0.00105, GA=1.15, PCY=0.00055, HOP=3.5, LS=0.8, PF=1.0, WS=0.27, WX=0.2)))
TRIES, SEED = 22000, 7

F32, BF = "float32", "bfloat16"
SCRATCH = {
    "K0": ("psum", [128, 512], F32), "K1": ("psum", [128, 512], F32), "B0": ("psum", [128, 512], F32), "B1": ("psum", [128, 512], F32),
    "D": ("psum", [128, 8, 2, 2, 2, 2, 4], F32), "SB0": ("psum", [128, 512], F32), "SB1": ("psum", [128, 512], F32),
    "SM": ("psum", [128, 512], F32),
    "ND": ("sbuf", [128, 16, 2, 4], "int32"), "P0": ("sbuf", [128, 2064], BF), "P1": ("sbuf", [128, 2064], BF),
    "P2": ("sbuf", [128, 2064], BF), "PT": ("sbuf", [128, 128], BF), "Ew": ("sbuf", [128, 2048], F32),
    "FC": ("sbuf", [128, 384], BF), "FR": ("sbuf", [128, 3072], BF), "ER": ("sbuf", [128, 384], BF), "DL": ("sbuf", [128, 4], F32),
    "MM": ("sbuf", [128, 4], F32), "IO": ("sbuf", [128, 128], "int32"), "TF": ("sbuf", [128, 40], F32),
    "Ib": ("sbuf", [128, 128], BF), "Ibig": ("sbuf", [128, 128], BF), "If": ("sbuf", [128, 128], F32), "Zero": ("sbuf", [128, 128], BF),
    "Zp0": ("sbuf", [128, 144], BF), "Zp1": ("sbuf", [128, 144], BF), "I16": ("sbuf", [128, 128], BF), "TR0": ("sbuf", [128, 128], "int32"),
    "PL": ("sbuf", [128, 128], F32), "DT": ("sbuf", [128, 256], F32), "TT": ("sbuf", [128, 128], F32),
    "Dm": ("sbuf", [128, 2048], BF), "CR": ("sbuf", [128, 768], BF), "SC": ("sbuf", [128, 128], F32), "S3": ("sbuf", [128, 192], F32),
    "AX": ("sbuf", [128, 4096], BF), "AB": ("sbuf", [128, 4096], BF), "PG": ("sbuf", [128, 2048], BF), "EQ": ("sbuf", [128, 2048], BF),
    "JG": ("sbuf", [128, 2048], BF), "JW": ("sbuf", [128, 768], BF), "RR": ("sbuf", [128, 1024], BF), "LF": ("sbuf", [128, 256], F32),
    "LL": ("sbuf", [128, 1024], "uint16"),
    "H": ("sbuf", [128, 8, 2, 2, 2, 2, 4], F32), "Y0": ("sbuf", [128, 2, 2, 2, 2, 2, 4], F32),
    "Y1": ("sbuf", [128, 2, 2, 2, 2, 2, 4], F32), "Y2": ("sbuf", [128, 2, 2, 2, 2, 2, 4], F32), "Y3": ("sbuf", [128, 2, 2, 2, 2, 2, 4], F32),
    "KI": ("sbuf", [128, 4, 2, 2, 2, 2, 4], "int32"),
    "O32": ("sbuf", [128, 128], "int32"), "D32": ("sbuf", [128, 128], "int32"), "O16": ("sbuf", [128, 128], "uint16"),
    "E": ("sbuf", [128, 4096], F32), "EB": ("sbuf", [128, 2048], BF), "V": ("sbuf", [128, 800], F32),
    "X2": ("sbuf", [128, 2048], F32), "NB": ("sbuf", [128, 4096], F32), "NC": ("sbuf", [128, 2, 1024], F32),
    "U": ("sbuf", [128, 128], F32), "X": ("sbuf", [128, 128], F32),
    "WF": ("sbuf", [128, 4096], F32), "WB": ("sbuf", [128, 4096], BF), "I2": ("sbuf", [128, 128], F32), "MK": ("sbuf", [128, 32], F32),
    "YB": ("sbuf", [128, 384], F32), "YS": ("sbuf", [128, 384], F32),
}
DMA_SEMS = ["d%d" % i for i in range(60)]
POOL_SEMS = ["p%d" % i for i in range(30)]
SEMAPHORES = ["pe", "dve", "act", "pool", "sent"] + DMA_SEMS + POOL_SEMS + ["ar%d%d" % (t, h) for t in range(DAYS) for h in range(2)]
EXT = {"pa": [128, 2048], "ea": [128, 2048], "nd": [128, 128], "fc": [128, 384], "er": [128, 384], "dl": [128, 1],
       "yb": [128, 384], "ys": [128, 384]}
S_ = slice(None)
R_ = slice(None, None, -1)
MAGIC = float(3 * 2 ** 26)


def A(name, *key):
    return (name, (S_,) + tuple(key))


def C(name, a, n, step=1):
    return A(name, slice(a, a + (n - 1) * step + 1, step if step > 1 else None))


def IND(win, off):
    return ("*", win, off)


def shape_of(n):
    return EXT[n] if n in EXT else SCRATCH[n][1]


def elems(ap):
    sh = shape_of(ap[0])[1:]
    return np.arange(int(np.prod(sh))).reshape(sh)[ap[1][1:]].ravel()


def where(ap):
    return "dram" if ap[0] in EXT else SCRATCH[ap[0]][0]


def width(ap):
    return 2 if SCRATCH[ap[0]][2] in (BF, "uint16") else 4


def isap(x):
    return isinstance(x, tuple)


def pieces(s):
    out, k = [], 0
    for j in range(0, len(s), 2):
        out.append((k, int(s[j]), s[j + 1]))
        k += int(s[j])
    return out


def own_list(t, h, a=0, n=64):
    return C("LL", t * 256 + h * 128 + a, n)


def arr_list(t, h, a=0, n=64):
    return C("LL", t * 256 + h * 128 + 64 + a, n)


def build():
    ops, hist, bank, nsem, part, held = [], {}, {}, {"hw": 0, "pool": 0}, [""], []

    def add(eng, call, args, outs, ins, busy, lat=0.0, sem=None, after=(), grp=None, behind=None):
        if held:
            held.append((call, args, outs, ins, busy))
            return None
        i = len(ops)
        deps = dict((d, True) for d in after)
        if behind is not None:
            deps[behind] = False
        flat = []
        for x in ins:
            flat += [x[1], x[2]] if x[0] == "*" else [x]
        for aps, wr in ((flat, False), (outs, True)):
            for ap in aps:
                m = np.zeros(int(np.prod(shape_of(ap[0])[1:])), bool)
                m[elems(ap)] = True
                h = hist.setdefault(ap[0], [])
                for (j, jw, jm) in h:
                    if j != i and (wr or jw) and (m & jm).any():
                        deps[j] = True
                if wr:
                    h[:] = [e for e in h if (e[2] & ~m).any()]
                h.append((i, wr, m))
        for n in set(ap[0] for ap in flat + list(outs) if where(ap) == "psum"):
            b = bank.setdefault(n, [None, [], []])
            if b[0] != eng:
                b[0], b[2], b[1] = eng, b[1], []
            for j in b[2]:
                deps[j] = True
            if eng == "pe":
                for j in b[1]:
                    deps[j] = True
            b[1].append(i)
        if grp is not None:
            deps = dict((d, True) for d in deps if ops[d]["grp"] != grp or d in after)
        ops.append(dict(grp=grp, part=part[0], eng=eng, call=call, args=args, deps=sorted(d for d in deps if deps[d]),
                        soft=[d for d in deps if not deps[d]], busy=busy, lat=lat, sem=sem))
        return i

    def begin():
        held.append(None)

    def end(eng, grp=None):
        calls = held[1:]
        del held[:]
        return add(eng, "many", [c[:2] for c in calls], [x for c in calls for x in c[2]], [x for c in calls for x in c[3]],
                   tuple(sum(c[4][j] for c in calls) for j in range(5)), grp=grp[0] if grp else None, after=grp[1] if grp else ())

    def n_of(ap):
        return 16 * len(elems(ap[2])) if ap[0] == "*" else len(elems(ap))

    def cyc(n):
        return (0.0, max(64, n), 0, 0, 1)

    def one(out, x):
        if x[0] == "*":
            return (0.05, 0, n_of(x), 0, 0)
        return cyc(n_of(x) * (0.5 if width(out) == 2 and width(x) == 2 else 1))

    def cp(out, x):
        return add("dve", "tensor_copy", (out, x), [out], [x], one(out, x))

    def ts(out, x, s1, o0, s2=None, o1=None):
        a = (out, x, s1, s2, o0) + (() if o1 is None else (o1,))
        return add("dve", "tensor_scalar", a, [out], [x] + [s for s in (s1, s2) if isap(s)], one(out, x))

    def tt(out, x, y, op):
        c = one(out, x) if x[0] == "*" else cyc(n_of(x) * (2 if where(x) == where(y) == "sbuf" else 1))
        return add("dve", "tensor_tensor", (out, x, y, op), [out], [x, y], c)

    def scan(out, d0, d1):
        return add("dve", "tensor_tensor_scan", (out, d0, d1, 0.0, ALU.mult, ALU.add), [out], [d0, d1], cyc(n_of(d1)))

    def ms(out, v):
        return add("dve", "memset", (out, v), [out], [], cyc(n_of(out) * width(out) / 4))

    def act(out, x, f=AF.Identity, scale=1.0, bias=0.0):
        c = (0.065, 0, n_of(x), 0, 0) if x[0] == "*" else cyc(n_of(x))
        return add("act", "activation", (out, x, f, scale, bias), [out], [x], c)

    def move(who, out, x):
        return act(out, x) if who == "a" else cp(out, x)

    def mm(out, l, r, start, stop, grp=None):
        c = (0.0, 0, 0, max(64, n_of(r)) * (4 if width(r) == 4 else 1), 0)
        return add("pe", "matmul", (out, l, r, start, stop), [out], [l, r], c, grp=grp)

    def dma(q, out, x, lat, call="dma_start", after=()):
        k = "pool" if q == "pool" else "hw"
        nsem[k] += 1
        sem = (POOL_SEMS if q == "pool" else DMA_SEMS)[nsem[k] - 1]
        return add(q, call, (out, x), [out], [x], (1.4 if q == "pool" else 0.1, 0, 0, 0, 0), lat + (0.2 if q == "pool" else -0.1), sem, after)

    def row(a, n, buf="CR"):
        return (buf, (slice(0, 1), slice(a, a + n)))

    def send(t, hs):
        s = add("pool", "send", (t, hs), [], [own_list(t, c) for c in hs], (1.0, 0, 0, 0, 0), 0.0, "sent")
        return [add("rx", "rx", (arr_list(t, c), own_list(t, c)), [arr_list(t, c)], [], (0.0, 0, 0, 0, 0),
                    ("hop", 2.0 if t == 0 else 0.0), "ar%d%d" % (t, c), after=[s]) for c in hs]

    def fr(t, h, a, n):
        return C("FR", (t * 2 + h) * 512 + a, n)

    def rr(t, h, a, n):
        return C("RR", t * 256 + h * 128 + a, n)

    def jw(t, h, a, n):
        return C("JW", t * 256 + h * 128 + a, n)

    part[0] = "0"
    dma("sp", A("ND"), C("nd", 0, 128), 2.1)
    dma("act", C("P0", 15, 2048), C("pa", 0, 2048), 2.9)
    dma("sp", C("FC", 0, 384), C("fc", 0, 384), 2.2)
    dma("sp", C("DL", 0, 1), A("dl", S_), 2.2)
    dma("sp", C("ER", 0, 384), C("er", 0, 384), 2.2)
    add("pool", "iota", (C("IO", 0, 128), [[1, 128]], 0, -1), [C("IO", 0, 128)], [], (0.4, 0, 0, 0, 0))
    for h in range(2):
        cp(own_list(0, h), A("ND", S_, h))
    rx0 = send(0, [0, 1])
    dma("pool", C("Ew", 0, 2048), C("ea", 0, 2048), 5.0, after=rx0)
    for p in ("P1", "P2"):
        dma("sp", C(p, 15, 2048), C("pa", 0, 2048), 3.0, after=rx0)
    ts(C("Ib", 0, 128), C("IO", 0, 128), 0.0, ALU.is_equal)

    def select(out, x, pattern, op, fill, base, mult):
        return add("pool", "affine_select", (out, x, pattern, op, fill, base, mult), [out], [x], (0.17, 2 * n_of(x), 0, 0, 0), behind=rx0[0] - 1)

    def diag(who, out, v):
        if who == "g":
            return select(out, C("Zero", 0, 128), [[1, 128]], ALU.not_equal, v, 0, -1)
        return act(out, C("Ib", 0, 128), AF.Identity, v) if who == "a" else ts(out, C("Ib", 0, 128), v, ALU.mult)

    ms(C("Zero", 0, 128), 0.0)
    for name, v in (("Ibig", 2.0 ** 30), ("I16", 1 / 16), ("If", 1.0), ("I2", 2.0)):
        diag("a", C(name, 0, 128), v)
    ts(C("TF", 16, 8), C("IO", 0, 8, 16), 0.0, ALU.is_le)
    ts(C("TF", 24, 8), C("IO", 0, 8, 16), -15.0, ALU.is_ge)
    tt(C("TF", 32, 8), C("TF", 16, 8), C("TF", 24, 8), ALU.mult)
    for two in set(PAR["TWO"]):
        ms(C("Zp%d" % two, 0, 144), 0.0)
        ts(C("Zp%d" % two, 16, 8, 16), C("TF", 32, 8), 8192.0 * 16 ** two, ALU.mult)
    ts(row(0, 128, "TR0"), row(0, 128, "IO"), 2, ALU.arith_shift_right)
    cp(row(128, 128), row(0, 128, "TR0"))
    ms(row(640, 128), 2048.0)
    for il in range(16):
        select(C("Dm", il * 128, 128), C("Ib", 0, 128), [[0, 8], [1, 16]], ALU.is_equal, 0.0, -il, 0)
    cp(row(0, 128), row(0, 128, "IO"))
    for k, v in enumerate((1.0, 32.0, 8.5)):
        ms(row(256 + 128 * k, 128), v)
    ms(C("SC", 0, 64, 2), 0.0)
    ms(C("SC", 1, 64, 2), 0.5)
    for j, v in enumerate((0.0, 1.0, -0.5)):
        ms(C("S3", j, 64, 3), v)
    act(C("MK", 0, 1), C("DL", 0, 1), AF.Identity, 2.0)
    for n in (1, 2, 4, 8):
        act(C("MK", n, n), C("MK", 0, n), AF.Identity, 2.0 ** n)
    act(C("MK", 16, 16), C("MK", 0, 16), AF.Identity, -1.0)
    act(C("MM", 0, 1), C("DL", 0, 1), AF.Identity, -1.0)
    m1, mn1, m2, mn2 = C("DL", 0, 1), C("MM", 0, 1), C("MK", 0, 1), C("MK", 16, 1)
    made = set()

    def power(t, k, sign):
        out = C("WF" if t else "WB", (k - 1 + 16 * (sign < 0)) * 128, 128)
        if (t > 0, k, sign) not in made:
            made.add((t > 0, k, sign))
            now, part[0] = part[0], "w%d" % (t > 0)
            diag(PAR["WQ"][t > 0][k % len(PAR["WQ"][t > 0])], out, sign * 2.0 ** k)
            part[0] = now
        return out

    cp(C("PT", 0, 128), C("P0", 15, 128, 16))
    cp(C("P0", 31, 128, 16), C("PT", 0, 128))
    for t in range(DAYS):
        part[0] = "f%d" % t
        for h in range(2):
            who = PAR["FQ"][t]
            for r in range(2):
                if who == "v":
                    ts(fr(t, h, r * 64, 64), C("FC", t * 128 + h * 64, 64), -1.0, ALU.mult)
                else:
                    act(fr(t, h, r * 64, 64), C("FC", t * 128 + h * 64, 64), AF.Identity, -1.0)
            for n in (128, 256):
                if who == "s":
                    dma("sp", fr(t, h, n, n), fr(t, h, 0, n), 2.2)
                else:
                    move(who, fr(t, h, n, n), fr(t, h, 0, n))
        for d in range(t):
            act(C("P%d" % t, 31 if d == 0 else 16, 128, 16), C("FC", d * 128, 128))
    part[0] = "0"

    def fields(t, h, a, src, out):
        s = 16.0 if PAR["TWO"][t] else 1.0
        ts(out, src, s, ALU.mult, -7.5 * s, ALU.add)
        ts(jw(t, h, a, 64), out, s * MAGIC, ALU.add, -s * MAGIC, ALU.add)
        if PAR["TWO"][t]:
            act(C("TT", h * 64, 64), jw(t, h, a, 64), AF.Identity, -17 / 16, 136.0)
            tt(C("DT", h * 128 + a, 64), out, C("TT", h * 64, 64), ALU.add)
        else:
            tt(rr(t, h, a, 64), out, jw(t, h, a, 64), ALU.subtract)

    for h in range(2):
        fields(0, h, 0, A("ND", S_, h), C("LF", h * 128, 64))
        cp(C("LF", h * 128 + 64, 64), C("LF", h * 128, 64))

    def distances(t, h, arr):
        part[0] = "d%d%d%d" % (t, h, arr)
        key, grp, a, two = C("K%d" % h, arr * 64, 64), (t, h, arr), arr * 64, PAR["TWO"][t]
        lst, dv = arr_list if arr else own_list, A("D", 4 * h)
        if two:
            mm(key, row(640, 128), row(128 + a, 64), True, False)
        else:
            begin()
            mm(key, row(512, 128), row(256, 64), True, False)
            mm(key, row(384, 128), row(a, 64), False, False)
            end("pe")
        if arr:
            fields(t, h, a, arr_list(t, h), dv)
        low = [mm(key, C("I16" if two else "Ib", 0, 128), (jw if two else rr)(t, h, a, 64), False, False, grp)]
        for q in range(4 if arr else 0):
            eq = [C("EQ", h * 1024 + r * 64, 64) for r in range(4 * q, 4 * q + 4)]
            for r in range(4):
                tt(eq[r], dv, C("LF", h * 128 + (4 * q + r) * 4, 64), ALU.is_equal)
            begin()
            for r in range(4):
                mm(key, C("Ibig", 0, 128), eq[r], False, False)
            end("pe", (grp, ()))
        base = (h * 2 + arr) * 1024
        cut = PAR["CUT"][arr]
        for k, n, form in pieces(PAR["ARR" if arr else "OWN"][t][h]):
            src = IND(C("P%d" % t, 16, 2048), lst(t, h, k * 4, n * 4))
            if form == "a":
                pg, buf, x0 = C("PG", h * 1024 + k * 64, n * 64), "SB%d" % h, 0
                act(pg, src)
                begin()
                mm(C(buf, 0, n * 64), C("Ib", 0, 128), fr(t, h, 0, n * 64), True, False)
                mm(C(buf, 0, n * 64), C("Ib", 0, 128), pg, False, True)
                end("pe")
            else:
                buf, x0 = "AX", base + k * 64
                tt(C(buf, x0, n * 64), src, fr(t, h, 0, n * 64), ALU.add)
            for j in range(cut):
                act(C("AB", base + k * 64 + j, n * 64 // cut, cut), C(buf, x0 + j, n * 64 // cut, cut), AF.Abs, 0.5)
        for q in range(4):
            begin()
            for il in range(q // 2 + q % 2 * 8, q // 2 + q % 2 * 8 + 8, 2):
                mm(key, C("Zp%d" % two, 16 - il, 128), C("AB", base + il, 64, 16), False, False)
            end("pe", (grp, low))
        if two:
            tt(C(key[0], 128, 64) if arr else A("H", h * 4 + 2), key, C("DT", h * 128 + a, 64), ALU.add)
        if not arr:
            act(A("H", h * (4 if two else 2)), key)

    def sel(buf, dims, fix={}, rev=()):
        name, pre = buf
        return A(name, *(pre + tuple(fix[b] if b in fix else (R_ if b in rev else S_) for b in dims) + (S_,)))

    mnx, mxn, full = ((0, ALU.min), (1, ALU.max)), ((0, ALU.max), (1, ALU.min)), [3, 2, 1, 0]

    def sort(h):
        n = [0]

        def two():
            n[0] += 1
            return [("H", (h * 2 + n[0] % 2,)), ("D", (h * 2 + n[0] % 2,))]

        def whole():
            n[0] += 1
            return ("Y%d" % (h * 2 + n[0] % 2), ())
        x, dims = two(), [1, 4, 3, 2]
        for side, op in mnx:
            tt(sel(x[side], dims), A("H", h * 2), C("K%d" % h, 64, 64), op)
        for lv in (1, 2, 3, 4):
            y = whole()
            yd = [lv] + [0 if b == lv else b for b in dims]
            for side, op in mnx[:1 if lv == 4 else 2]:
                tt(sel(y, yd, {lv: side}, [0] if side else []), sel(x[0], dims), sel(x[1], dims, {}, range(1, lv + 1)), op)
            if lv == 4:
                break
            c = lv - 1
            while c >= 0:
                if c == 0:
                    x, dims = two(), [b for b in yd if b != 0]
                    for side, op in mnx:
                        tt(sel(x[side], dims), sel(y, yd, {0: 0}), sel(y, yd, {0: 1}), op)
                    break
                x, dims = two(), [c] + [b for b in yd if b not in (c, c - 1)]
                for side, op in mnx:
                    for v in (0, 1):
                        tt(sel(x[v], dims, {c: side}), sel(y, yd, {c: 0, c - 1: v}), sel(y, yd, {c: 1, c - 1: v}), op)
                c -= 1
                if c == 0:
                    x2 = two()
                    for side, op in mnx:
                        tt(sel(x2[side], dims), sel(x[0], dims), sel(x[1], dims), op)
                    x = x2
                    break
                y, yd = whole(), [c] + dims
                for side, op in mnx:
                    tt(sel(y, yd, {c: side}), sel(x[0], dims), sel(x[1], dims), op)
                c -= 1
        y, yd = (y[0], y[1] + (0,)), yd[1:]
        for c in (3, 2, 1, 0):
            z = whole()
            z = (z[0], z[1] + (0,)) if c else ("KI", (h,))
            zd = [b for b in yd if b != c]
            zd.insert(3 - c, c)
            for side, op in mxn:
                tt(sel(z, zd, {c: side}), sel(y, yd, {c: 0}), sel(y, yd, {c: 1}), op)
            y, yd = z, zd

    def network(two, x, dims, yz):
        for lv in (1, 2, 3, 4):
            y, c2 = two(*((0,) if lv == 4 else ())), lv - 1
            yd = ([] if lv == 4 else [lv]) + [0 if b == lv else b for b in dims if (b != c2 if c2 else b != lv)]
            for side, op in mnx[:1 if lv == 4 else 2]:
                for v in (0, 1):
                    if c2:
                        fx, fp, rv = {c2: v}, {c2: 1 - v}, [0] if side else []
                    else:
                        fx, fp, rv = {lv: v ^ side}, {lv: 1 - (v ^ side)}, []
                    tt(sel(y[v], yd, {lv: side}, rv), sel(x[0], dims, fx), sel(x[1], dims, fp, range(1, lv + 1)), op)
            x, dims = y, yd
            for c in range(c2, -1, -1) if lv < 4 else ():
                y = two()
                yd = [c] + [b for b in dims if b != c - 1] if c else dims
                for side, op in mnx:
                    if c == 0:
                        tt(sel(y[side], yd), sel(x[0], dims), sel(x[1], dims), op)
                    for v in (0, 1) if c else ():
                        tt(sel(y[v], yd, {c: side}), sel(x[0], dims, {c - 1: v}), sel(x[1], dims, {c - 1: v}), op)
                x, dims = y, yd
        z, zd = (yz, (S_,)), [3] + dims
        for side, op in mxn:
            tt(sel(z, zd, {3: side}), sel(x[0], dims), sel(x[1], dims), op)
        y = two(0)
        for side, op in mxn:
            for v in (0, 1):
                tt(sel(y[v], [3, 2, 0], {2: side}), sel(z, zd, {2: 0, 1: v}), sel(z, zd, {2: 1, 1: v}), op)
        for side, op in mxn:
            tt(sel(z, full, {1: side}), sel(y[0], [3, 2, 0]), sel(y[1], [3, 2, 0]), op)

    def sort_both():
        n = [0]

        def two(*more):
            n[0] += 1
            j = n[0] % 2
            return [("H", (slice(j, 4, 2),) + more), ("D", (slice(2 * j, 2 * j + 2),) + more)]
        x, dims = two(), [1, 4, 3, 2]
        for h in range(2):
            for side, op in mnx:
                tt(A(*(("H", h * 2 + 1), ("D", 2 + h))[side]), A("H", h * 2), C("K%d" % h, 64, 64), op)
        network(two, x, dims, "Y0")
        for h in range(2):
            for side, op in mxn:
                tt(sel(("KI", (h,)), full, {0: side}), sel(("Y0", (h,)), full, {0: 0}), sel(("Y0", (h,)), full, {0: 1}), op)

    def sort_two(h):
        n = [0]

        def two(*more):
            n[0] += 1
            j = n[0] % 2
            return [("H", (slice(4 * h + j, 4 * h + 4, 2),) + more), ("D", (slice(4 * h + 2 * j, 4 * h + 2 * j + 2),) + more)]
        x, dims, y = two(), [1, 4, 3, 2], ("Y%d" % h, (S_,))
        for side, op in mnx:
            tt(sel(x[side], dims), A("H", slice(4 * h, 4 * h + 4, 2)), C("K%d" % h, 64, 128), op)
        network(two, x, dims, y[0])
        for side, op in mxn:
            tt(sel(("KI", (slice(2 * h, 2 * h + 2),)), full, {0: side}), sel(y, full, {0: 0}), sel(y, full, {0: 1}), op)

    def choose_two(t, h):
        part[0] = "s%d%d" % (t, h)
        sort_two(h)
        part[0] = "l%d%d" % (t, h)
        oa, ob, pl = C("O32", h * 64, 64), C("D32", h * 64, 64), C("PL", h * 64, 64)
        ts(oa, A("KI", 2 * h), 2032, ALU.bitwise_and)
        ts(ob, A("KI", 2 * h + 1), 4, ALU.arith_shift_right, 15, ALU.bitwise_and)
        tt(pl, oa, ob, ALU.add)
        cp(own_list(t + 1, h), pl)
        if t < DAYS - 1:
            send(t + 1, [h])
            s = 16.0 if PAR["TWO"][t + 1] else 1.0
            begin()
            for r in range(2):
                act(C("LF", h * 128 + r * 64, 64), pl, AF.Identity, s, -7.5 * s)
            end("act")
            ts(jw(t + 1, h, 0, 64), oa, s, ALU.mult)
            if PAR["TWO"][t + 1]:
                ts(A("D", 4 * h + 1), ob, 16.0, ALU.mult, 16.0, ALU.add)
                tt(C("DT", h * 128, 64), A("D", 4 * h + 1), oa, ALU.subtract)
            else:
                ts(rr(t + 1, h, 0, 64), ob, -7.5, ALU.add)

    def choose(t, h):
        if PAR["TWO"][t]:
            return choose_two(t, h)
        if not PAR["JOINT"][t]:
            part[0] = "s%d%d" % (t, h)
            sort(h)
        elif not h:
            part[0] = "s%d0" % t
            sort_both()
        part[0] = "l%d%d" % (t, h)
        ki, o32, o16 = A("KI", h), C("O32", h * 64, 64), C("O16", h * 64, 64)
        ts(o32, ki, 5, ALU.arith_shift_right, 127, ALU.bitwise_and)
        cp(o16, o32)
        ts(C("D32", h * 64, 64), ki, 15, ALU.bitwise_and)
        ts(rr(t + 1, h, 0, 64), C("D32", h * 64, 64), -7.5, ALU.add)
        last, kb, a = t == DAYS - 1, "K%d" % h, 0
        for k, n, who in pieces(PAR["LOOK"][t][h]):
            move(who, C("JG", h * 1024 + k * 64, n * 64), IND(jw(t, h, 0, 128), C("O16", h * 64 + k * 4, n * 4)))
            c0 = (k + n) * 4
            if last or c0 == 64:
                lk = C(kb, 128 + a, c0 - a)
                mm(lk, C("Ib", 0, 128), rr(t + 1, h, a, c0 - a), True, False)
                for q in range(0, 16, 4):
                    begin()
                    for il in range(q, q + 4):
                        mm(lk, C("Dm", il * 128, 128), C("JG", h * 1024 + a * 16 + il, c0 - a, 16), False, il == 15)
                    end("pe")
                ts(own_list(t + 1, h, a, c0 - a), lk, 7.5, ALU.add)
                a = c0
        if not last:
            send(t + 1, [h])
            begin()
            for r in range(2):
                act(C("LF", h * 128 + r * 64, 64), C(kb, 128, 64))
            end("act")
            ts(jw(t + 1, h, 0, 64), C("LF", h * 128, 64), MAGIC, ALU.add, -MAGIC, ALU.add)

    def e_of(t, h, k, n=1):
        return C("E" if t else "EB", max(t - 1, 0) * 2048 + h * 1024 + k * 64, n * 64)

    def errors(t, h):
        part[0] = "e%d%d" % (t, h)
        for k, n, who in pieces(PAR["ECH"][t][h]):
            move(who, e_of(t, h, k, n), IND(C("Ew", 0, 2048), own_list(t + 1, h, k * 4, n * 4)))

    def bias(t, h, steps):
        forms, bk = [f for _, n, f in pieces(PAR["BIAS"][t][h]) for _ in range(n)], "B%d" % h
        k0 = forms.index("p") if "p" in forms else 16
        u, x = C("U", h * 64, 64), C("X", h * 64, 64)
        part[0] = "b%d%d0" % (t, h)
        for k in steps:
            ek = e_of(t, h, k)
            if forms[k] == "t":
                w0, w1 = [(h * 2 + (k + j) % 2) * 200 for j in range(2)]
                if k == 0:
                    ms(C("V", w0 + 1, 64, 3), 0.0)
                if k < 15:
                    move(PAR["TRICP"][h], C("V", w0 + 3, 64, 3), e_of(t, h, k + 1))
                else:
                    ms(C("V", w0 + 3, 64, 3), 0.0)
                y = C("V", w0 + 2, 64, 3)
                ts(y, y if k > 0 else ek, m2, ALU.min, mn2, ALU.max)
                scan(C("V", w1, 192) if k < 15 else C(bk, 0, 192), C("S3", 0, 192), C("V", w0 + 1, 192))
            elif forms[k] == "p":
                j = k - k0
                z = C(bk if k % 2 or k < PAR["BANK2"][t] else "SB%d" % h, 256, 64)
                if k == k0 > 0:
                    tt(u, ek, C(bk, (k % 2) * 128 + 1, 64, 2), ALU.subtract)
                ts(x, u if k > 0 else ek, C("MK", j, 1), ALU.min, C("MK", 16 + j, 1), ALU.max)
                wts = [power(t, j + 1, 1) if k < 15 else None, power(t, j + 1, -1) if k > 0 else None]
                begin()
                if k < 15:
                    mm(z, wts[0], e_of(t, h, k + 1), True, k == 0)
                if k > 0:
                    mm(z, wts[1], ek, k == 15, False)
                end("pe")
                if k > 0:
                    mm(z, C("I2", 0, 128), u, False, True)
                tt(u, z, x, ALU.subtract)
                if k == 15:
                    ts(z, u, -2.0 ** (k0 - 16), ALU.mult)
            elif k == 0:
                ts(x, ek, 0.5, ALU.mult, m1, ALU.min)
                ts(C(bk, 129, 64, 2), x, mn1, ALU.max)
            else:
                w0, w1 = (k % 2) * 128, (1 - k % 2) * 128
                tt(u, ek, C(bk, w0 + 1, 64, 2), ALU.subtract)
                ts(C(bk, w0, 64, 2), u, m2, ALU.min, mn2, ALU.max)
                scan(C(bk, w1, 128), C("SC", 0, 128), C(bk, w0, 128))
        return {"t": (C(bk, 2, 64, 3), -1.0), "d": (C(bk, 1, 64, 2), 1.0), "p": (C(bk, 256, 64), 1.0)}[forms[15]]

    def finish(t, h, b, sign):
        part[0] = "u%d%d" % (t, h)
        lo = t * 128 + h * 64
        if t < DAYS - 1:
            tt(C("Ew", h * 1024 + t, 64, 16), C("ER", lo, 64), b, ALU.subtract if sign > 0 else ALU.add)
        ts(C("YB", lo, 64), b, sign, ALU.mult)
        dma("sp", C("yb", lo, 64), C("YB", lo, 64), 2.0)

    def spread(t, h, b, sign):
        part[0] = "x%d%d" % (t, h)
        lo = t * 128 + h * 64
        yb, ys, last = C("YB", lo, 64), C("YS", lo, 64), t == DAYS - 1
        sm = C("K%d" % h if last else "SM", 384, 64)
        buf, x0 = ("X2", h * 1024) if last else ("NB", (t * 2 + h) * 1024)
        if not last:
            n = PAR["NACT"][t]
            begin()
            for r in range(4):
                act(C(buf, x0 + r * 64, 64), yb, AF.Identity, -1.0)
            end("act")
            for r in range(4, n, 4):
                act(C(buf, x0 + r * 64, 256), C(buf, x0, 256))
            for r in range(n, 16, n):
                dma("sp", C(buf, x0 + r * 64, n * 64), C(buf, x0, n * 64), 2.2)
            dma("pool", C(buf, x0, 1024), e_of(t, h, 0, 16), 3.6, "dma_add")
        todo = pieces(PAR["TAILQ"][h] if last else PAR["SPQ"][t])
        for k0, n, form in todo:
            a, m = x0 + k0 * 64, n
            x = C(buf, a, n * 64)
            if last:
                begin()
                for k in range(k0, k0 + n):
                    tt(C(buf, x0 + k * 64, 64), e_of(t, h, k), b, ALU.subtract if sign > 0 else ALU.add)
                end("dve")
            act(x, x, AF.Abs)
            if form != "n":
                m = n // 2
                ps = C("SB%d" % h, 0, m * 64) if form == "p" else A("D", slice(4 * h, 4 * h + m))
                begin()
                act(ps, C(buf, a + m * 64, m * 64), AF.Exp, -1.0)
                act(C(buf, a, m * 64), C(buf, a, m * 64), AF.Exp, -1.0)
                end("act")
                tt(C(buf, a, m * 64), C(buf, a, m * 64), ps, ALU.add)
            else:
                act(A("NC", h, slice(k0 * 64, (k0 + n) * 64)) if PAR["DADD"][t] else x, x, AF.Exp, -1.0)
            if last and k0 + n == 16:
                tt(ys, sm, C(buf, a, 64), ALU.add)
                return dma("sp", C("ys", lo, 64), ys, 2.0)
            for k in range(0, 0 if PAR["DADD"][t] else m, 2):
                begin()
                for j in range(k, min(k + 2, m)):
                    mm(sm, C("If", 0, 128), C(buf, a + j * 64, 64), k0 + j == 0, k0 + n == (todo[-1][0] if last else 16) and j == m - 1)
                end("pe")
        if not PAR["DADD"][t]:
            act(ys, sm)
            return dma("sp", C("ys", lo, 64), ys, 2.0 + PAR["SAFE"][t])
        if h == 1:
            m = 16
            for _ in range(PAR["DADD"][t]):
                m //= 2
                dma("pool", A("NC", S_, slice(0, m * 64)), A("NC", S_, slice(m * 64, m * 128)), 3.3, "dma_add")
            for g in range(2):
                for k in range(0, m, 2):
                    begin()
                    for j in (k, k + 1):
                        mm(sm, C("If", 0, 128), A("NC", g, slice(j * 64, j * 64 + 64)), j == 0, j == m - 1)
                    end("pe")
                act(C("YS", t * 128 + g * 64, 64), sm)
            dma("sp", C("ys", t * 128, 128), C("YS", t * 128, 128), 2.0 + PAR["SAFE"][t])

    for arr in range(2):
        for h in range(2):
            distances(0, h, arr)
    for h in range(2):
        choose(0, h)
    for t in range(DAYS):
        for h in range(2):
            if t + 1 < DAYS:
                distances(t + 1, h, 0)
            errors(t, h)
        for h in range(2):
            bias(t, h, range(PAR["BANK2"][t]))
            if t + 1 < DAYS:
                distances(t + 1, h, 1)
        bs = [bias(t, h, range(PAR["BANK2"][t], 16)) for h in range(2)]
        for h in range(2):
            finish(t, h, *bs[h])
        if t + 1 < DAYS:
            for h in range(2):
                choose(t + 1, h)
        for h in range(2):
            spread(t, h, *bs[h])
    above = []
    for o in ops:
        far = 0
        for d in o["deps"]:
            far |= above[d]
        o["near"] = [d for d in o["deps"] + o["soft"] if not far >> d & 1]
        for d in o["near"]:
            far |= above[d] | 1 << d
        above.append(far)
    return ops


def priced(ops, cost):
    out = []
    for o in ops:
        f, c, gth, p, n = o["busy"]
        b = f * (cost["PF"] if o["eng"] == "pool" else 1.0) + n * cost["FIX"] + (c + gth * cost["GA"]) * cost["CY"] + p * cost["PCY"]
        out.append((b, b + (cost["HOP"] + o["lat"][1] * cost["LS"] if isap(o["lat"]) else o["lat"] * cost["LS"])))
    return out


def gap(ops, d, i, cost):
    a, b = ops[d]["eng"], ops[i]["eng"]
    return 0.0 if (a == b == "pe" or b == "rx" or d in ops[i]["soft"]) else cost["WS" if a == b else "WX"]


def place(eng, busy, lat, pred, succ, prio, back, old=None, cut=0.0):
    n = len(eng)
    begin, end = [[] for _ in range(6)], [[] for _ in range(6)]
    st, rdy = [0.0] * n if old is None else old.tolist(), [cut] * n
    rank = np.argsort(prio, kind="stable")
    if old is None:
        left = [len(p) for p in pred]
    else:
        rank, left = rank[old[rank] >= cut], [0] * n
        for i in np.nonzero((old < cut) & (old > cut - 3.0))[0].tolist():
            if st[i] + busy[i] > cut and eng[i]:
                begin[eng[i]], end[eng[i]] = [st[i]], [st[i] + busy[i]]
        for i in rank.tolist():
            for d, g in pred[i]:
                if st[d] >= cut:
                    left[i] += 1
                elif st[d] + lat[d] + g > rdy[i]:
                    rdy[i] = st[d] + lat[d] + g
    pos = np.empty(n, int)
    pos[rank] = np.arange(len(rank))
    rank, pos = rank.tolist(), pos.tolist()
    ready, j = [not x for x in left], 0
    for _ in rank:
        while not ready[rank[j]]:
            j += 1
        i = rank[j]
        ready[i] = False
        b, l, e, t = busy[i], lat[i], eng[i], rdy[i]
        if e:
            s, f = begin[e], end[e]
            off = l - b if back else 0.0
            t += off
            if not f or f[-1] <= t:
                s.append(t)
                f.append(t + b)
            else:
                lo, hi = 0, len(f)
                m = hi
                while lo < hi:
                    mid = (lo + hi) // 2
                    if f[mid] <= t:
                        lo = mid + 1
                    else:
                        hi = mid
                while lo < m and s[lo] < t + b - 1e-9:
                    t = f[lo]
                    lo += 1
                s.insert(lo, t)
                f.insert(lo, t + b)
            t -= off
        st[i] = t
        t += l
        for k, g in succ[i]:
            if t + g > rdy[k]:
                rdy[k] = t + g
            left[k] -= 1
            if not left[k]:
                ready[k] = True
                if pos[k] < j:
                    j = pos[k]
    return np.array(st)


def replay(seq, eng, pred, busy, lat, old, keep):
    free, fin = [0.0] * 6, [0.0] * len(seq) if old is None else list(old)
    seen = 1
    for i in seq[keep - 1::-1] if keep else ():
        if not seen >> eng[i] & 1:
            seen |= 1 << eng[i]
            free[eng[i]] = fin[i] - lat[i] + busy[i]
            if seen == 63:
                break
    for i in seq[keep:]:
        e = eng[i]
        t = free[e]
        for d, g in pred[i]:
            x = fin[d] + g
            if x > t:
                t = x
        if e:
            free[e] = t + busy[i]
        fin[i] = t + lat[i]
    return fin


def search(ops, tries):
    n, price, rs = len(ops), priced(ops, COST), np.random.RandomState(SEED)
    eng = [("rx", "dve", "act", "pe", "pool", "sp").index(o["eng"]) for o in ops]
    sets = []
    for w, v in VARY:
        c = dict(COST, **v)
        p = priced(ops, c)
        sets.append((w, [[(d, gap(ops, d, i, c)) for d in o["near"]] for i, o in enumerate(ops)], [x[0] for x in p], [x[1] for x in p]))
    pred, succ = [[] for _ in ops], [[] for _ in ops]
    for i, o in enumerate(ops):
        for d in o["near"]:
            pred[i].append((d, gap(ops, d, i, COST)))
            succ[d].append((i, gap(ops, d, i, COST)))
    parts = sorted(set(o["part"] for o in ops))
    of = np.array([parts.index(o["part"]) for o in ops])
    busy, lat = [p[0] for p in price], [p[1] for p in price]
    alat, queue = np.array(lat), np.array(eng)
    prio = [0.0] * n
    for i in range(n - 1, -1, -1):
        prio[i] = min([prio[s] - g for s, g in succ[i]] + [0.0]) - lat[i]
    prio = np.array(prio) + np.array([PAR["LAG"] * ((q[2:3] == "1") + 3 * (q[0] == "x" and q[1] != "2")) for q in parts])[of]
    best, now, masks, ends = None, None, {}, [None] * len(sets)
    for it in range(tries):
        base, cut = prio.copy(), 0.0
        if it % PAR["BACK"] == PAR["BACK"] - 1:
            base = -place(eng, busy, lat, succ, pred, -times - alat, True) - alat
        elif it:
            near = rs.rand() < 0.6
            if near:
                base = times.copy()
            for _ in range(1 + (rs.rand() < PAR["MORE"])):
                p = parts[rs.randint(len(parts))][:rs.randint(2, 5)]
                if p not in masks:
                    masks[p] = np.array([q.startswith(p) for q in parts])[of]
                m = masks[p]
                if rs.rand() < 0.5:
                    lo, hi = times[m].min(), times[m].max()
                    a = lo + rs.rand() * (hi - lo)
                    m = m & ((times >= a) if rs.rand() < 0.5 else (times <= a))
                if rs.rand() < 0.3:
                    m = m & (queue == 1 + rs.randint(3))
                base[m] += rs.randn() * (0.4, 1.5, 5.0)[it % 3]
            if near:
                m = base != times
                if not m.any():
                    continue
                cut = max(0.0, np.minimum(base, times)[m].min() - 1.0)
        st = place(eng, busy, lat, pred, succ, base, False, times if cut else None, cut)
        bar = 1e9 if now is None else now - PAR["TEMP"] * (1 - it / tries) * np.log(rs.rand())
        early, mine = PAR["EARLY"] * st.mean(), (st + alat).max()
        if now is not None and mine + early > head + (bar - now) * 2 + 0.6:
            continue
        seq, keep = np.argsort(st, kind="stable").tolist(), int((st < cut).sum())
        new = [replay(seq, eng, s[1], s[2], s[3], e, keep) for s, e in zip(sets, ends)]
        r = [max(x) for x in new]
        q = [x * s[0] for x, s in zip(r, sets)]
        score = (sum(q) / len(q) + max(q)) / 2 + early
        if score <= bar:
            now, prio, times, head, ends = score, base, st, mine + early, new
            if best is None or score < best[0]:
                best = (score, r, st)
    for i, o in enumerate(ops):
        o["t"] = float(best[2][i])
    return best[:2]


def waits(ops, order):
    inc = set()
    for i, o in enumerate(ops):
        if o["eng"] != "rx":
            inc.update(d for d in o["deps"] if not (o["eng"] == "pe" == ops[d]["eng"]))
    tick, total = {}, {}
    for e in order:
        for i in order[e]:
            if ops[i]["sem"] is None and i in inc:
                total[e] = total.get(e, 0) + (len(ops[i]["args"]) if ops[i]["call"] == "many" else 1)
                tick[i] = (e, total[e])
            elif ops[i]["sem"] is not None:
                tick[i] = (ops[i]["sem"], 1)
    know = dict((e, {}) for e in order)
    after = {}
    for i in sorted(range(len(ops)), key=lambda j: (ops[j]["t"], j)):
        o = ops[i]
        k = know[o["eng"]]
        need = {}
        if o["eng"] != "rx":
            for d in sorted(o["deps"], key=lambda j: -ops[j]["t"]):
                if o["eng"] == "pe" == ops[d]["eng"]:
                    continue
                s, v = tick[d]
                if k.get(s, 0) < v:
                    need[s] = max(need.get(s, 0), v)
                    for s2, v2 in after[d].items():
                        k[s2] = max(k.get(s2, 0), v2)
        o["wait"] = need
        o["tick"] = tick.get(i)
        a = {} if o["eng"] == "rx" else dict(k)
        if i in tick:
            a[tick[i][0]] = max(a.get(tick[i][0], 0), tick[i][1])
        after[i] = a
    return total


PLAN = {}


def plan():
    if not PLAN:
        ops = build()
        best = search(ops, TRIES)
        order = dict((e, []) for e in ("pe", "dve", "act", "pool", "sp", "rx"))
        for i in sorted(range(len(ops)), key=lambda j: (ops[j]["t"], j)):
            order[ops[i]["eng"]].append(i)
        last = dict((ops[i]["grp"], i) for i in order["pe"] if ops[i]["grp"] is not None)
        for i in last.values():
            if ops[i]["call"] == "many":
                ops[i]["args"][-1] = ("matmul", ops[i]["args"][-1][1][:4] + (True,))
            else:
                ops[i]["args"] = ops[i]["args"][:4] + (True,)
        PLAN.update(best=best, ops=ops, order=order, total=waits(ops, order))
    return PLAN


def bits(engs):
    return sum(1 << e for e in engs)


def relays_of(T, topo, r):
    src, dst = T.cores[r], T.cores[(r + 1) % len(T.cores)]
    free = sorted((c for c in topo.cores_of(src) if T.rank_of(c) is None), key=lambda c: (topo.die(c) != topo.die(src), c))
    return [c for c in free if topo.may_write(c, dst)][:2]


def relay_program(g, core, T, topo):
    for r, src in enumerate(T.cores):
        relays = relays_of(T, topo, r)
        if core in relays:
            h, dst = relays.index(core), T.cores[(r + 1) % len(T.cores)]
            n_in = len(topo.engines(src, core))
            out = topo.engines(core, dst)
            rid, pid = topo.addr(dst, core)
            for t in range(DAYS):
                name, key = arr_list(t, h)
                sem = T.sem["ar%d%d" % (t, h)]
                g.wait_ge(sem, n_in // 2 if t == 0 else n_in)
                g.remote_dma(T[name][key], T[name][key], sem, T.sem.sent, pid, rid, bits(out))
            g.wait_ge(T.sem.sent, DAYS * len(out))


def issue(q, call, a):
    if call == "iota":
        return q.iota(*a)
    if call == "affine_select":
        return q.affine_select(*a)
    if call == "dma_start":
        return q.dma_start(a[0], a[1])
    if call == "dma_add":
        return q.dma_start(a[0], a[1], accum_op=ALU.add)
    if call == "activation":
        return q.activation(a[0], a[1], a[2], bias=a[4], scale=a[3])
    if call == "matmul":
        return q.matmul(*a)
    if call == "tensor_copy":
        return q.tensor_copy(*a)
    if call == "tensor_scalar":
        return q.tensor_scalar(*a)
    if call == "tensor_tensor":
        return q.tensor_tensor(*a)
    if call == "tensor_tensor_scan":
        return q.tensor_tensor_scan(*a)
    return q.memset(*a)


def rank_program(g, core, T, topo):
    r = T.rank_of(core)
    if r is None:
        return relay_program(g, core, T, topo)
    p = plan()
    ops = p["ops"]
    relays = relays_of(T, topo, r)
    before = relays_of(T, topo, (r - 1) % len(T.cores))
    step = dict((s, 16) for s in DMA_SEMS + POOL_SEMS)
    for t in range(DAYS):
        for h in range(2):
            step["ar%d%d" % (t, h)] = len(topo.engines(before[h], core))
    queue = {"pe": g.tensor, "dve": g.vector, "act": g.scalar, "pool": g, "sp": g.sync}
    sent, used = [0], []

    def ap(x):
        if not isap(x):
            return x
        if x[0] == "*":
            return ap(x[1]).indirect(ap(x[2]))
        return T[x[0]][x[1]]

    for i in sorted(range(len(ops)), key=lambda j: (ops[j]["t"], j)):
        o = ops[i]
        if o["sem"] not in (None, "sent"):
            used.append(o["sem"])
        if o["eng"] == "rx":
            continue
        q = queue[o["eng"]]
        for s, v in o["wait"].items():
            q.wait_ge(T.sem[s], v * step.get(s, 1))
        if o["call"] == "send":
            (t, hs), tr = o["args"], []
            for j, h in enumerate(hs):
                en = topo.engines(core, relays[h])
                en = en[j * len(en) // len(hs):(j + 1) * len(en) // len(hs)]
                rid, pid = topo.addr(relays[h], core)
                tr.append(RemoteDMATransfer(dst_ids=[DstId(rid=rid, pnc=pid)], dma_engine_mask=bits(en),
                                            remote_sem=T.sem["ar%d%d" % (t, h)], src=ap(own_list(t, h)), dst=ap(arr_list(t, h))))
                sent[0] += len(en)
            g.remote_dma_fused(tr, local_sem=T.sem.sent)
            continue
        for call, args in o["args"] if o["call"] == "many" else [(o["call"], o["args"])]:
            ins = issue(q, call, [ap(x) for x in args])
            if o["tick"]:
                ins.then_inc(T.sem[o["tick"][0]], step.get(o["tick"][0], 1))
    g.wait_ge(T.sem.sent, sent[0])
    for s, v in p["total"].items():
        g.wait_ge(T.sem[s], v)
    for s in used:
        g.wait_ge(T.sem[s], step[s])
